import numpy as np, ml_dtypes
CORES = [6,15,38,47]
N = 4
BF = ml_dtypes.bfloat16
def gentries(a):
    return np.ascontiguousarray(a.reshape(8, 16, -1).transpose(0, 2, 1)).reshape(8, -1)
def gtable(e):
    e = np.asarray(e); return np.ascontiguousarray(e.reshape(8, -1, 16).transpose(0, 2, 1)).reshape(128, -1).astype(np.int32)
S, M, NA, RO = 256, 1024, 2048, 3
W0 = M + (N - 1) * S; W = W0 + RO * S
def parts(rng):
    amp = rng.choice(np.array([255, 160, 96]), (1, 8, 1, 1))
    y = (rng.random((N, 8, 16, W0)) * (amp + 1)).astype(np.int64)
    l = rng.integers(0, W0, (N, 8, 16, NA)); c = rng.integers(0, NA, (N, 8, 16, M))
    f = np.where(rng.random((N, 8, W0)) < 0.3, rng.integers(0, W0, (N, 8, W0)), np.arange(W0))
    th = (amp[..., 0] * (4.6 + 2.2 * rng.random((N, 8, S)))).astype(np.int64)
    return y, l, c, f, th
def pack(y, l, c, f, th):
    return {"y0": np.ascontiguousarray(y.reshape(N, 128, W0)).astype(np.float32).astype(BF), "lk": np.ascontiguousarray(l.reshape(N, 128, NA)).astype(np.int32),
            "cl": np.ascontiguousarray(c.reshape(N, 128, M)).astype(np.int32), "fw0": np.stack([gtable(z) for z in f]), "th": np.ascontiguousarray(th).astype(np.int32)}
def uneven(rng, hi, *shape):
    z = rng.random(shape) ** 3; side = rng.random(shape[:2] + (1,) * (len(shape) - 2)) < 0.5
    return np.minimum((hi * np.where(side, z, 1 - z)).astype(np.int64), hi - 1)
def far(y, l, c, f):
    r4 = np.arange(N)[:, None, None, None]; g4 = np.arange(8)[None, :, None, None]; k4 = np.arange(16)[None, None, :, None]
    a = c[..., :S]; b = f[r4, g4, l[r4, g4, k4, a]].reshape(N, 8, 1, 16 * S); e = f[r4, g4, l[r4, g4, (k4 + 5) % 16, a]].reshape(N, 8, 1, 16 * S)
    z = ((np.take_along_axis(y, b, 3) + np.take_along_axis(y, e, 3)) >> 1).reshape(N, 8, 16, 16, S)
    return np.max(np.add.reduce(np.abs(z - y[..., :S][:, :, :, None, :]), axis=2), axis=2)
def setup_inputs(rng):
    return pack(*parts(rng))
def setup_inputs_spread(rng):
    y, l, c, f, th = parts(rng)
    y = np.minimum((np.exp2(8 * rng.random((N, 8, 1, W0))) * rng.random((N, 8, 16, W0))).astype(np.int64), 255)
    l = uneven(rng, W0, N, 8, 16, NA); c = uneven(rng, NA, N, 8, 16, M)
    f = np.where(rng.random((N, 8, W0)) < 0.5, uneven(rng, W0, N, 8, W0), f)
    th = np.minimum((4081 * rng.random((N, 8, S)) ** 3).astype(np.int64), 4080)
    return pack(y, l, c, f, th)
def setup_inputs_ends(rng):
    y, l, c, f, th = parts(rng)
    y = np.where(rng.random((N, 8, 1, W0)) < 0.6, 255 * rng.integers(0, 2, (N, 8, 1, W0)), 255 * rng.integers(0, 2, (N, 8, 16, W0)))
    y[..., 0] = 0; y[..., W0 - 1] = 255; y[..., S - 1] = 0
    l = np.where(rng.random(l.shape) < 0.72, (W0 - 1) * rng.integers(0, 2, l.shape), l)
    c = np.where(rng.random(c.shape) < 0.72, (NA - 1) * rng.integers(0, 2, c.shape), c)
    f = np.where(rng.random(f.shape) < 0.7, (W0 - 1) * rng.integers(0, 2, f.shape), rng.integers(0, W0, f.shape))
    f[..., 0] = 0; f[..., W0 - 1] = W0 - 1
    l[:, 1::2, :, 0] = 0; l[:, 1::2, :, NA - 1] = W0 - 1
    c[:, :, 0, S - 1] = 0; c[:, :, 14, S - 1] = 0; c[:, :, 2, S - 1] = NA - 1; c[:, :, 15, S - 1] = NA - 1
    th = 4080 * rng.integers(0, 2, (N, 8, S))
    near = np.maximum(far(y, l, c, f) - rng.choice(np.array([0, 0, 1, 1, 1, 2, 9, 15, 16]), th.shape), 0)
    th = np.where(rng.random(th.shape) < 0.28, near, th)
    th[..., S - 1] = 0; th[:, 1::4, S - 1] = 4079
    th[np.arange(N), 2 * rng.integers(0, 4, N)] = 4080
    return pack(y, l, c, f, th)
def setup_inputs_corners(rng):
    y, l, c, f, th = parts(rng); x = np.arange(W0)
    th = np.where(rng.random(th.shape) < 0.25, 4080 * rng.integers(0, 2, th.shape), th)
    for r in range(N):
        o = rng.permutation(8)
        for g in range(8):
            f[r, g] = (x, np.maximum(x - 1, 0), (x + 1) % W0, x ^ 1, x * 0, x * 0 + W0 - 1, rng.choice(np.array([0, M - 1, M, W0 - 1]), W0), W0 - 1 - x)[int(o[g])]
            j = int(rng.integers(0, 6)); h = int(rng.integers(0, 6))
            if o[g] == 0: j = 5; h = 1; th[r, g] = 0
            if o[g] == 2: th[r, g] = 4080
            if j == 0: l[r, g] = np.arange(NA) % M
            if j == 1: l[r, g] = rng.choice(np.array([0, M - 1, M, W0 - 1]), (16, NA))
            if j == 2: l[r, g] = rng.integers(M, W0, (16, NA))
            if j == 3: l[r, g] = rng.integers(0, M, (16, NA))
            if j == 4: l[r, g, 1::2] = W0 - 1
            if h == 0: c[r, g] = c[r, g, :1]
            if h == 1: c[r, g] = np.arange(M) % NA
            if h == 2: c[r, g] = rng.choice(np.array([0, NA - 1]), (16, M))
            if h == 3: c[r, g] = (np.arange(M)[None, :] * 7 + np.arange(16)[:, None]) % NA
    return pack(y, l, c, f, th)
def setup_inputs_crowd(rng):
    y, l, c, f, th = parts(rng); y = rng.integers(0, 8, y.shape); th = rng.integers(25, 60, th.shape); i = np.arange(S)
    for r in range(N):
        for g in range(8):
            m = (1, 1, 2, 2, 16, 16, 1, 1)[g]; o = rng.permutation(NA); a = o[:m]
            x = int(rng.integers(M - S, M)) if g % 4 < 2 else int(rng.integers(M, W0))
            if r == N - 1 and g > 5: x = W0 - 1
            y[r, g, :, x] = 255; f[r, g, x] = x; l[r, g][:, a] = x
            c[r, g][rng.integers(0, 16, S), i] = a[i % m]
            if g in (1, 3, 4, 6):
                e = int(rng.integers(0, S)); f[r, g, e] = e; l[r, g, :, o[m]] = e; c[r, g, :, e] = o[m]
    return pack(y, l, c, f, th)
def setup_inputs_ties(rng):
    y, l, c, f, th = parts(rng)
    step = rng.choice(np.array([1, 3]), (1, 8, 1)); low = np.array([0, 127, 200, 252, 0, 127, 200, 252])[rng.permutation(8)].reshape(1, 8, 1)
    o = rng.permutation(8); step[0, o[:2]] = 1
    y = low[..., None] + step[..., None] * rng.integers(0, 2, y.shape)
    th = step * rng.integers(0, 11, th.shape)
    for g in o[:2]:
        y[:, g, 0] = low[0, g, 0]; th[:, g] = 0
        for r in range(N):
            e = int(rng.integers(0, S)); b = int(rng.integers(0, NA))
            f[r, g, e] = e; l[r, g, :, b] = e; c[r, g, :, e] = b
    B = NA // RO
    for r in range(N):
        for j in (2, 3):
            g = int(o[j]); e = int(rng.integers(0, S)); h = int(rng.integers(0, 16)); x = int(rng.integers(40, 175)); d = int(rng.integers(4, 41))
            s = np.array([x, x, x + d, x - d, x + 2 * d]) if j == 2 else np.array([x, x + 1, x + 1 + d, x + 1, x + 1 + d])
            y[r, g, :, :RO * S] = rng.integers(0, 256, (16, 1)); y[r, g, h, :RO * S] = np.repeat(s[:RO], S); y[r, g, h, (RO - 1) * S + e] = s[RO]
            f[r, g, :RO * S] = np.arange(RO * S)
            for t in range(RO):
                c[r, g, :, t * S:(t + 1) * S] = rng.integers(t * B, (t + 1) * B, (16, S))
                l[r, g, :, t * B:(t + 1) * B] = (t + 1) * S + (e + rng.integers(1, S, (16, B))) % S if t < RO - 1 else t * S + e
            if j == 2: th[r, g] = (1 + r % (RO - 1)) * d - 1
            else:
                k = 1 + r % 3; th[r, g] = d - rng.integers(1, k + 1, S); th[r, g, rng.permutation(S)[:k]] = 0
    w = far(y, l, c, f); th[:, o[4:6]] = w[:, o[4:6]]; g = int(o[5])
    for r in range(N): th[r, g, np.argsort(-w[r, g])[:1 + r % 3]] -= 1
    return pack(y, l, c, f, np.maximum(th, 0))
def check_inputs(d):
    bad = []
    for k, lo, hi in (("y0", 0, 255), ("lk", 0, W0 - 1), ("cl", 0, NA - 1), ("fw0", 0, W0 - 1), ("th", 0, 4080)):
        z = np.asarray(d[k]).astype(np.float64)
        if not np.all((z >= lo) & (z <= hi)): bad.append("range of " + k)
        elif not np.all(z == np.floor(z)): bad.append("whole numbers in " + k)
    return bad
def at(z, k):
    return np.take_along_axis(z, k[:, :, None, :], 2)[:, :, 0]
def reference(y0, lk, cl, fw0, th):
    Y = np.zeros((N, 8, 16, W), np.int64); Y[..., :W0] = y0.astype(np.float32).astype(np.int64).reshape(N, 8, 16, W0)
    L = lk.astype(np.int64).reshape(N, 8, 16, NA)
    C = np.zeros((N, 8, 16, W), np.int64); C[..., :M] = cl.astype(np.int64).reshape(N, 8, 16, M)
    F = np.tile(np.arange(W), (N, 8, 1)); F[:, :, :W0] = np.stack([gentries(z) for z in fw0])
    lane = np.arange(S); v = np.tile(lane, (N, 8, 1)); A = np.zeros((N, 8), np.int64); lim = th.astype(np.int64).reshape(N, 8, S)
    rk = np.arange(N)[:, None, None]; gr = np.arange(8)[None, :, None]; row = np.arange(16)[None, None, :, None]
    rk4 = rk[..., None]; gr4 = gr[..., None]
    for t in range(RO):
        a = np.take_along_axis(C, v[:, :, None, :], 3)
        b = np.take_along_axis(L, a, 3); c = L[rk4, gr4, (row + 5) % 16, a]
        fb = F[rk4, gr4, b].reshape(N, 8, 1, 16 * S); fc = F[rk4, gr4, c].reshape(N, 8, 1, 16 * S)
        y = ((np.take_along_axis(Y, fb, 3) + np.take_along_axis(Y, fc, 3)) >> 1).reshape(N, 8, 16, 16, S)
        own = np.take_along_axis(Y, v[:, :, None, :], 3)
        D = np.add.reduce(np.abs(y - own[:, :, :, None, :]), axis=2)
        p = np.argmax(D, axis=2); q = np.argmin(D, axis=2)
        big = at(D, p) > lim + (A % 16)[:, :, None]
        ap = at(a, p); bp = at(b, p); bq = at(b, q)
        yp = np.take_along_axis(y, p[:, :, None, None, :], 3)[:, :, :, 0]; yq = np.take_along_axis(y, q[:, :, None, None, :], 3)[:, :, :, 0]
        n = W0 + t * S + lane; new = own + np.sign(yq - own); u = np.add.reduce(own, axis=2)
        Y[..., W0 + t * S:W0 + (t + 1) * S] = yp
        C[..., W0 + t * S:W0 + (t + 1) * S] = a
        C[rk, gr, p, v] = (ap + u + t + 1) % NA
        Y[rk4, gr4, row, v[:, :, None, :]] = new
        for r in range(N):
            for s in range(N - 1): Y[r, :, :, M + s * S:M + (s + 1) * S] = new[(r + 1 + s) % N]
        for i in range(S - 1, -1, -1):
            i0, i1 = np.nonzero(big[:, :, i])
            L[i0, i1, 1::2, ap[i0, i1, i]] = n[i]
        F[rk, gr, v] = np.where(big, F[rk, gr, v], F[rk, gr, bq])
        F = np.take_along_axis(F, F, 2)
        w = F[rk, gr, bp]
        v = np.where((w < M) | (w >= W0), w - w % S + lane, np.where(big, n, (v + S) % M))
        A = np.add.reduce(big.astype(np.int64), axis=2)
    return {"yo": Y.reshape(N, 128, W).astype(np.float32).astype(BF), "lo": L.reshape(N, 128, NA).astype(np.float32), "fo": np.stack([gtable(z) for z in F]).astype(np.float32)}

@@ -1,0 +1,831 @@
+from concourse.bass import DstId, RemoteDMATransfer
+from concourse.mybir import AluOpType as Alu, ActivationFunctionType as Act
+
+N, S, M, NA, RO = 4, 256, 1024, 2048, 3
+W0 = M + (N - 1) * S
+W = W0 + RO * S
+MAGIC = 12582912.0
+OFS = 1280.0
+
+f32, b16, h16, i32, u16 = "float32", "bfloat16", "float16", "int32", "uint16"
+SB = {
+    "LK": (NA, i32), "L": (16 + NA, f32), "C": (W0 + 2 * S, i32), "Y": (W, b16), "YF": (W0 + 2 * S, b16),
+    "FA": (W, b16), "FB": (W, b16), "FW": (112, i32), "FL": (160, u16), "FO": (160, f32),
+    "TH": (S, i32), "TF": (S, f32), "G": (4096, h16), "G1": (4096, f32), "YH": (4096, h16), "AB": (4096, b16),
+    "A32": (S, i32), "AU": (S, u16), "A1": (S, f32), "BC": (2 * S, u16), "B32": (2 * S, f32),
+    "OWN": (S, b16), "OT": (S, b16), "FV": (S, b16), "U": (S, f32),
+    "S0": (384, f32), "S1": (384, f32), "ST0": (400, b16), "ST1": (400, b16),
+    "PR": (5 * S, h16), "LU": (64, u16), "AL": (16, f32), "AR": (S, f32), "EQ": (S, b16),
+    "OC": (16, u16), "OS": (32, u16), "VAL": (S, f32), "NR": (RO * S, f32),
+    "DF": (S, b16), "EF": (S, b16), "PQ": (4 * S, b16), "SG": (2 * S, b16), "RP": (S, f32),
+    "NEW": (RO * S, b16), "LAND": (RO * (N - 1) * S, b16),
+    "PC": (S, f32), "CN": (S, i32), "MR": (S, b16), "MT": (S, b16), "X1": (S, b16), "PW": (S, b16), "VU": (16, u16),
+    "AI": (128, f32), "AJ": (128, b16),
+    "ONE": (128, b16), "ID": (128, b16), "NI": (128, b16), "HI": (128, b16), "BO": (128, b16), "TMP": (128, b16),
+    "BIG": (128, b16), "TM2": (128, b16), "ZD": (2064, b16), "ZT": (2064, b16), "ZE": (144, b16), "ZF": (144, b16),
+    "ZV": (144, b16), "ZX": (144, b16), "GO": (16, b16), "GX": (128, f32), "S16": (128, f32), "E0": (128, b16),
+    "RM": (S, f32), "KC": (S, b16), "K0": (128, b16), "C128": (128, b16), "C16": (128, b16),
+    "BLI": (24, i32), "BL": (24, u16), "SF": (32, f32), "PI": (4, i32), "PF": (4, f32), "IDL": (160, f32), "LI": (16, b16),
+    "R": (1024, b16), "HF": (S, b16), "CT": (16, f32), "LO": (S, b16),
+}
+SCRATCH = {k: ("sbuf", [128, v[0]], v[1]) for k, v in SB.items()}
+for _k in range(8):
+    SCRATCH["P%d" % _k] = ("psum", [128, 512], f32)
+GUESS = [dict(cyc=1.04, gath=1.62, scat=3.95, pe=0.55, dma=0.004, rem=4000.0, hop=100.0),
+         dict(cyc=0.92, gath=1.05, scat=1.90, pe=0.65, dma=0.005, rem=5000.0, hop=150.0),
+         dict(cyc=1.15, gath=2.25, scat=6.20, pe=0.50, dma=0.003, rem=3500.0, hop=70.0)]
+FIX, DMA_FIX, LEAN, HEAT, SEED = 55.0, 2000.0, 0.5, 0.005, 1
+TURNS, NOISE, SHIFTS = 60, 0.3, 24000
+PLAN = {}
+GHOST_POOL = True
+NDMA = 20
+
+
+def arrange(kind, size, queue, before, after):
+    n_ops = len(kind)
+    cost = [[size[n] * G[kind[n]] + (0.0 if kind[n] in ("pe", "dma", "rem") else FIX) for n in range(n_ops)] for G in GUESS]
+    code = [1 if k == "dma" else 2 if k == "rem" else 0 for k in kind]
+    pred = [sorted(set(before[n]) | set(after[n])) for n in range(n_ops)]
+    succ = [[] for n in range(n_ops)]
+    for n in range(n_ops):
+        for m in pred[n]:
+            succ[m].append(n)
+
+    def span(seq, j):
+        c, hop = cost[j], GUESS[j]["hop"]
+        free, done, dfree = [0.0] * 5, [0.0] * n_ops, 0.0
+        for n in seq:
+            q = queue[n]
+            s = free[q]
+            for m in before[n]:
+                if done[m] > s:
+                    s = done[m]
+            if code[n] == 0:
+                s += c[n]
+                free[q] = s
+                done[n] = s + hop
+            elif code[n] == 1:
+                free[q] = s + 60.0
+                dfree = max(dfree, s + 0.7 * DMA_FIX) + c[n]
+                done[n] = dfree + 0.3 * DMA_FIX + hop
+            else:
+                free[q] = s + 1000.0
+                done[n] = s + c[n] + hop
+        return done
+
+    hop = GUESS[0]["hop"]
+    full = [cost[0][n] + (DMA_FIX if code[n] == 1 else 0.0) for n in range(n_ops)]
+    rest = [0.0] * n_ops
+    for n in range(n_ops - 1, -1, -1):
+        rest[n] = full[n] + max([rest[m] + hop for m in succ[n]], default=0.0)
+    missing = [len(p) for p in pred]
+    ready = {n: 0.0 for n in range(n_ops) if missing[n] == 0}
+    free, done, seq = [0.0] * 5, {}, []
+    while ready:
+        begin = {n: max(r, free[queue[n]]) for n, r in ready.items()}
+        n0 = min(begin, key=lambda n: (begin[n], n))
+        n = max((m for m in begin if queue[m] == queue[n0] and begin[m] <= begin[n0] + 1.5 * hop), key=lambda m: (rest[m], -m))
+        done[n] = begin[n] + full[n]
+        free[queue[n]] = done[n] if code[n] == 0 else begin[n] + 60.0
+        del ready[n]
+        seq.append(n)
+        for m in succ[n]:
+            missing[m] -= 1
+            if missing[m] == 0:
+                ready[m] = max([done[k] + hop for k in before[m]], default=0.0)
+    unit = [max(span(seq, j)) for j in range(len(GUESS))]
+
+    res = [5 if code[n] == 1 else queue[n] for n in range(n_ops)]
+    waited = [set(b) for b in before]
+
+    lead0 = [0.7 * DMA_FIX if code[n] == 1 else 0.0 for n in range(n_ops)]
+    split = {back: [([m for m in near[n] if ((n in waited[m]) if back else (m in waited[n]))],
+                     [m for m in near[n] if not ((n in waited[m]) if back else (m in waited[n]))]) for n in range(n_ops)]
+             for back, near in ((False, pred), (True, succ))}
+
+    def pack(order, near, c, back):
+        lead = lead0
+        busy = [1000.0 if code[n] == 2 else c[n] for n in range(n_ops)]
+        tail = [0.3 * DMA_FIX if code[n] == 1 else c[n] - busy[n] for n in range(n_ops)]
+        if back:
+            lead, tail = tail, lead
+        line, end, first = [[] for q in range(6)], [0.0] * n_ops, [0.0] * n_ops
+        ties = split[back]
+        for n in order:
+            s = -hop
+            tied, loose = ties[n]
+            for m in tied:
+                if end[m] > s:
+                    s = end[m]
+            s += hop + lead[n]
+            for m in loose:
+                s = max(s, end[m] - tail[m])
+            ln = line[res[n]]
+            k = top = len(ln)
+            while k and ln[k - 1][1] > s:
+                k -= 1
+            while k < top and s + busy[n] > ln[k][0]:
+                if ln[k][1] > s:
+                    s = ln[k][1]
+                k += 1
+            ln.insert(k, (s, s + busy[n]))
+            first[n], end[n] = s - lead[n], s + busy[n] + tail[n]
+        return first, end
+
+    def rank_by(key, near):
+        key = list(key)
+        for n in (range(n_ops) if near is pred else range(n_ops - 1, -1, -1)):
+            for m in near[n]:
+                if key[m] >= key[n]:
+                    key[n] = key[m] + 0.001
+        return sorted(range(n_ops), key=lambda n: key[n])
+
+    def plain(s):
+        return sum(max(span(s, j)) / unit[j] for j in range(len(GUESS)))
+    best, seed, cur = plain(seq), SEED, list(seq)
+    for turn in range(TURNS):
+        c = []
+        for n in range(n_ops):
+            seed = (seed * 6364136223846793005 + 1442695040888963407) % 2 ** 64
+            c.append(cost[0][n] * (1.0 + NOISE * (((seed >> 33) & 1023) / 512.0 - 1.0)))
+        first, end = pack(cur, pred, c, False)
+        first, end = pack(rank_by([-x for x in end], succ), succ, c, True)
+        first, end = pack(rank_by([-x for x in end], pred), pred, cost[0], False)
+        cand = rank_by(first, pred)
+        w = plain(cand)
+        if w < best + 0.01:
+            cur = cand
+            if w < best:
+                best, seq = w, cand
+        elif turn % 8 == 7:
+            cur = list(seq)
+
+    def tight(s, j):
+        d, pairs, prev, lastq = span(s, j), [], {}, {}
+        for n in s:
+            prev[n] = lastq.get(queue[n])
+            lastq[queue[n]] = n
+        n = max(range(n_ops), key=lambda m: d[m])
+        while n is not None:
+            m = max(before[n], key=lambda k: d[k], default=None)
+            p = prev[n]
+            if p is not None and code[p] == 0 and (m is None or d[p] - GUESS[j]["hop"] >= d[m]):
+                if p not in pred[n]:
+                    pairs.append((n, p))
+                n = p
+            else:
+                n = m if m is not None else p
+        return pairs
+    key = pack(seq, pred, cost[0], False)[0]
+    now = best = 100.0
+    cur = seq
+    pairs = tight(cur, 0)
+    for turn in range(SHIFTS):
+        new = list(key)
+        seed = (seed * 6364136223846793005 + 1442695040888963407) % 2 ** 64
+        if turn % 16 == 0:
+            pairs = tight(cur, (seed >> 40) % len(GUESS))
+        for rep in range(1 + (seed >> 60) % 3):
+            seed = (seed * 6364136223846793005 + 1442695040888963407) % 2 ** 64
+            n = (seed >> 33) % n_ops
+            far = ((seed >> 12) & 1023) / 1024.0 * (3000.0 if (seed >> 24) & 1 else 500.0)
+            if (seed >> 26) & 1 and pairs:
+                n, p = pairs[(seed >> 33) % len(pairs)]
+                if (seed >> 27) & 1:
+                    new[n] = key[p] - 1.0 - far * ((seed >> 28) & 1)
+                else:
+                    new[p] = key[n] + 1.0 + far * ((seed >> 28) & 1)
+            else:
+                new[n] += far if (seed >> 27) & 1 else -far
+            if new[n] < key[n]:
+                stack = [n]
+                while stack:
+                    x = stack.pop()
+                    for m in pred[x]:
+                        if new[m] >= new[x]:
+                            new[m] = new[x] - 0.001
+                            stack.append(m)
+        first, end = pack(rank_by(new, pred), pred, cost[0], False)
+        w = 3.0 * (max(end) + LEAN * sum(end) / n_ops) / unit[0]
+        if w <= now + HEAT * (1.0 - turn / SHIFTS) * ((seed >> 50) & 7) / 7.0:
+            cand = rank_by(first, pred)
+            now, key, cur = w, first, cand
+            if w < best:
+                best, seq = w, cand
+
+    return seq
+
+
+SEMAPHORES = ["pe", "dve", "act", "pool", "sent", "out"] + ["arr%d" % t for t in range(RO)] + ["d%d" % k for k in range(NDMA)]
+
+
+def rank_program(g, core, T, topo):
+    rank = T.rank_of(core)
+    if rank is None:
+        return
+    Q = {"pe": g.tensor, "dve": g.vector, "act": g.scalar, "pool": g, "sp": g.sync}
+    ops = []
+
+    def V(name, a=0, b=None, s=1, p=None):
+        if b is None:
+            b = T[name].shape[1]
+        ap = T[name][:, a:b:s] if p is None else T[name][p[0]:p[1]:p[2], a:b:s]
+        n = len(range(a, b, s))
+        if name[0] == "P" and name[1:].isdigit():
+            return (ap, [(name, 0, 512)], [], n, 4, "p")
+        rows = 128 if p is None else len(range(*p))
+        return (ap, [(name, a, b)], [], n, 4 if SB[name][1] in (f32, i32) else 2, "s", rows)
+
+    def X(win, off):
+        return (win[0].indirect(off[0]), win[1], off[1], 16 * off[3], win[4], "x")
+
+    def H(ap):
+        return (ap, [], [], 0, 4, "h")
+
+    def op(eng, fn, out, ins, dma=False, pre=(), cost=None, per=1.0):
+        rd = list(out[2])
+        ins = [x for x in ins if isinstance(x, tuple)]
+        for x in ins:
+            rd += x[1] + x[2]
+        if cost is None:
+            n = out[3]
+            wide = [x for x in ins + [out] if x[3] == n]
+            if dma:
+                side = out if out[5] == "s" else ins[0]
+                cost = ("dma", side[3] * side[4] * side[6])
+            elif eng == "pool":
+                cost = ("cyc", 100 + 2 * n)
+            elif out[5] == "x":
+                cost = ("scat", n)
+            elif any(x[5] == "x" for x in ins):
+                cost = ("gath", n)
+            elif eng == "act":
+                cost = ("cyc", n)
+            else:
+                if not all(x[5] == "s" for x in ins if x[3] == n):
+                    per = 1.0
+                cost = ("cyc", max(64, n * per * (0.5 if all(x[4] == 2 for x in wide) else 1.0)))
+        ops.append({"e": eng, "fn": fn, "w": out[1], "r": rd, "dma": dma, "pre": pre, "c": cost})
+
+    def a_(x):
+        return x[0] if isinstance(x, tuple) else x
+
+    def mms(items):
+        def fn():
+            for o, l, r, st, sp in items:
+                ins = g.tensor.matmul(o[0], l[0], r[0], st, sp)
+            return ins
+        op("pe", fn, items[0][0], [x for it in items for x in it[1:3]],
+           cost=("pe", sum(max(min(64, l[3]), r[3]) * (4 if r[4] == 4 else 1) for o, l, r, st, sp in items)))
+
+    def mm(o, l, r, st=True, sp=True):
+        mms([(o, l, r, st, sp)])
+
+    def grp(o, pairs):
+        return [(o, l, r, n == 0, n == len(pairs) - 1) for n, (l, r) in enumerate(pairs)]
+
+    def group(o, pairs):
+        mms(grp(o, pairs))
+
+    def act(o, i, f=Act.Identity, bias=0.0, scale=1.0, pre=()):
+        op("act", lambda: g.scalar.activation(o[0], i[0], f, bias=a_(bias), scale=a_(scale)), o, [i, bias, scale], pre=pre)
+
+    def cp(o, i):
+        op("dve", lambda: g.vector.tensor_copy(o[0], i[0]), o, [i])
+
+    def tt(o, x, y, f):
+        op("dve", lambda: g.vector.tensor_tensor(o[0], x[0], y[0], f), o, [x, y], per=2.0)
+
+    def ts(o, x, s1, f0, s2=None, f1=None):
+        if f1 is None:
+            op("dve", lambda: g.vector.tensor_scalar(o[0], x[0], a_(s1), None, f0), o, [x, s1])
+        else:
+            op("dve", lambda: g.vector.tensor_scalar(o[0], x[0], a_(s1), a_(s2), f0, f1), o, [x, s1, s2])
+
+    def ms(o, c):
+        op("dve", lambda: g.vector.memset(o[0], c), o, [])
+
+    def iota(o, pat, base=0, cm=0):
+        if SB[o[1][0][0]][1] == i32:
+            op("pool", lambda: g.iota(o[0], pat, base, cm), o, [])
+        else:
+            op("pool", lambda: g.iota(o[0], pat, base, cm, allow_small_or_imprecise_dtypes=True), o, [])
+
+    def fill(o, c):
+        iota(o, [[0, o[3]]], c)
+
+    def sel(o, i, pat, cmp, base, cm, other=0.0, pre=()):
+        op("pool", lambda: g.affine_select(o[0], i[0], pat, cmp, other, base, cm), o, [i], pre=pre)
+
+    def move(o, i, pre=()):
+        sel(o, i, [[0, o[3]]], Alu.is_ge, 0, 0, pre=pre)
+
+    def dma(q, o, i, pre=()):
+        op(q, lambda: Q[q].dma_start(o[0], i[0]), o, [i], dma=True, pre=pre)
+
+    def win(z, blk, r):
+        return V(z, 128 * blk + 15 - r, 128 * blk + 143 - r)
+
+    def to_list(o, z, src, a, b, first=True, last=True, per_r=False):
+        mms([(o, win(z, r if per_r else 0, r), V(src, a + r, b, 16), first and r == 0, last and r == 15) for r in range(16)])
+
+    others = [(rank + N - 1 - s) % N for s in range(N - 1)]
+    far = max(range(N - 1), key=lambda s: 0 if (topo.mates(topo.chip(core), topo.chip(T.cores[others[s]]))
+                                               or topo.same_plane(topo.chip(core), topo.chip(T.cores[others[s]]))) else 1)
+    eng = topo.engines(core, T.cores[others[far]])
+    near = [s for s in range(N - 1) if s != far]
+    share = {far: eng[1::2], near[0]: eng[0::2][:len(eng) // 4], near[1]: eng[0::2][len(eng) // 4:]}
+    nsig = len(eng)
+
+    def send(t):
+        src = V("NEW", t * S, (t + 1) * S)
+        trs = []
+        for s in range(N - 1):
+            rid, pid, _ = topo.addr(T.cores[others[s]])
+            c0 = (t * (N - 1) + s) * S
+            trs.append(RemoteDMATransfer(dst_ids=[DstId(rid=rid, pnc=pid)], dma_engine_mask=sum(1 << e for e in share[s]),
+                                         remote_sem=T.sem["arr%d" % t], src=src[0], dst=T.LAND[:, c0:c0 + S]))
+        op("pool", lambda: g.remote_dma_fused(trs, local_sem=T.sem.sent), H(None), [src], cost=("rem", 1))
+        ops[-1]["send"] = "arr%d" % t
+
+    dma("sp", V("C", 0, S), H(T.cl[:, 0:S]))
+    dma("act", V("FW"), H(T.fw0[:, :]))
+    for q in range(4):
+        dma("sp", V("LK", 512 * q, 512 * (q + 1)), H(T.lk[:, 512 * q:512 * (q + 1)]))
+    dma("sp", V("Y", 0, W0), H(T.y0[:, :]))
+    dma("sp", V("TH", p=(0, 8, 1)), H(T.th[:, :]))
+    dma("sp", V("C", S, M), H(T.cl[:, S:M]))
+    dma("sp", V("C", W0, W0 + S), H(T.cl[:, 0:S]))
+
+    ms(V("ONE"), 1.0)
+    ms(V("HF"), 0.0)
+    ms(V("ZD"), 0.0)
+    iota(V("PI", 0, 1), [[0, 1]], 0, 1)
+    iota(V("LO"), [[1, S]])
+    iota(V("HF", 1, 160, 16), [[S, 10]])
+    iota(V("HF", 3, 64, 16), [[S, 4]])
+    iota(V("HF", 115, 160, 16), [[S, 3]], W0)
+    iota(V("HF", 4, 48, 16), [[S, 3]], S)
+    iota(V("HF", 132, 160, 16), [[S, 2]], S)
+    sel(V("ZD", 15, 2063, 16), V("ONE"), [[-1, 16], [-16, 8]], Alu.is_equal, 0, 1)
+    sel(V("ID"), V("ONE"), [[-1, 128]], Alu.is_equal, 0, 1)
+    for a, b, s, c in ((66, 112, 16, 1.0), (69, 112, 16, 1.0), (162, 163, 1, S - W0), (165, 166, 1, 2 * S), (178, 179, 1, W0),
+                       (179, 181, 1, 1.0), (194, 195, 1, -(W0 + S)), (210, 211, 1, W0 + S), (211, 212, 1, 1.0), (224, 225, 1, 1.0)):
+        ms(V("HF", a, b, s), float(c))
+    cp(V("AU"), V("C", 0, S))
+    cp(V("FL", 0, 112), V("FW"))
+    to_list(V("P7", 0, 16), "ZD", "HF", 0, S, per_r=True)
+    act(V("CT"), V("P7", 0, 16))
+    ts(V("PI", 1, 2), V("PI", 0, 1), 15, Alu.bitwise_and)
+    ts(V("PI", 2, 3), V("PI", 0, 1), 63, Alu.bitwise_and)
+    ts(V("PI", 3, 4), V("PI", 0, 1), 1, Alu.bitwise_and)
+    fill(V("ZE"), 0)
+    fill(V("BIG"), -4096)
+    fill(V("S16"), 16)
+    cp(V("PF"), V("PI"))
+    sel(V("TMP"), V("ONE"), [[-16, 8], [0, 16]], Alu.is_ge, 0, 1)
+    sel(V("BO"), V("TMP"), [[16, 8], [0, 16]], Alu.is_ge, 15, -1)
+    iota(V("R"), [[1, 64], [0, 16]])
+    sel(V("GX"), V("S16"), [[-1, 8], [0, 16]], Alu.is_equal, 0, 1)
+    iota(V("KC"), [[-15, 2], [0, 8], [-1, 16]], 15)
+    iota(V("BLI", 0, 16), [[1, 16]])
+    iota(V("BLI", 16, 24), [[1, 8]])
+    fill(V("K0"), 120)
+    iota(V("IDL"), [[16, 160]])
+    iota(V("NR"), [[1, RO * S]], W0)
+    act(V("YF", 0, W0), X(V("Y", 0, W0), V("FL", 0, 112)), scale=0.5)
+    act(V("NI"), V("ID"), scale=-1.0)
+    act(V("OWN"), V("Y", 0, S))
+    for B in range(10):
+        act(V("FB", S * B, S * (B + 1)), V("LO"), scale=V("CT", 14, 15), bias=V("CT", B, B + 1))
+    for q in range(3):
+        cp(V("L", 16 + 512 * q, 16 + 512 * (q + 1)), V("LK", 512 * q, 512 * (q + 1)))
+
+    def late_a():
+        ts(V("R"), V("R"), V("PF", 2, 3), Alu.is_equal)
+        ts(V("GO", 0, 8), V("BO", 0, 128, 16), 16.0, Alu.mult)
+        ts(V("GO", 8, 16), V("BO", 0, 128, 16), -16.0, Alu.mult)
+        sel(V("C128"), V("ONE"), [[0, 128]], Alu.is_equal, 0, 1)
+        cp(V("TF", p=(0, 8, 1)), V("TH", p=(0, 8, 1)))
+
+    def late_b():
+        for h in range(2):
+            mm(V("P7", 128 * h, 128 * (h + 1)), V("TF", 128 * h, 128 * (h + 1), p=(0, 8, 1)), V("GX", p=(0, 8, 1)))
+        for h in range(2):
+            act(V("S%d" % h, 256, 384), V("P7", 128 * h, 128 * (h + 1)), bias=15.0)
+        act(V("FA", 0, W0), X(V("FB"), V("FL", 0, 112)))
+        dma("sp", V("FA", W0, W), V("FB", W0, W))
+        fill(V("RM"), 0)
+        fill(V("RM", 0, S, 16), -16000000)
+        sel(V("E0"), V("ONE"), [[0, 8], [1, 16]], Alu.is_equal, 0, 0)
+        move(V("FV"), V("FA", 0, S))
+        cp(V("BL"), V("BLI"))
+        fill(V("ST0", 15, 16), 1)
+        fill(V("ST1", 15, 16), 1)
+        move(V("ZE", 15, 143, 16), V("BO", 0, 128, 16))
+        cp(V("L", 16 + 1536, 16 + NA), V("LK", 1536, NA))
+        fill(V("L", 0, 16), 0)
+        dma("sp", H(T.lo[0:128:2, :]), V("L", 16, 16 + NA, p=(0, 128, 2)))
+
+    def late_c():
+        for q in range(4):
+            fill(V("ZT", 516 * q, 516 * (q + 1)), 0)
+        sel(V("TM2"), V("BIG"), [[0, 16], [-16, 8]], Alu.is_ge, 0, 1)
+        sel(V("ZT", 15, 2063, 16), V("TM2"), [[1, 16], [16, 8]], Alu.is_gt, 0, -1)
+        tt(V("ZF", 0, 143), V("ZD", 0, 143), V("ZD", 128, 271), Alu.add)
+        tt(V("ZV", 0, 143), V("ZD", 256, 399), V("ZD", 384, 527), Alu.add)
+        tt(V("ZX", 0, 143), V("ZD", 512, 655), V("ZD", 640, 783), Alu.add)
+        ts(V("IDL"), V("IDL"), V("PF", 1, 2), Alu.add)
+        fill(V("C16"), 16)
+        fill(V("C", M, W0), 0)
+        cp(V("FL", 112, 160), V("IDL", 112, 160))
+        act(V("LI"), V("IDL", 0, 16))
+        act(V("HI"), V("ID"), scale=0.5)
+        act(V("NR"), V("NR"), scale=V("PF", 3, 4))
+        move(V("FO", 144, 160), V("IDL", 144, 160))
+
+    def nrs():
+        return [(V("C16"), V("ST%d" % h, 272, 400)) for h in range(2)]
+
+    def keys0(h, more):
+        bank = "P%d" % (5 + h)
+        mms([(V(bank, 0, S), V("C128"), V("KC"), True, False)] + [(V(bank, 0, 128), l, r, False, False) for l, r in more])
+
+    pend = []
+    for t in range(RO):
+        wt = W0 + t * S
+        F, F2 = ("FA", "FB") if t % 2 == 0 else ("FB", "FA")
+        last = t == RO - 1
+        a32 = V("C", 0, S) if t == 0 else V("A32")
+        fv = V("FV")
+        lwin = V("LK") if t == 0 else V("L", 16, 16 + NA)
+
+        def links(q):
+            for j in ((2 * q, 2 * q + 1) if q == 1 else (None,)):
+                c0, c1 = (64 * q, 64 * (q + 1)) if j is None else (32 * j, 32 * (j + 1))
+                ts(V("G", 16 * c0, 16 * c1), X(lwin, V("AU", c0, c1)), OFS, Alu.subtract)
+
+        def lists(q):
+            bank, c0 = "P%d" % (q // 2), 64 * (q % 2)
+            for j in range(2):
+                group(V(bank, 128 * j + c0, 128 * j + c0 + 64),
+                      [(win("ZD", (k + 5 * j) % 16, k), V("G", 1024 * q + k, 1024 * (q + 1), 16)) for k in range(16)])
+                if j == 0 or q == 0:
+                    ts(V("BC", S * j + 64 * q, S * j + 64 * (q + 1)), V(bank, 128 * j + c0, 128 * j + c0 + 64), OFS, Alu.add)
+            if q == 1:
+                ts(V("BC", S + 64, S + 128), V(bank, 192, S), OFS, Alu.add)
+            if q == 3:
+                ts(V("BC", S + 128, 2 * S), V(bank, 128, S), OFS, Alu.add)
+            if q % 2:
+                act(V("B32", S * (q // 2), S * (q // 2 + 1)), V(bank, 0, S))
+
+        def bl(j, o):
+            return V("BC", S * o + 32 * j, S * o + 32 * (j + 1))
+
+        def ga(j):
+            act(V("G1", 512 * j, 512 * (j + 1)), X(V("YF", 0, wt), bl(j, 0)), bias=1023.75)
+
+        def gb(j):
+            tt(V("YH", 512 * j, 512 * (j + 1)), X(V("YF", 0, wt), bl(j, 1)), V("G1", 512 * j, 512 * (j + 1)), Alu.add)
+            h, u = j // 4, (j % 4) // 2
+            group(V("P%d" % (2 + j % 3)), [(V("ID"), V("YH", 512 * j, 512 * (j + 1))),
+                                           (V("OT", 128 * h, 128 * (h + 1), p=(64 * u, 64 * u + 64, 1)),
+                                            V("R", 512 * (j % 2), 512 * (j % 2 + 1), p=(64 * u, 64 * u + 64, 1)))])
+
+        def ab(j):
+            act(V("AB", 512 * j, 512 * (j + 1)), V("P%d" % (2 + j % 3)), Act.Abs, bias=-1024.0)
+
+        def keys(h):
+            bank = "P%d" % (5 + h)
+            if t == 0:
+                keys0(h, [])
+            for a, b in (((0, 128),) if h == 0 else ((0, 64), (64, 96), (96, 128))):
+                mms([(V(bank, k, S, 16, p=(a, b, 1)), V("AB", 2048 * h + 16 * a + k, 2048 * h + 16 * b, 16), V("GO"), False,
+                      k == 15) for k in range(16)])
+
+        def choose(h):
+            sb, st = "S%d" % h, "ST%d" % h
+            o, d0, d1 = V(sb, 0, S), V("RM"), V("P%d" % (5 + h), 0, S)
+            op("dve", lambda: g.vector.tensor_tensor_scan(o[0], d0[0], d1[0], 0.0, Alu.add, Alu.max), o, [d0, d1])
+            ops[-1]["hint"] = list(early)
+            cp(V("SF", 16 * h, 16 * (h + 1)), V(sb, 15, S, 16))
+            tt(V(st, 16, 400), X(V("SF", 16 * h, 16 * (h + 1)), V("BL", 0, 24)), V(sb), Alu.is_le)
+
+            def hot(c):
+                return [(V(st, c, c + 128), V("ID")), (V(st, c - 1, c + 127), V("NI")), (V("E0"), V("ID"))]
+            mms(grp(oh(h, 0), hot(144)) + grp(oh(h, 1), [(V(st, 272, 400), V("ID"))]))
+            mms(grp(oh(h, 3), hot(16) + [(V(st, 272, 400), V("NI"))]) + grp(oh(h, 2), hot(16)))
+
+        def oh(h, j):
+            return V("P4" if h == 1 and j > 1 else "P%d" % h, 128 * j, 128 * (j + 1))
+
+        def half(name, h, c0=0):
+            return V(name, c0 + 128 * h, c0 + 128 * (h + 1))
+
+        def picks_q(h):
+            for o in range(2):
+                tt(half("PR", h, S * (3 + o)), oh(h, 0), half("B32", o, S * h), Alu.mult)
+
+        def picks_p(h):
+            tt(half("PR", h), oh(h, 3), half("A1", h), Alu.mult)
+            for o in range(2):
+                tt(half("PR", h, S * (1 + o)), oh(h, 2), half("B32", o, S * h), Alu.mult)
+
+        early = []
+        links(0)
+        if t > 0:
+            act(V("OWN"), X(V("Y", 0, wt), V("VU")))
+            act(V("FV"), X(V(F, 0, wt), V("VU")))
+        for h in range(2):
+            mm(V("P7", 128 * h, 128 * (h + 1)), V("OWN", 128 * h, 128 * (h + 1)), V("NI"))
+        if not last:
+            mm(V("P7", S, 2 * S), V("BO"), V("OWN"))
+        act(V("OT"), V("P7", 0, S))
+        if not last:
+            act(V("U"), V("P7", S, 2 * S), bias=float(t + 1))
+        if t == 0:
+            late_a()
+        links(1)
+        lists(0)
+        first_list = len(ops) - 3
+        ga(0)
+        ga(1)
+        for fn in pend:
+            fn()
+        pend = []
+        gb(0)
+        links(2)
+        ops[-1]["hint"] = [first_list]
+        lists(1)
+        ab(0)
+        ga(2)
+        gb(1)
+        ga(3)
+        ab(1)
+        gb(2)
+        links(3)
+        lists(2)
+        lists(3)
+        ab(2)
+        ga(4)
+        gb(3)
+        if t == 0:
+            late_b()
+        ts(V("A1"), a32, 1.0, Alu.add)
+        ga(5)
+        ab(3)
+        keys(0)
+        gb(4)
+        ga(6)
+        ab(4)
+        if t == 0:
+            late_c()
+        gb(5)
+        choose(0)
+        ga(7)
+        ab(5)
+        gb(6)
+        ab(6)
+        gb(7)
+        ab(7)
+        keys(1)
+        picks_q(0)
+        picks_p(0)
+        early = range(len(ops) - 5, len(ops))
+
+        choose(1)
+        picks_q(1)
+        to_list(V("P2", 0, 32), "ZE", "PR", 3 * S, 5 * S)
+        picks_p(1)
+        to_list(V("P3", 0, 48), "ZE", "PR", 0, 3 * S)
+        mm(V("P3", S, 2 * S), V("BO"), V("PR", 0, S))
+        to_list(V("P5", 0, 16), "ZE", "PR", 0, S, last=False)
+        ts(V("LU", 32, 64), V("P2", 0, 32), OFS, Alu.add)
+        act(V("PQ", 2 * S, 4 * S), X(V("YF", 0, wt), V("LU", 32, 64)))
+        group(V("P7", 0, S), [(V("ID"), V("PQ", 2 * S, 3 * S)), (V("ID"), V("PQ", 3 * S, 4 * S)), (V("NI"), V("OWN"))])
+        tt(V("DF"), X(V(F, 0, wt), V("LU", 32, 48)), fv, Alu.subtract)
+        ts(V("LU", 0, 32), V("P3", 16, 48), OFS, Alu.add)
+        for h in range(2):
+            tt(half("EF", h), oh(h, 1), half("DF", h), Alu.mult)
+        act(V("AL"), V("P3", 0, 16))
+        act(V("AR"), V("P3", S, 2 * S))
+        act(V("SG", 0, S), V("P7", 0, S), Act.Sign, bias=-0.75)
+        act(V("SG", S, 2 * S), V("P7", 0, S), Act.Sign, bias=0.25)
+        group(V("P7", S, 2 * S), [(V("ID"), V("OWN")), (V("HI"), V("SG", 0, S)), (V("HI"), V("SG", S, 2 * S))])
+        tt(V(F, 0, S) if t == 0 else X(V(F, 0, wt), V("VU")), V("EF"), fv, Alu.add)
+        new = V("NEW", t * S, (t + 1) * S)
+        act(new, V("P7", S, 2 * S))
+        send(t)
+        nb = S if t == 0 else M
+        to_list(V("P2", 0, nb // 16), "ZF", F, 0, nb)
+        if t > 0:
+            to_list(V("P2", 64, 64 + 16 * t), "ZF", F, W0, wt)
+        act(V(F2, M, W0), X(V(F, 0, wt), V("FL", 64, 112)))
+        tt(V("EQ"), X(V("AL"), V("BL", 0, 16)), V("AR"), Alu.is_equal)
+        to_list(V("P5", 0, 16), "ZT", "EQ", 0, S, first=False, per_r=True)
+        cp(V("FL", 0, nb // 16), V("P2", 0, nb // 16))
+        if t > 0:
+            cp(V("FL", 112, 112 + 16 * t), V("P2", 64, 64 + 16 * t))
+        act(V(F2, 0, M), X(V(F, 0, wt), V("FL", 0, 64)))
+        if t > 0:
+            act(V(F2, W0, wt), X(V(F, 0, wt), V("FL", 112, 112 + 16 * t)))
+        ts(V("OC"), V("P5", 0, 16), 15.0, Alu.add, V("PF", 1, 2), Alu.max)
+        ts(V("OS", 0, 32, 2), V("P5", 0, 16), 15.0, Alu.add, V("PF", 1, 2), Alu.max)
+        act(V("VAL"), X(V("L"), V("OC")))
+
+        def ys():
+            if t == 0:
+                move(V("Y", 0, S), new)
+            else:
+                cp(X(V("Y", 0, wt), V("VU")), new)
+
+        def room():
+            act(V("PQ", 0, 2 * S), X(V("YF", 0, wt), V("LU", 0, 32)))
+            group(V("P7", 0, S), [(V("ID"), V("PQ", 0, S)), (V("ID"), V("PQ", S, 2 * S))])
+            act(V("RP"), V("P7", 0, S), bias=MAGIC, scale=1.0 - 2.0 ** -10)
+            act(V("Y", wt, wt + S), V("RP"), bias=-MAGIC)
+
+        def f2list(bank, a, b):
+            to_list(V(bank, a // 16, b // 16), "ZF", F2, a, b)
+
+        def c1():
+            for h in range(2):
+                tt(half("PC", h), oh(h, 2), half("U", h), Alu.mult)
+
+        def c2():
+            tt(V("C", 0, S) if t == 0 else V("CN"), V("PC"), a32, Alu.add)
+
+        def c3():
+            if t > 0:
+                cp(X(V("C", 0, wt), V("VU")), V("CN"))
+
+        def m1():
+            if t == 0:
+                for h in range(2):
+                    act(half("MR", h), oh(h, 1), bias=V("CT", 11, 12), scale=V("CT", 10, 11))
+            else:
+                for h in range(2):
+                    tt(half("MT", h), oh(h, 1), half("X1", h), Alu.mult)
+                act(V("MR"), V("MT"), bias=V("CT", 13, 14))
+
+        def l1():
+            f2list("P2", M, W0)
+            cp(V("FL", 64, 112), V("P2", 64, 112))
+
+        def l2():
+            f2list("P3", 0, M)
+            if t > 0:
+                f2list("P3", W0, wt)
+            cp(V("FL", 0, 64), V("P3", 0, 64))
+            if t > 0:
+                cp(V("FL", 112, 112 + 16 * t), V("P3", 112, 112 + 16 * t))
+
+        def yf():
+            c0 = t * (N - 1) * S
+            (move if GHOST_POOL else act)(V("Y", M, W0), V("LAND", c0, c0 + (N - 1) * S), pre=[("arr%d" % t, nsig)])
+            act(V("YF", 0, wt + S), X(V("Y", 0, wt + S), V("FL", 0, 112 + 16 * (t + 1))), scale=0.5)
+
+        def w1():
+            tt(V("PW"), X(V(F2, 0, wt), V("LU", 0, 16)), V("MR"), Alu.mult)
+            mm(V("P6", 0, 16), V("ID"), V("LI"), True, False)
+            to_list(V("P6", 0, 16), "ZV", "PW", 0, S, first=False)
+            if t == 0:
+                mm(V("P7", 0, S), win("ZX", 0, 2), V("PW"))
+
+        def w2():
+            cp(V("VU"), V("P6", 0, 16))
+
+        def w3():
+            ts(V("A32"), X(V("C", 0, wt + S), V("VU")), NA - 1, Alu.bitwise_and)
+
+        def w4():
+            cp(V("AU"), V("A32"))
+            if t == 0:
+                dma("sp", V("C", wt + S, wt + 2 * S), V("A32"))
+
+        def count():
+            group(V("P7", 0, 128), nrs() + [(V("C128"), V("K0"))])
+            act(V("AI"), V("P7", 0, 128), bias=MAGIC + 16.0, scale=-1.0 / 256)
+            act(V("AJ"), V("AI"), bias=-256.0 * MAGIC - 4096.0, scale=256.0)
+            for h in range(2):
+                keys0(h, nrs() + [(V("C128"), V("AJ"))])
+
+        def x1():
+            act(V("X1"), V("P7", 0, S), bias=V("CT", 12, 13))
+
+        def out_y():
+            dma("act", H(T.yo[:, W0:W]), V("Y", W0, W))
+            dma("act", H(T.yo[:, 0:M]), V("Y", 0, M))
+
+        def out_f():
+            f2list("P7", 0, M)
+            f2list("P7", M, wt)
+            act(V("FO", 0, wt // 16), V("P7", 0, wt // 16))
+            dma("act", H(T.fo[:, :]), V("FO"))
+
+        if last:
+            between = {}
+            after = [lambda: dma("sp", H(T.lo[1:128:2, :]), V("L", 16, 16 + NA, p=(1, 128, 2))), room, ys, out_y, out_f,
+                     lambda: dma("sp", H(T.yo[:, M:W0]), V("LAND", t * (N - 1) * S, (t + 1) * (N - 1) * S),
+                                 pre=[("arr%d" % t, nsig)])]
+        else:
+            between = {15: [ys, room], 14: [m1], 13: [l1], 12: [c1], 11: [l2], 10: [c2], 9: [w1, yf], 8: [c3], 7: [w2],
+                       6: [w3], 5: [w4]}
+            after = []
+            pend = [count]
+        for c in range(15, -1, -1):
+            tt(X(V("L"), V("OS", 2 * c, 2 * c + 1)), V("VAL", 16 * c, 16 * (c + 1)),
+               V("NR", t * S + 16 * c, t * S + 16 * (c + 1)), Alu.max)
+            for fn in between.get(c, ()):
+                fn()
+        if t == 0:
+            x1()
+        n0 = len(ops)
+        for fn in after:
+            fn()
+        for o in ops[n0:]:
+            o["end"] = True
+
+    seen, sends, lastdma = {}, {}, {}
+    for n, o in enumerate(ops):
+        e = o["e"]
+        deps, order = set(), set()
+        for kind, regs in (("r", o["r"]), ("w", o["w"])):
+            for name, a, b in regs:
+                psum = name[0] == "P" and name[1:].isdigit()
+                for m, k2, a2, b2 in seen.get(name, ()):
+                    if a2 < b and a < b2 and m != n:
+                        same = ops[m]["e"] == e and not ops[m]["dma"]
+                        if same and e == "pe":
+                            if psum:
+                                order.add(m)
+                        elif kind == "w" or k2 == "w" or (psum and not same):
+                            deps.add(m)
+        for kind, regs in (("r", o["r"]), ("w", o["w"])):
+            for name, a, b in regs:
+                lst = seen.setdefault(name, [])
+                if kind == "w":
+                    lst[:] = [x for x in lst if not (a <= x[2] and x[3] <= b)]
+                lst.append((n, kind, a, b))
+        if "send" in o:
+            sends[o["send"]] = n
+        late = {sends[name] for name, v in o["pre"]}
+        if o["dma"] and not o["r"]:
+            order |= {lastdma[e]} if e in lastdma else set()
+            lastdma[e] = n
+        o["deps"], o["order"], o["late"] = deps, order | set(o.get("hint", ())), late
+
+    if "seq" not in PLAN:
+        names = sorted(Q)
+        PLAN["seq"] = arrange([o["c"][0] for o in ops], [o["c"][1] for o in ops], [names.index(o["e"]) for o in ops],
+                              [sorted(o["deps"] | o["late"]) for o in ops], [sorted(o["order"]) for o in ops])
+    seq = PLAN["seq"]
+    place = {n: k for k, n in enumerate(seq)}
+    ops = [ops[n] for n in seq]
+
+    known = {e: {} for e in Q}
+    clock, waits, needed = [], [], set()
+    ndma = 0
+    for n, o in enumerate(ops):
+        e = o["e"]
+        mine = []
+        for m in sorted((place[k] for k in o["deps"]), reverse=True):
+            key = ops[m]["key"]
+            if known[e].get(key, -1) >= m:
+                continue
+            mine.append(m)
+            needed.add(m)
+            for k2, v2 in clock[m].items():
+                if known[e].get(k2, -1) < v2:
+                    known[e][k2] = v2
+        waits.append(mine)
+        if o["dma"] and not o["w"] and o.get("end"):
+            o["key"] = "out"
+        elif o["dma"]:
+            o["key"] = "d%d" % ndma
+            ndma += 1
+        else:
+            o["key"] = e
+        ck = dict(known[e])
+        ck[o["key"]] = n
+        clock.append(ck)
+    value, count_of, left = {}, {}, []
+    for n, o in enumerate(ops):
+        q = Q[o["e"]]
+        for m in waits[n]:
+            q.wait_ge(T.sem[ops[m]["key"]], value[m])
+        for name, v in o["pre"]:
+            q.wait_ge(T.sem[name], v)
+        ins = o["fn"]()
+        if o["dma"]:
+            ins.then_inc(T.sem[o["key"]], 16)
+            value[n] = 16
+            if n not in needed:
+                left.append(o["key"])
+        elif n in needed:
+            count_of[o["key"]] = count_of.get(o["key"], 0) + 1
+            value[n] = count_of[o["key"]]
+            ins.then_inc(T.sem[o["key"]], 1)
+    g.wait_ge(T.sem.sent, RO * nsig)
+    for key in sorted(set(left)):
+        g.wait_ge(T.sem[key], 16 * left.count(key))

@@ -4,40 +4,44 @@ from concourse.mybir import AluOpType as Alu, ActivationFunctionType as Act
 N, S, M, NA, RO = 4, 256, 1024, 2048, 3
 W0 = M + (N - 1) * S
 W = W0 + RO * S
+GH = (N - 1) * S
 MAGIC = 12582912.0
 OFS = 1280.0
 
 f32, b16, h16, i32, u16 = "float32", "bfloat16", "float16", "int32", "uint16"
 SB = {
-    "LK": (NA, i32), "L": (16 + NA, f32), "C": (W0 + 2 * S, i32), "Y": (W, b16), "YF": (W0 + 2 * S, b16),
-    "FA": (W, b16), "FB": (W, b16), "FW": (112, i32), "FL": (160, u16), "FO": (160, f32),
+    "LK": (NA, i32), "L": (32 + NA, f32), "C": (W0 + 2 * S, i32), "Y": (W + RO * GH, b16), "YF": (W0 + 2 * S, b16),
+    "FA": (W + S, b16), "FB": (W + S, b16), "VB": (S, f32), "BV": (128, b16), "LJ": (16, h16), "FW": (112, i32), "FL": (160, u16), "FO": (160, f32),
     "TH": (S, i32), "TF": (S, f32), "G": (4096, h16), "G1": (4096, f32), "YH": (4096, h16), "AB": (4096, b16),
     "A32": (S, i32), "AU": (S, u16), "A1": (S, f32), "BC": (2 * S, u16), "B32": (2 * S, f32),
     "OWN": (S, b16), "OT": (S, b16), "FV": (S, b16), "U": (S, f32),
     "S0": (384, f32), "S1": (384, f32), "ST0": (400, b16), "ST1": (400, b16),
-    "PR": (5 * S, h16), "LU": (64, u16), "AL": (16, f32), "AR": (S, f32), "EQ": (S, b16),
-    "OC": (16, u16), "OS": (32, u16), "VAL": (S, f32), "NR": (RO * S, f32),
+    "PR": (6 * S, h16), "LU": (80, u16), "AL": (16, f32), "AR": (2 * S, f32), "EQ": (2 * S, b16),
+    "OC": (16, u16), "ZB": (144, b16), "N2": (128, b16), "VAL": (S, f32), "NR": (RO * S, f32),
     "DF": (S, b16), "EF": (S, b16), "PQ": (4 * S, b16), "SG": (2 * S, b16), "RP": (S, f32),
-    "NEW": (RO * S, b16), "LAND": (RO * (N - 1) * S, b16),
+    "NEW": (RO * S, b16), "FY": (144, u16), "ZY0": (144, b16), "ZY1": (144, b16), "ZK": (288, b16),
     "PC": (S, f32), "CN": (S, i32), "MR": (S, b16), "MT": (S, b16), "X1": (S, b16), "PW": (S, b16), "VU": (16, u16),
     "AI": (128, f32), "AJ": (128, b16),
-    "ONE": (128, b16), "ID": (128, b16), "NI": (128, b16), "HI": (128, b16), "BO": (128, b16), "TMP": (128, b16),
+    "ONE": (128, b16), "ID": (128, b16), "IF": (128, f32), "NI": (128, b16), "HI": (128, b16), "BO": (128, b16), "TMP": (128, b16),
     "BIG": (128, b16), "TM2": (128, b16), "ZD": (2064, b16), "ZT": (2064, b16), "ZE": (144, b16), "ZF": (144, b16),
     "ZV": (144, b16), "ZX": (144, b16), "GO": (16, b16), "GX": (128, f32), "S16": (128, f32), "E0": (128, b16),
     "RM": (S, f32), "KC": (S, b16), "K0": (128, b16), "C128": (128, b16), "C16": (128, b16),
-    "BLI": (24, i32), "BL": (24, u16), "SF": (32, f32), "PI": (4, i32), "PF": (4, f32), "IDL": (160, f32), "LI": (16, b16),
+    "BLI": (40, i32), "BL": (40, u16), "SF": (32, f32), "PI": (4, i32), "PF": (5, f32), "IDL": (160, f32), "LI": (16, b16),
     "R": (1024, b16), "HF": (S, b16), "CT": (16, f32), "LO": (S, b16),
 }
 SCRATCH = {k: ("sbuf", [128, v[0]], v[1]) for k, v in SB.items()}
 for _k in range(8):
     SCRATCH["P%d" % _k] = ("psum", [128, 512], f32)
-GUESS = [dict(cyc=1.04, gath=1.62, scat=3.95, pe=0.55, dma=0.004, rem=4000.0, hop=100.0),
+GUESS = [dict(cyc=0.95, gath=1.48, scat=3.6, pe=0.5, dma=0.004, rem=5500.0, hop=100.0),
          dict(cyc=0.92, gath=1.05, scat=1.90, pe=0.65, dma=0.005, rem=5000.0, hop=150.0),
          dict(cyc=1.15, gath=2.25, scat=6.20, pe=0.50, dma=0.003, rem=3500.0, hop=70.0)]
 FIX, DMA_FIX, LEAN, HEAT, SEED = 55.0, 2000.0, 0.5, 0.005, 1
-TURNS, NOISE, SHIFTS = 60, 0.3, 24000
+TURNS, NOISE, SHIFTS = 40, 0.3, 12000
+PASSES, PARTS, STEPS, WARM = 2, 8, 3000, 120.0
 PLAN = {}
-GHOST_POOL = True
+HINT = False
+F2_DVE = False
+GA_DVE = {(0, 7)}
 NDMA = 20
 
 
@@ -213,7 +217,85 @@ def arrange(kind, size, queue, before, after):
             if w < best:
                 best, seq = w, cand
 
-    return seq
+
+    c0 = cost[0]
+    busy = [1000.0 if code[n] == 2 else c0[n] for n in range(n_ops)]
+    tail = [0.3 * DMA_FIX if code[n] == 1 else c0[n] - busy[n] for n in range(n_ops)]
+    ties = split[False]
+
+    def extend(order, line, first, end):
+        for n in order:
+            s = -hop
+            tied, loose = ties[n]
+            for m in tied:
+                if end[m] > s:
+                    s = end[m]
+            s += hop + lead0[n]
+            for m in loose:
+                s = max(s, end[m] - tail[m])
+            ln, b = line[res[n]], busy[n]
+            k = top = len(ln)
+            while k and ln[k - 1][1] > s:
+                k -= 1
+            while k < top and s + b > ln[k][0]:
+                if ln[k][1] > s:
+                    s = ln[k][1]
+                k += 1
+            ln.insert(k, (s, s + b))
+            first[n], end[n] = s - lead0[n], s + b + tail[n]
+
+    def whole(s):
+        first, end = pack(s, pred, c0, False)
+        return max(end) + 0.1 * sum(end) / n_ops, first
+    best, key = whole(seq)
+    for turn in range(PASSES * PARTS):
+        total = max(key)
+        t0 = total * (turn % PARTS) / PARTS - 1e4
+        t1, t2 = t0 + 1e4 + 1.5 * total / PARTS, t0 + 1e4 + 2.7 * total / PARTS
+        t0 = t0 + 1e4 - 0.5 * total / PARTS
+        order = rank_by(key, pred)
+        held = [n for n in order if key[n] < t0]
+        live = sorted(n for n in order if t0 <= key[n] < t2)
+        moving = [n for n in live if key[n] < t1]
+        mark = [n for n in live if key[n] >= t1]
+        inside = set(live)
+        near = {n: [m for m in pred[n] if m in inside] for n in live}
+        line0, first0, end0 = [[] for q in range(6)], [0.0] * n_ops, [0.0] * n_ops
+        extend(held, line0, first0, end0)
+        line0 = [ln[-12:] for ln in line0]
+        cur, now, keep, top = {n: key[n] for n in live}, 1e18, None, 1e18
+        for step in range(STEPS):
+            new = dict(cur)
+            for rep in range(0 if step == 0 else 1 + (seed >> 60) % 2):
+                seed = (seed * 6364136223846793005 + 1442695040888963407) % 2 ** 64
+                n = moving[(seed >> 33) % len(moving)]
+                far = ((seed >> 12) & 1023) / 1024.0 * (2500.0 if (seed >> 24) & 1 else 500.0)
+                new[n] += far if (seed >> 27) & 1 else -far
+                stack = [n]
+                while stack:
+                    x = stack.pop()
+                    for m in near[x]:
+                        if new[m] >= new[x]:
+                            new[m] = new[x] - 0.001
+                            stack.append(m)
+            for n in live:
+                for m in near[n]:
+                    if new[m] >= new[n]:
+                        new[n] = new[m] + 0.001
+            first, end = list(first0), list(end0)
+            extend(sorted(live, key=lambda n: new[n]), [list(ln) for ln in line0], first, end)
+            w = 0.1 * sum(end[n] for n in live) / len(live)
+            w += max(end) if t2 > total else sum(end[n] for n in mark) / len(mark)
+            if w <= now + WARM * (1.0 - step / STEPS) * ((seed >> 50) & 7) / 7.0:
+                now, cur = w, {n: first[n] for n in live}
+                if w < top:
+                    top, keep = w, cur
+        shift = max(keep.values()) - min([key[n] for n in order if key[n] >= t2], default=1e18)
+        cand = rank_by([keep[n] if n in inside else key[n] + (max(shift, 0.0) if key[n] >= t2 else 0.0) for n in range(n_ops)], pred)
+        w, first = whole(cand)
+        if w < best:
+            best, key = w, first
+    return rank_by(key, pred)
 
 
 SEMAPHORES = ["pe", "dve", "act", "pool", "sent", "out"] + ["arr%d" % t for t in range(RO)] + ["d%d" % k for k in range(NDMA)]
@@ -330,21 +412,17 @@ def rank_program(g, core, T, topo):
         mms([(o, win(z, r if per_r else 0, r), V(src, a + r, b, 16), first and r == 0, last and r == 15) for r in range(16)])
 
     others = [(rank + N - 1 - s) % N for s in range(N - 1)]
-    far = max(range(N - 1), key=lambda s: 0 if (topo.mates(topo.chip(core), topo.chip(T.cores[others[s]]))
-                                               or topo.same_plane(topo.chip(core), topo.chip(T.cores[others[s]]))) else 1)
-    eng = topo.engines(core, T.cores[others[far]])
-    near = [s for s in range(N - 1) if s != far]
-    share = {far: eng[1::2], near[0]: eng[0::2][:len(eng) // 4], near[1]: eng[0::2][len(eng) // 4:]}
-    nsig = len(eng)
+    mask = topo.mask(core, T.cores[others[0]])
+    for r in others:
+        mask &= topo.mask(core, T.cores[r])
+    nloc = bin(mask).count("1")
+    nsig = (N - 1) * nloc
 
     def send(t):
         src = V("NEW", t * S, (t + 1) * S)
-        trs = []
-        for s in range(N - 1):
-            rid, pid, _ = topo.addr(T.cores[others[s]])
-            c0 = (t * (N - 1) + s) * S
-            trs.append(RemoteDMATransfer(dst_ids=[DstId(rid=rid, pnc=pid)], dma_engine_mask=sum(1 << e for e in share[s]),
-                                         remote_sem=T.sem["arr%d" % t], src=src[0], dst=T.LAND[:, c0:c0 + S]))
+        ids = [DstId(rid=topo.addr(T.cores[r])[0], pnc=topo.addr(T.cores[r])[1]) for r in others]
+        dsts = [T.Y[:, W + t * GH + s * S:W + t * GH + (s + 1) * S] for s in range(N - 1)]
+        trs = [RemoteDMATransfer(dst_ids=ids, dma_engine_mask=mask, remote_sem=T.sem["arr%d" % t], srcs=[src[0]], dsts=dsts)]
         op("pool", lambda: g.remote_dma_fused(trs, local_sem=T.sem.sent), H(None), [src], cost=("rem", 1))
         ops[-1]["send"] = "arr%d" % t
 
@@ -370,7 +448,8 @@ def rank_program(g, core, T, topo):
     sel(V("ZD", 15, 2063, 16), V("ONE"), [[-1, 16], [-16, 8]], Alu.is_equal, 0, 1)
     sel(V("ID"), V("ONE"), [[-1, 128]], Alu.is_equal, 0, 1)
     for a, b, s, c in ((66, 112, 16, 1.0), (69, 112, 16, 1.0), (162, 163, 1, S - W0), (165, 166, 1, 2 * S), (178, 179, 1, W0),
-                       (179, 181, 1, 1.0), (194, 195, 1, -(W0 + S)), (210, 211, 1, W0 + S), (211, 212, 1, 1.0), (224, 225, 1, 1.0)):
+                       (179, 181, 1, 1.0), (194, 195, 1, -(W0 + S)), (210, 211, 1, W0 + S), (211, 212, 1, 1.0), (224, 225, 1, 1.0),
+                       (242, 244, 1, 1.0 / 16)):
         ms(V("HF", a, b, s), float(c))
     cp(V("AU"), V("C", 0, S))
     cp(V("FL", 0, 112), V("FW"))
@@ -382,24 +461,26 @@ def rank_program(g, core, T, topo):
     fill(V("ZE"), 0)
     fill(V("BIG"), -4096)
     fill(V("S16"), 16)
-    cp(V("PF"), V("PI"))
+    cp(V("PF", 0, 4), V("PI"))
+    act(V("PF", 4, 5), V("PF", 1, 2), bias=16.0)
     sel(V("TMP"), V("ONE"), [[-16, 8], [0, 16]], Alu.is_ge, 0, 1)
     sel(V("BO"), V("TMP"), [[16, 8], [0, 16]], Alu.is_ge, 15, -1)
     iota(V("R"), [[1, 64], [0, 16]])
     sel(V("GX"), V("S16"), [[-1, 8], [0, 16]], Alu.is_equal, 0, 1)
     iota(V("KC"), [[-15, 2], [0, 8], [-1, 16]], 15)
     iota(V("BLI", 0, 16), [[1, 16]])
-    iota(V("BLI", 16, 24), [[1, 8]])
+    iota(V("BLI", 16, 32), [[0, 2], [1, 8]])
+    iota(V("BLI", 32, 40), [[2, 4], [0, 2]])
     fill(V("K0"), 120)
     iota(V("IDL"), [[16, 160]])
     iota(V("NR"), [[1, RO * S]], W0)
     act(V("YF", 0, W0), X(V("Y", 0, W0), V("FL", 0, 112)), scale=0.5)
     act(V("NI"), V("ID"), scale=-1.0)
-    act(V("OWN"), V("Y", 0, S))
+    sel(V("IF"), V("ONE"), [[-1, 128]], Alu.is_equal, 0, 1)
     for B in range(10):
         act(V("FB", S * B, S * (B + 1)), V("LO"), scale=V("CT", 14, 15), bias=V("CT", B, B + 1))
     for q in range(3):
-        cp(V("L", 16 + 512 * q, 16 + 512 * (q + 1)), V("LK", 512 * q, 512 * (q + 1)))
+        cp(V("L", 32 + 512 * q, 32 + 512 * (q + 1)), V("LK", 512 * q, 512 * (q + 1)))
 
     def late_a():
         ts(V("R"), V("R"), V("PF", 2, 3), Alu.is_equal)
@@ -413,7 +494,7 @@ def rank_program(g, core, T, topo):
             mm(V("P7", 128 * h, 128 * (h + 1)), V("TF", 128 * h, 128 * (h + 1), p=(0, 8, 1)), V("GX", p=(0, 8, 1)))
         for h in range(2):
             act(V("S%d" % h, 256, 384), V("P7", 128 * h, 128 * (h + 1)), bias=15.0)
-        act(V("FA", 0, W0), X(V("FB"), V("FL", 0, 112)))
+        act(V("FA", 0, W0), X(V("FB", 0, W0), V("FL", 0, 112)))
         dma("sp", V("FA", W0, W), V("FB", W0, W))
         fill(V("RM"), 0)
         fill(V("RM", 0, S, 16), -16000000)
@@ -423,9 +504,11 @@ def rank_program(g, core, T, topo):
         fill(V("ST0", 15, 16), 1)
         fill(V("ST1", 15, 16), 1)
         move(V("ZE", 15, 143, 16), V("BO", 0, 128, 16))
-        cp(V("L", 16 + 1536, 16 + NA), V("LK", 1536, NA))
-        fill(V("L", 0, 16), 0)
-        dma("sp", H(T.lo[0:128:2, :]), V("L", 16, 16 + NA, p=(0, 128, 2)))
+        act(V("ZB"), V("ZE"), scale=-4096.0)
+        act(V("N2"), V("ID"), scale=-2.0)
+        cp(V("L", 32 + 1536, 32 + NA), V("LK", 1536, NA))
+        fill(V("L", 0, 32), 0)
+        dma("sp", H(T.lo[0:128:2, :]), V("L", 32, 32 + NA, p=(0, 128, 2)))
 
     def late_c():
         for q in range(4):
@@ -439,6 +522,15 @@ def rank_program(g, core, T, topo):
         fill(V("C16"), 16)
         fill(V("C", M, W0), 0)
         cp(V("FL", 112, 160), V("IDL", 112, 160))
+        cp(V("FY", 112, 144), V("IDL", 112, 144))
+        fill(V("Y", W0 + S, W), 0)
+        fill(V("FA", W, W + S), 0)
+        fill(V("FB", W, W + S), 0)
+        ts(V("LJ"), V("IDL", 0, 16), W - OFS, Alu.add)
+        act(V("BV"), V("BO"), scale=V("CT", 15, 16))
+        for u in range(2):
+            act(V("ZK", 144 * u, 144 * u + 143), V("ZD", 256, 399), scale=float(W - M + u * GH))
+            tt(V("ZY%d" % u, 0, 143), V("ZK", 144 * u, 144 * u + 143), V("ZF", 0, 143), Alu.add)
         act(V("LI"), V("IDL", 0, 16))
         act(V("HI"), V("ID"), scale=0.5)
         act(V("NR"), V("NR"), scale=V("PF", 3, 4))
@@ -458,7 +550,8 @@ def rank_program(g, core, T, topo):
         last = t == RO - 1
         a32 = V("C", 0, S) if t == 0 else V("A32")
         fv = V("FV")
-        lwin = V("LK") if t == 0 else V("L", 16, 16 + NA)
+        own = "Y" if t == 0 else "OWN"
+        lwin = V("LK") if t == 0 else V("L", 32, 32 + NA)
 
         def links(q):
             for j in ((2 * q, 2 * q + 1) if q == 1 else (None,)):
@@ -483,7 +576,10 @@ def rank_program(g, core, T, topo):
             return V("BC", S * o + 32 * j, S * o + 32 * (j + 1))
 
         def ga(j):
-            act(V("G1", 512 * j, 512 * (j + 1)), X(V("YF", 0, wt), bl(j, 0)), bias=1023.75)
+            if (t, j) in GA_DVE:
+                ts(V("G1", 512 * j, 512 * (j + 1)), X(V("YF", 0, wt), bl(j, 0)), 1023.75, Alu.add)
+            else:
+                act(V("G1", 512 * j, 512 * (j + 1)), X(V("YF", 0, wt), bl(j, 0)), bias=1023.75)
 
         def gb(j):
             tt(V("YH", 512 * j, 512 * (j + 1)), X(V("YF", 0, wt), bl(j, 1)), V("G1", 512 * j, 512 * (j + 1)), Alu.add)
@@ -514,7 +610,7 @@ def rank_program(g, core, T, topo):
             def hot(c):
                 return [(V(st, c, c + 128), V("ID")), (V(st, c - 1, c + 127), V("NI")), (V("E0"), V("ID"))]
             mms(grp(oh(h, 0), hot(144)) + grp(oh(h, 1), [(V(st, 272, 400), V("ID"))]))
-            mms(grp(oh(h, 3), hot(16) + [(V(st, 272, 400), V("NI"))]) + grp(oh(h, 2), hot(16)))
+            mms(grp(oh(h, 3), hot(16) + [(V(st, 272, 400), V("N2"))]) + grp(oh(h, 2), hot(16)))
 
         def oh(h, j):
             return V("P4" if h == 1 and j > 1 else "P%d" % h, 128 * j, 128 * (j + 1))
@@ -524,22 +620,66 @@ def rank_program(g, core, T, topo):
 
         def picks_q(h):
             for o in range(2):
-                tt(half("PR", h, S * (3 + o)), oh(h, 0), half("B32", o, S * h), Alu.mult)
+                tt(half("PR", 3 + o, 768 * h), oh(h, 0), half("B32", o, S * h), Alu.mult)
+            if t > 0:
+                tt(half("PR", 5, 768 * h), oh(h, 1), half("VB", h), Alu.mult)
+
+        def lists_of(h, bank, a, b, skip):
+            b -= 1 if t == 0 and b == 6 else 0
+            to_list(V(bank, 0, 8 * (b - a)), "ZE", "PR", 768 * h + 128 * a, 768 * h + 128 * b, last=b < 6)
+            if b == 6:
+                mm(V(bank, 8 * (5 - a), 8 * (6 - a)), V("ID"), V("LJ", 8 * h, 8 * h + 8), False, True)
+            return lambda: ts(V("LU", 40 * h + 8 * (a + skip - 1), 40 * h + 8 * (b - 1)), V(bank, 8 * skip, 8 * (b - a)), OFS, Alu.add)
 
         def picks_p(h):
-            tt(half("PR", h), oh(h, 3), half("A1", h), Alu.mult)
+            tt(half("PR", 0, 768 * h), oh(h, 3), half("A1", h), Alu.mult)
             for o in range(2):
-                tt(half("PR", h, S * (1 + o)), oh(h, 2), half("B32", o, S * h), Alu.mult)
+                tt(half("PR", 1 + o, 768 * h), oh(h, 2), half("B32", o, S * h), Alu.mult)
+
+        def state_q(h):
+            c0 = 512 * h + S
+            act(V("PQ", c0, c0 + S), X(V("YF", 0, wt), V("LU", 40 * h + 16, 40 * h + 32)))
+            group(V("P7", 0, 128), [(V("ID"), half("PQ", 0, c0)), (V("ID"), half("PQ", 1, c0)), (V("NI"), half(own, h))])
+            act(half("SG", 0, S * h), V("P7", 0, 128), Act.Sign, bias=-0.75)
+            act(half("SG", 1, S * h), V("P7", 0, 128), Act.Sign, bias=0.25)
+            group(V("P7", 128, S), [(V("ID"), half(own, h)), (V("HI"), half("SG", 0, S * h)), (V("HI"), half("SG", 1, S * h))])
+            act(half("NEW", h, t * S), V("P7", 128, S))
+
+        def state_p(h):
+            c0 = 512 * h
+            act(V("PQ", c0, c0 + S), X(V("YF", 0, wt), V("LU", 40 * h, 40 * h + 16)))
+            group(V("P7", S, S + 128), [(V("ID"), half("PQ", 0, c0)), (V("ID"), half("PQ", 1, c0))])
+            act(half("RP", h), V("P7", S, S + 128), bias=MAGIC, scale=1.0 - 2.0 ** -10)
+            act(half("Y", h, wt), half("RP", h), bias=-MAGIC)
+
+        def claims(h):
+            z = V("P5", 8 * h, 8 * (h + 1))
+            mm(z, V("IF"), V("AL", 8 * h, 8 * (h + 1)), True, False)
+            c0 = S * h
+            tt(V("EQ", c0, c0 + S), X(V("AL", 8 * h, 8 * (h + 1)), V("BL", 24, 40)), V("AR", c0, c0 + S), Alu.is_equal)
+            mms([(V("P5", 8 * h + 1, 8 * h + 8, 2), win("ZB", 0, r), V("EQ", c0 + 144 + r, c0 + S, 32), False, False)
+                 for r in range(16)]
+                + [(z, win("ZT", r, r), V("EQ", c0 + r, c0 + 128, 16), False, r == 15) for r in range(16)])
+            for u in range(2):
+                ts(V("OC", 8 * h + u, 8 * (h + 1), 2), V("P5", 8 * h + u, 8 * (h + 1), 2), 31.0, Alu.add,
+                   V("PF", 1 + 3 * u, 2 + 3 * u), Alu.max)
+            act(half("VAL", h), X(V("L"), V("OC", 8 * h, 8 * (h + 1))))
+
+        def forward(h):
+            if t > 0:
+                act(half("EF", h), X(V(F, 0, wt), V("LU", 40 * h + 16, 40 * h + 24)))
+                return
+            tt(half("DF", h), X(V(F, 0, wt), V("LU", 40 * h + 16, 40 * h + 24)), half("FV", h), Alu.subtract)
+            tt(half("EF", h), oh(h, 1), half("DF", h), Alu.mult)
 
         early = []
         links(0)
         if t > 0:
             act(V("OWN"), X(V("Y", 0, wt), V("VU")))
-            act(V("FV"), X(V(F, 0, wt), V("VU")))
         for h in range(2):
-            mm(V("P7", 128 * h, 128 * (h + 1)), V("OWN", 128 * h, 128 * (h + 1)), V("NI"))
+            mm(V("P7", 128 * h, 128 * (h + 1)), half(own, h), V("NI"))
         if not last:
-            mm(V("P7", S, 2 * S), V("BO"), V("OWN"))
+            mm(V("P7", S, 2 * S), V("BO"), V(own, 0, S))
         act(V("OT"), V("P7", 0, S))
         if not last:
             act(V("U"), V("P7", S, 2 * S), bias=float(t + 1))
@@ -591,59 +731,74 @@ def rank_program(g, core, T, topo):
         keys(1)
         picks_q(0)
         picks_p(0)
-        early = range(len(ops) - 5, len(ops))
+        early = range(len(ops) - (5 if t == 0 else 6), len(ops))
+        take = lists_of(0, "P5", 0, 6, 1)
+        mms([(half("P5", u), V("BO"), half("PR", 0), True, True) for u in (1, 2)])
+        take()
+        act(V("AL", 0, 8), V("P5", 0, 8))
+        act(V("AR", 0, S), V("P5", 128, 384))
+        state_q(0)
+        state_p(0)
+        forward(0)
+        claims(0)
 
         choose(1)
         picks_q(1)
-        to_list(V("P2", 0, 32), "ZE", "PR", 3 * S, 5 * S)
+        take = lists_of(1, "P2", 3, 6, 0)
         picks_p(1)
-        to_list(V("P3", 0, 48), "ZE", "PR", 0, 3 * S)
-        mm(V("P3", S, 2 * S), V("BO"), V("PR", 0, S))
-        to_list(V("P5", 0, 16), "ZE", "PR", 0, S, last=False)
-        ts(V("LU", 32, 64), V("P2", 0, 32), OFS, Alu.add)
-        act(V("PQ", 2 * S, 4 * S), X(V("YF", 0, wt), V("LU", 32, 64)))
-        group(V("P7", 0, S), [(V("ID"), V("PQ", 2 * S, 3 * S)), (V("ID"), V("PQ", 3 * S, 4 * S)), (V("NI"), V("OWN"))])
-        tt(V("DF"), X(V(F, 0, wt), V("LU", 32, 48)), fv, Alu.subtract)
-        ts(V("LU", 0, 32), V("P3", 16, 48), OFS, Alu.add)
-        for h in range(2):
-            tt(half("EF", h), oh(h, 1), half("DF", h), Alu.mult)
-        act(V("AL"), V("P3", 0, 16))
-        act(V("AR"), V("P3", S, 2 * S))
-        act(V("SG", 0, S), V("P7", 0, S), Act.Sign, bias=-0.75)
-        act(V("SG", S, 2 * S), V("P7", 0, S), Act.Sign, bias=0.25)
-        group(V("P7", S, 2 * S), [(V("ID"), V("OWN")), (V("HI"), V("SG", 0, S)), (V("HI"), V("SG", S, 2 * S))])
-        tt(V(F, 0, S) if t == 0 else X(V(F, 0, wt), V("VU")), V("EF"), fv, Alu.add)
-        new = V("NEW", t * S, (t + 1) * S)
-        act(new, V("P7", S, 2 * S))
+        take_p = lists_of(1, "P3", 0, 3, 1)
+        mms([(half("P3", u), V("BO"), half("PR", 0, 768), True, True) for u in (1, 2)])
+        take()
+        state_q(1)
+        n_new = len(ops) - 1
         send(t)
+        forward(1)
+        take_p()
+        act(V("AL", 8, 16), V("P3", 0, 8))
+        act(V("AR", S, 2 * S), V("P3", 128, 384))
+        n_ar = len(ops) - 1
+        claims(1)
+        n_val = len(ops) - 1
+        if t == 0:
+            tt(V(F, 0, S), V("EF"), fv, Alu.add)
+        else:
+            for h in range(2):
+                cp(X(V(F), V("LU", 40 * h + 32, 40 * h + 40)), half("EF", h))
+        if last and HINT:
+            ops[-1]["hint"] = [n_val - 4]
+        new = V("NEW", t * S, (t + 1) * S)
         nb = S if t == 0 else M
         to_list(V("P2", 0, nb // 16), "ZF", F, 0, nb)
         if t > 0:
             to_list(V("P2", 64, 64 + 16 * t), "ZF", F, W0, wt)
         act(V(F2, M, W0), X(V(F, 0, wt), V("FL", 64, 112)))
-        tt(V("EQ"), X(V("AL"), V("BL", 0, 16)), V("AR"), Alu.is_equal)
-        to_list(V("P5", 0, 16), "ZT", "EQ", 0, S, first=False, per_r=True)
         cp(V("FL", 0, nb // 16), V("P2", 0, nb // 16))
         if t > 0:
             cp(V("FL", 112, 112 + 16 * t), V("P2", 64, 64 + 16 * t))
         act(V(F2, 0, M), X(V(F, 0, wt), V("FL", 0, 64)))
-        if t > 0:
+        if last:
+            ops[-1]["hint"] = [n_val]
+        elif t > 0:
             act(V(F2, W0, wt), X(V(F, 0, wt), V("FL", 112, 112 + 16 * t)))
-        ts(V("OC"), V("P5", 0, 16), 15.0, Alu.add, V("PF", 1, 2), Alu.max)
-        ts(V("OS", 0, 32, 2), V("P5", 0, 16), 15.0, Alu.add, V("PF", 1, 2), Alu.max)
-        act(V("VAL"), X(V("L"), V("OC")))
+
+        def f2room():
+            (cp if F2_DVE else act)(V(F2, W0, wt), X(V(F, 0, wt), V("FL", 112, 112 + 16 * t)))
+            if F2_DVE:
+                ops[-1]["hint"] = [n_link]
 
         def ys():
             if t == 0:
                 move(V("Y", 0, S), new)
             else:
                 cp(X(V("Y", 0, wt), V("VU")), new)
+                if last and HINT:
+                    ops[-1]["hint"] = [n_link]
 
         def room():
-            act(V("PQ", 0, 2 * S), X(V("YF", 0, wt), V("LU", 0, 32)))
-            group(V("P7", 0, S), [(V("ID"), V("PQ", 0, S)), (V("ID"), V("PQ", S, 2 * S))])
-            act(V("RP"), V("P7", 0, S), bias=MAGIC, scale=1.0 - 2.0 ** -10)
-            act(V("Y", wt, wt + S), V("RP"), bias=-MAGIC)
+            n0 = len(ops)
+            state_p(1)
+            if last:
+                ops[n0]["hint"] = [n_ar]
 
         def f2list(bank, a, b):
             to_list(V(bank, a // 16, b // 16), "ZF", F2, a, b)
@@ -669,28 +824,30 @@ def rank_program(g, core, T, topo):
                 act(V("MR"), V("MT"), bias=V("CT", 13, 14))
 
         def l1():
+            to_list(V("P2", M // 16, wt // 16), "ZY%d" % t, F2, M, wt)
+            cp(V("FY", M // 16, wt // 16), V("P2", M // 16, wt // 16))
+
+        def l2():
+            to_list(V("P3", 0, 64), "ZY%d" % t, F2, 0, M)
+            cp(V("FY", 0, 64), V("P3", 0, 64))
+
+        def l3():
             f2list("P2", M, W0)
             cp(V("FL", 64, 112), V("P2", 64, 112))
 
-        def l2():
-            f2list("P3", 0, M)
-            if t > 0:
-                f2list("P3", W0, wt)
-            cp(V("FL", 0, 64), V("P3", 0, 64))
-            if t > 0:
-                cp(V("FL", 112, 112 + 16 * t), V("P3", 112, 112 + 16 * t))
-
         def yf():
-            c0 = t * (N - 1) * S
-            (move if GHOST_POOL else act)(V("Y", M, W0), V("LAND", c0, c0 + (N - 1) * S), pre=[("arr%d" % t, nsig)])
-            act(V("YF", 0, wt + S), X(V("Y", 0, wt + S), V("FL", 0, 112 + 16 * (t + 1))), scale=0.5)
+            act(V("YF", 0, wt + S), X(V("Y", 0, W + (t + 1) * GH), V("FY", 0, 112 + 16 * (t + 1))), scale=0.5,
+                pre=[("arr%d" % t, nsig)])
 
         def w1():
-            tt(V("PW"), X(V(F2, 0, wt), V("LU", 0, 16)), V("MR"), Alu.mult)
+            for h in range(2):
+                tt(half("PW", h), X(V(F2, 0, wt), V("LU", 40 * h, 40 * h + 8)), half("MR", h), Alu.mult)
             mm(V("P6", 0, 16), V("ID"), V("LI"), True, False)
             to_list(V("P6", 0, 16), "ZV", "PW", 0, S, first=False)
             if t == 0:
                 mm(V("P7", 0, S), win("ZX", 0, 2), V("PW"))
+            mm(V("P7", S, 2 * S), V("BV"), V("PW"))
+            act(V("VB"), V("P7", S, 2 * S), bias=-W / 16.0)
 
         def w2():
             cp(V("VU"), V("P6", 0, 16))
@@ -725,17 +882,19 @@ def rank_program(g, core, T, topo):
 
         if last:
             between = {}
-            after = [lambda: dma("sp", H(T.lo[1:128:2, :]), V("L", 16, 16 + NA, p=(1, 128, 2))), room, ys, out_y, out_f,
-                     lambda: dma("sp", H(T.yo[:, M:W0]), V("LAND", t * (N - 1) * S, (t + 1) * (N - 1) * S),
+            after = [lambda: dma("sp", H(T.lo[1:128:2, :]), V("L", 32, 32 + NA, p=(1, 128, 2))), f2room, room, ys, out_y, out_f,
+                     lambda: dma("sp", H(T.yo[:, M:W0]), V("Y", W + t * GH, W + (t + 1) * GH),
                                  pre=[("arr%d" % t, nsig)])]
         else:
-            between = {15: [ys, room], 14: [m1], 13: [l1], 12: [c1], 11: [l2], 10: [c2], 9: [w1, yf], 8: [c3], 7: [w2],
+            between = {15: [ys, room], 14: [m1], 13: [l1], 12: [c1], 11: [l2], 10: [c2], 9: [w1, yf, l3], 8: [c3], 7: [w2],
                        6: [w3], 5: [w4]}
             after = []
             pend = [count]
+        for c in range(7, -1, -1):
+            tt(X(V("L"), V("OC", 2 * c, 2 * c + 2)), V("VAL", 32 * c, 32 * (c + 1)),
+               V("NR", t * S + 32 * c, t * S + 32 * (c + 1)), Alu.max)
+        n_link = len(ops) - 1
         for c in range(15, -1, -1):
-            tt(X(V("L"), V("OS", 2 * c, 2 * c + 1)), V("VAL", 16 * c, 16 * (c + 1)),
-               V("NR", t * S + 16 * c, t * S + 16 * (c + 1)), Alu.max)
             for fn in between.get(c, ()):
                 fn()
         if t == 0:
@@ -826,6 +985,6 @@ def rank_program(g, core, T, topo):
             count_of[o["key"]] = count_of.get(o["key"], 0) + 1
             value[n] = count_of[o["key"]]
             ins.then_inc(T.sem[o["key"]], 1)
-    g.wait_ge(T.sem.sent, RO * nsig)
+    g.wait_ge(T.sem.sent, RO * nloc)
     for key in sorted(set(left)):
         g.wait_ge(T.sem[key], 16 * left.count(key))

@@ -7,295 +7,271 @@ W = W0 + RO * S
 GH = (N - 1) * S
 MAGIC = 12582912.0
 OFS = 1280.0
+KEY = 4096.0
 
 f32, b16, h16, i32, u16 = "float32", "bfloat16", "float16", "int32", "uint16"
 SB = {
     "LK": (NA, i32), "L": (32 + NA, f32), "C": (W0 + 2 * S, i32), "Y": (W + RO * GH, b16), "YF": (W0 + 2 * S, b16),
-    "FA": (W + S, b16), "FB": (W + S, b16), "VB": (S, f32), "BV": (128, b16), "LJ": (16, h16), "FW": (112, i32), "FL": (160, u16), "FO": (160, f32),
-    "TH": (S, i32), "TF": (S, f32), "G": (4096, h16), "G1": (4096, f32), "YH": (4096, h16), "AB": (4096, b16),
-    "A32": (S, i32), "AU": (S, u16), "A1": (S, f32), "BC": (2 * S, u16), "B32": (2 * S, f32),
-    "OWN": (S, b16), "OT": (S, b16), "FV": (S, b16), "U": (S, f32),
-    "S0": (384, f32), "S1": (384, f32), "ST0": (400, b16), "ST1": (400, b16),
-    "PR": (6 * S, h16), "LU": (80, u16), "AL": (16, f32), "AR": (2 * S, f32), "EQ": (2 * S, b16),
-    "OC": (16, u16), "ZB": (144, b16), "N2": (128, b16), "VAL": (S, f32), "NR": (RO * S, f32),
-    "DF": (S, b16), "EF": (S, b16), "PQ": (4 * S, b16), "SG": (2 * S, b16), "RP": (S, f32),
-    "NEW": (RO * S, b16), "FY": (144, u16), "ZY0": (144, b16), "ZY1": (144, b16), "ZK": (288, b16),
-    "PC": (S, f32), "CN": (S, i32), "MR": (S, b16), "MT": (S, b16), "X1": (S, b16), "PW": (S, b16), "VU": (16, u16),
-    "AI": (128, f32), "AJ": (128, b16),
-    "ONE": (128, b16), "ID": (128, b16), "IF": (128, f32), "NI": (128, b16), "HI": (128, b16), "BO": (128, b16), "TMP": (128, b16),
-    "BIG": (128, b16), "TM2": (128, b16), "ZD": (2064, b16), "ZT": (2064, b16), "ZE": (144, b16), "ZF": (144, b16),
-    "ZV": (144, b16), "ZX": (144, b16), "GO": (16, b16), "GX": (128, f32), "S16": (128, f32), "E0": (128, b16),
-    "RM": (S, f32), "KC": (S, b16), "K0": (128, b16), "C128": (128, b16), "C16": (128, b16),
-    "BLI": (40, i32), "BL": (40, u16), "SF": (32, f32), "PI": (4, i32), "PF": (5, f32), "IDL": (160, f32), "LI": (16, b16),
-    "R": (1024, b16), "HF": (S, b16), "CT": (16, f32), "LO": (S, b16),
+    "FS": (W + 2 * GH, b16), "FP": (W + GH, b16), "FW": (112, i32), "FL": (144, u16), "FY": (144, u16), "FO": (160, f32),
+    "TH": (S, i32), "TF": (S, h16), "G": (4096, h16), "GA": (4096, b16), "GB": (4096, b16), "AB": (4096, b16),
+    "A32": (S, i32), "AU": (S, u16), "BC": (2 * S, u16), "B32": (S, f32), "OWN": (S, b16), "OT": (384, b16), "U": (S, f32),
+    "SC": (2 * S, f32), "MI": (32, i32), "JI": (32, i32), "JU": (32, u16), "NR": (16, b16), "NV": (16, b16), "VS": (16, b16),
+    "NB": (16, b16), "NH": (16, h16), "AD": (16, b16), "PR": (3 * S, h16), "LQ": (32, u16), "LP": (32, u16), "PQ": (4 * S, b16), "SG": (S, b16),
+    "NEW": (RO * S, b16), "EF": (S, b16), "AT": (S, h16), "EQ": (384, b16), "EA": (384, b16), "OC": (32, u16), "VAL": (S, f32),
+    "NW": (RO * S, f32), "PC": (S, f32), "CN": (S, i32), "MR": (S, b16), "W1": (S, b16), "WU": (16, u16), "PW": (S, b16),
+    "VU": (16, u16), "LIM": (16, f32), "LI0": (16, f32), "AI": (4, f32),
+    "ONE": (128, b16), "ID": (128, b16), "NI": (128, b16), "IE": (128, h16), "N4": (128, b16), "BO": (128, b16),
+    "MG": (S, b16), "KA": (16, h16), "E2": (128, b16), "GX": (144, b16), "KR": (512, b16), "PG": (1, b16), "OB": (4, f32),
+    "ZP": (2064, b16), "Z5": (128, b16), "CK": (S, f32), "ZD": (2064, b16), "ZE": (144, b16), "ZK": (144, b16), "ZB": (144, b16), "ZF": (144, b16), "ZV": (144, b16),
+    "ZG": (288, b16), "ZY0": (144, b16), "ZY1": (144, b16), "R": (1536, b16), "EYE": (4096, b16), "KI": (S, b16), "TRI": (S, b16),
+    "RP": (S, b16), "RQ": (S, b16), "XJ": (16, f32), "IDL": (160, f32), "LI": (16, b16), "LJ": (48, h16), "PF": (4, b16),
+    "HF": (56, b16), "HG": (64, b16), "CT": (18, f32), "LO": (S, b16), "VA": (48, b16), "JK": (16, f32), "LL": (64, u16),
 }
 SCRATCH = {k: ("sbuf", [128, v[0]], v[1]) for k, v in SB.items()}
+SCRATCH["AB"] = ("sbuf", [128, 16, S], b16)
 for _k in range(8):
     SCRATCH["P%d" % _k] = ("psum", [128, 512], f32)
-GUESS = [dict(cyc=0.95, gath=1.48, scat=3.6, pe=0.5, dma=0.004, rem=5500.0, hop=100.0),
-         dict(cyc=0.92, gath=1.05, scat=1.90, pe=0.65, dma=0.005, rem=5000.0, hop=150.0),
-         dict(cyc=1.15, gath=2.25, scat=6.20, pe=0.50, dma=0.003, rem=3500.0, hop=70.0)]
-FIX, DMA_FIX, LEAN, HEAT, SEED = 55.0, 2000.0, 0.5, 0.005, 1
-TURNS, NOISE, SHIFTS = 40, 0.3, 12000
-PASSES, PARTS, STEPS, WARM = 2, 8, 3000, 120.0
+
+PARTS = [[(0, 16)]] * RO
+LINKS = [(192, 256), (128, 192), (64, 128), (0, 64)]
+PICKS = [(192, 256), (128, 192), (64, 128), (0, 64)]
+STATES = [(192, 256), (128, 192), (64, 128), (32, 64), (0, 32)]
+SUMS = [(14, 16), (12, 14), (10, 12), (8, 10), (6, 8), (4, 6), (2, 4), (0, 2)]
+KEYS, SCANS = [(12, 16), (8, 12), (4, 8), (0, 4)], 4
+TWICE = True
+MERGE, QFIRST, DIRECT = True, (0, 0, 0), True
+PAIRS = 1
+PACKED = True
+INORDER = False
+APART = False
+EQ_ACT = (False, True, False)
+LOADS, LEAD = ("FW", "C", "TH", "LK", "Y"), 20000.0
+BOTH = ("sp", "act")
+GUESS = [dict(cyc=0.95, gath=1.45, scat=3.5, pe=0.48, dma=0.004, rem=4500.0, hop=80.0),
+         dict(cyc=1.0, gath=1.1, scat=4.5, pe=0.58, dma=0.004, rem=3000.0, hop=100.0),
+         dict(cyc=1.15, gath=2.2, scat=4.5, pe=0.56, dma=0.004, rem=3500.0, hop=70.0)]
+FIX = {"dve": 50.0, "act": 65.0, "pe": 30.0, "pool": 0.0, "sp": 0.0}
+DMA_FIX, ISSUE, COOL, REFIT = 2000.0, 1000.0, 1.0, 8
+LEAN, HEAT, SEEDS, PASSES, WINDOW, MOVES = 0.6, 0.012, (1, 2, 3, 4, 5, 6), 4, 80, 2500
 PLAN = {}
-HINT = False
-F2_DVE = False
-GA_DVE = {(0, 7)}
-NDMA = 20
+NDMA = 30
+QUEUES = ("act", "dve", "pe", "pool", "sp")
 
 
-def arrange(kind, size, queue, before, after):
-    n_ops = len(kind)
-    cost = [[size[n] * G[kind[n]] + (0.0 if kind[n] in ("pe", "dma", "rem") else FIX) for n in range(n_ops)] for G in GUESS]
-    code = [1 if k == "dma" else 2 if k == "rem" else 0 for k in kind]
-    pred = [sorted(set(before[n]) | set(after[n])) for n in range(n_ops)]
+def arrange(ways, before, near, after, lead):
+    n_ops, models = len(ways), range(len(GUESS))
+    cost = [[{QUEUES.index(q): size * G[kind] + FIX[q] * (kind not in ("dma", "rem")) for q, kind, size in ways[n]}
+             for n in range(n_ops)] for G in GUESS]
+    queue = [[QUEUES.index(q) for q, kind, size in ways[n]] for n in range(n_ops)]
+    code = [{"dma": 1, "rem": 2}.get(ways[n][0][1], 0) for n in range(n_ops)]
+    loose = [sorted(set(near[n]) | set(after[n])) for n in range(n_ops)]
+    pred = [sorted(set(before[n]) | set(loose[n])) for n in range(n_ops)]
     succ = [[] for n in range(n_ops)]
     for n in range(n_ops):
         for m in pred[n]:
             succ[m].append(n)
 
-    def span(seq, j):
+    def run(j, part, on, done, fin, free):
         c, hop = cost[j], GUESS[j]["hop"]
-        free, done, dfree = [0.0] * 5, [0.0] * n_ops, 0.0
-        for n in seq:
-            q = queue[n]
+        for n in part:
+            q = on[n]
             s = free[q]
             for m in before[n]:
                 if done[m] > s:
                     s = done[m]
+            for m in near[n]:
+                if done[m] > s and on[m] != q:
+                    s = done[m]
             if code[n] == 0:
-                s += c[n]
-                free[q] = s
+                s += c[n][q]
                 done[n] = s + hop
             elif code[n] == 1:
-                free[q] = s + 60.0
-                dfree = max(dfree, s + 0.7 * DMA_FIX) + c[n]
+                free[5] = max(free[5], s + 0.7 * DMA_FIX) + c[n][q]
+                done[n] = free[5] + 0.3 * DMA_FIX + hop
+                s += 60.0
+            else:
+                free[5] = max(free[5], s + 0.7 * DMA_FIX) + c[n][q]
+                done[n] = free[5] + 0.3 * DMA_FIX + hop
+                s += ISSUE
+            free[q] = fin[n] = s
+
+    def tails(j, part, on):
+        c, hop = cost[j], GUESS[j]["hop"]
+        tail, free = {}, [0.0] * 6
+        for n in reversed(part):
+            q = on[n]
+            behind = hop + max([tail[m] for m in succ[n] if n in before[m] or (n in near[m] and on[m] != q)], default=0.0)
+            if code[n] == 0:
+                free[q] = c[n][q] + max(behind, free[q])
+            else:
+                free[5] = c[n][q] + max(0.3 * DMA_FIX + behind, free[5])
+                free[q] = max((60.0 if code[n] == 1 else ISSUE) + free[q], 0.7 * DMA_FIX + free[5])
+            tail[n] = free[q]
+        return tail, free
+
+    def whole(seq, on):
+        times = [([0.0] * n_ops, [0.0] * n_ops) for j in models]
+        for j in models:
+            run(j, seq, on, times[j][0], times[j][1], [0.0] * 6)
+        return times
+
+    def pack(order, on):
+        c, hop = cost[0], GUESS[0]["hop"]
+        line, first, done, dfree = [[] for q in range(5)], [0.0] * n_ops, [0.0] * n_ops, 0.0
+        for n in order:
+            s0 = max([done[m] for m in before[n]], default=0.0)
+            best = None
+            for q in queue[n]:
+                s = max([s0] + [first[m] + 60.0 if code[m] else done[m] - hop * (on[m] == q) for m in loose[n]])
+                b = c[n][q] if code[n] == 0 else 60.0 if code[n] == 1 else ISSUE
+                ln = line[q]
+                k = top = len(ln)
+                while k and ln[k - 1][1] > s:
+                    k -= 1
+                while k < top and s + b > ln[k][0]:
+                    s = max(s, ln[k][1])
+                    k += 1
+                if best is None or s + b < best[0]:
+                    best = (s + b, s, q, k)
+            e, s, q, k = best
+            on[n] = q
+            line[q].insert(k, (s, e))
+            first[n] = s
+            if code[n] == 0:
+                done[n] = e + hop
+            elif code[n] == 1:
+                dfree = max(dfree, s + 0.7 * DMA_FIX) + c[n][q]
                 done[n] = dfree + 0.3 * DMA_FIX + hop
             else:
-                free[q] = s + 1000.0
-                done[n] = s + c[n] + hop
-        return done
+                done[n] = s + c[n][q] + hop
+        return first
 
-    hop = GUESS[0]["hop"]
-    full = [cost[0][n] + (DMA_FIX if code[n] == 1 else 0.0) for n in range(n_ops)]
-    rest = [0.0] * n_ops
-    for n in range(n_ops - 1, -1, -1):
-        rest[n] = full[n] + max([rest[m] + hop for m in succ[n]], default=0.0)
-    missing = [len(p) for p in pred]
-    ready = {n: 0.0 for n in range(n_ops) if missing[n] == 0}
-    free, done, seq = [0.0] * 5, {}, []
-    while ready:
-        begin = {n: max(r, free[queue[n]]) for n, r in ready.items()}
-        n0 = min(begin, key=lambda n: (begin[n], n))
-        n = max((m for m in begin if queue[m] == queue[n0] and begin[m] <= begin[n0] + 1.5 * hop), key=lambda m: (rest[m], -m))
-        done[n] = begin[n] + full[n]
-        free[queue[n]] = done[n] if code[n] == 0 else begin[n] + 60.0
-        del ready[n]
-        seq.append(n)
-        for m in succ[n]:
-            missing[m] -= 1
-            if missing[m] == 0:
-                ready[m] = max([done[k] + hop for k in before[m]], default=0.0)
-    unit = [max(span(seq, j)) for j in range(len(GUESS))]
-
-    res = [5 if code[n] == 1 else queue[n] for n in range(n_ops)]
-    waited = [set(b) for b in before]
-
-    lead0 = [0.7 * DMA_FIX if code[n] == 1 else 0.0 for n in range(n_ops)]
-    split = {back: [([m for m in near[n] if ((n in waited[m]) if back else (m in waited[n]))],
-                     [m for m in near[n] if not ((n in waited[m]) if back else (m in waited[n]))]) for n in range(n_ops)]
-             for back, near in ((False, pred), (True, succ))}
-
-    def pack(order, near, c, back):
-        lead = lead0
-        busy = [1000.0 if code[n] == 2 else c[n] for n in range(n_ops)]
-        tail = [0.3 * DMA_FIX if code[n] == 1 else c[n] - busy[n] for n in range(n_ops)]
-        if back:
-            lead, tail = tail, lead
-        line, end, first = [[] for q in range(6)], [0.0] * n_ops, [0.0] * n_ops
-        ties = split[back]
-        for n in order:
-            s = -hop
-            tied, loose = ties[n]
-            for m in tied:
-                if end[m] > s:
-                    s = end[m]
-            s += hop + lead[n]
-            for m in loose:
-                s = max(s, end[m] - tail[m])
-            ln = line[res[n]]
-            k = top = len(ln)
-            while k and ln[k - 1][1] > s:
-                k -= 1
-            while k < top and s + busy[n] > ln[k][0]:
-                if ln[k][1] > s:
-                    s = ln[k][1]
-                k += 1
-            ln.insert(k, (s, s + busy[n]))
-            first[n], end[n] = s - lead[n], s + busy[n] + tail[n]
-        return first, end
-
-    def rank_by(key, near):
+    def rank_by(key):
         key = list(key)
-        for n in (range(n_ops) if near is pred else range(n_ops - 1, -1, -1)):
-            for m in near[n]:
+        for n in range(n_ops):
+            for m in pred[n]:
                 if key[m] >= key[n]:
                     key[n] = key[m] + 0.001
         return sorted(range(n_ops), key=lambda n: key[n])
 
-    def plain(s):
-        return sum(max(span(s, j)) / unit[j] for j in range(len(GUESS)))
-    best, seed, cur = plain(seq), SEED, list(seq)
-    for turn in range(TURNS):
-        c = []
-        for n in range(n_ops):
-            seed = (seed * 6364136223846793005 + 1442695040888963407) % 2 ** 64
-            c.append(cost[0][n] * (1.0 + NOISE * (((seed >> 33) & 1023) / 512.0 - 1.0)))
-        first, end = pack(cur, pred, c, False)
-        first, end = pack(rank_by([-x for x in end], succ), succ, c, True)
-        first, end = pack(rank_by([-x for x in end], pred), pred, cost[0], False)
-        cand = rank_by(first, pred)
-        w = plain(cand)
-        if w < best + 0.01:
-            cur = cand
-            if w < best:
-                best, seq = w, cand
-        elif turn % 8 == 7:
-            cur = list(seq)
+    def moved(seq, a, b, ahead):
+        part, take = seq[a:b + 1], {seq[b] if ahead else seq[a]}
+        for n in (part[::-1] if ahead else part):
+            if n in take:
+                take.update(pred[n] if ahead else succ[n])
+        if (seq[a] if ahead else seq[b]) in take:
+            return None
+        one, two = [n for n in part if n in take], [n for n in part if n not in take]
+        return seq[:a] + (one + two if ahead else two + one) + seq[b + 1:]
 
-    def tight(s, j):
-        d, pairs, prev, lastq = span(s, j), [], {}, {}
-        for n in s:
-            prev[n] = lastq.get(queue[n])
-            lastq[queue[n]] = n
-        n = max(range(n_ops), key=lambda m: d[m])
-        while n is not None:
-            m = max(before[n], key=lambda k: d[k], default=None)
-            p = prev[n]
-            if p is not None and code[p] == 0 and (m is None or d[p] - GUESS[j]["hop"] >= d[m]):
-                if p not in pred[n]:
-                    pairs.append((n, p))
-                n = p
-            else:
-                n = m if m is not None else p
-        return pairs
-    key = pack(seq, pred, cost[0], False)[0]
-    now = best = 100.0
-    cur = seq
-    pairs = tight(cur, 0)
-    for turn in range(SHIFTS):
-        new = list(key)
-        seed = (seed * 6364136223846793005 + 1442695040888963407) % 2 ** 64
-        if turn % 16 == 0:
-            pairs = tight(cur, (seed >> 40) % len(GUESS))
-        for rep in range(1 + (seed >> 60) % 3):
-            seed = (seed * 6364136223846793005 + 1442695040888963407) % 2 ** 64
-            n = (seed >> 33) % n_ops
-            far = ((seed >> 12) & 1023) / 1024.0 * (3000.0 if (seed >> 24) & 1 else 500.0)
-            if (seed >> 26) & 1 and pairs:
-                n, p = pairs[(seed >> 33) % len(pairs)]
-                if (seed >> 27) & 1:
-                    new[n] = key[p] - 1.0 - far * ((seed >> 28) & 1)
-                else:
-                    new[p] = key[n] + 1.0 + far * ((seed >> 28) & 1)
-            else:
-                new[n] += far if (seed >> 27) & 1 else -far
-            if new[n] < key[n]:
-                stack = [n]
-                while stack:
-                    x = stack.pop()
-                    for m in pred[x]:
-                        if new[m] >= new[x]:
-                            new[m] = new[x] - 0.001
-                            stack.append(m)
-        first, end = pack(rank_by(new, pred), pred, cost[0], False)
-        w = 3.0 * (max(end) + LEAN * sum(end) / n_ops) / unit[0]
-        if w <= now + HEAT * (1.0 - turn / SHIFTS) * ((seed >> 50) & 7) / 7.0:
-            cand = rank_by(first, pred)
-            now, key, cur = w, first, cand
-            if w < best:
-                best, seq = w, cand
+    rest = [0.0] * n_ops
+    for n in range(n_ops - 1, -1, -1):
+        rest[n] = (min(cost[0][n].values()) + DMA_FIX * (code[n] == 1) + lead[n]
+                   + max([rest[m] + GUESS[0]["hop"] for m in succ[n]], default=0.0))
+    on0 = [0] * n_ops
+    seq0 = rank_by(pack(rank_by([-x for x in rest]), on0))
+    unit = [max(x[0]) for x in whole(seq0, on0)]
 
+    def stretch(seq, on, p0, heat, seed):
+        times = whole(seq, on)
+        seq = rank_by([times[0][1][n] - (cost[0][n][on[n]] if code[n] == 0 else 60.0 if code[n] == 1 else ISSUE)
+                       for n in range(n_ops)])
+        p0, p1 = max(p0, 0), min(p0 + WINDOW, n_ops)
+        part, free0, ext, base, queue_tail = seq[p0:p1], [], [], [], []
+        for j in models:
+            free0.append([0.0] * 6)
+            run(j, seq[:p0], on, times[j][0], times[j][1], free0[j])
+            tail, free = tails(j, seq[p1:], on)
+            ext.append({n: max([tail[m] for m in succ[n] if m in tail], default=0.0) for n in seq[:p1]})
+            base.append(max([times[j][0][n] + ext[j][n] for n in seq[:p0]], default=0.0))
+            queue_tail.append(free)
 
-    c0 = cost[0]
-    busy = [1000.0 if code[n] == 2 else c0[n] for n in range(n_ops)]
-    tail = [0.3 * DMA_FIX if code[n] == 1 else c0[n] - busy[n] for n in range(n_ops)]
-    ties = split[False]
+        def worth(part, on, a, old):
+            last = {on[n]: n for n in part[:a]}
+            dmas = [n for n in part[:a] if code[n]]
+            w, new, behind = 0.0, [], part[a:]
+            for j in models:
+                done, fin, free, e = list(old[j][0]), list(old[j][1]), list(free0[j]), ext[j]
+                for q, n in last.items():
+                    free[q] = fin[n]
+                if dmas:
+                    free[5] = done[dmas[-1]] - 0.3 * DMA_FIX - GUESS[j]["hop"]
+                run(j, behind, on, done, fin, free)
+                ends = [done[n] + e[n] for n in part]
+                end = max(max(ends), base[j], max(x + y for x, y in zip(free, queue_tail[j])))
+                w += (end + LEAN * (sum(ends) / len(ends) + sum(free[:3]) / 3)) / unit[j]
+                new.append((done, fin))
+            return w, new
 
-    def extend(order, line, first, end):
-        for n in order:
-            s = -hop
-            tied, loose = ties[n]
-            for m in tied:
-                if end[m] > s:
-                    s = end[m]
-            s += hop + lead0[n]
-            for m in loose:
-                s = max(s, end[m] - tail[m])
-            ln, b = line[res[n]], busy[n]
-            k = top = len(ln)
-            while k and ln[k - 1][1] > s:
-                k -= 1
-            while k < top and s + b > ln[k][0]:
-                if ln[k][1] > s:
+        def refit(part, on, a, old):
+            c, hop, done, first = cost[0], GUESS[0]["hop"], list(old[0]), {}
+            free = list(free0[0])
+            for n in part[:a]:
+                free[on[n]] = old[1][n]
+            line = [[(0.0, f)] for f in free]
+            for n in part[a:]:
+                q = on[n]
+                s = 0.0
+                for m in before[n]:
+                    if done[m] > s:
+                        s = done[m]
+                for m in loose[n]:
+                    d = done[m] if on[m] != q else first.get(m, 0.0) + 1.0
+                    if d > s:
+                        s = d
+                b = c[n][q] if code[n] == 0 else 60.0 if code[n] == 1 else ISSUE
+                ln = line[q]
+                k = top = len(ln)
+                while ln[k - 1][1] > s and k > 1:
+                    k -= 1
+                s = max(s, ln[k - 1][1])
+                while k < top and s + b > ln[k][0]:
                     s = ln[k][1]
-                k += 1
-            ln.insert(k, (s, s + b))
-            first[n], end[n] = s - lead0[n], s + b + tail[n]
+                    k += 1
+                ln.insert(k, (s, s + b))
+                first[n] = s
+                done[n] = s + b + hop if code[n] == 0 else s + DMA_FIX + c[n][q] + hop
+            return part[:a] + sorted(part[a:], key=lambda n: first[n])
+        now, cur = worth(part, on, 0, times)
+        best, keep = now, (part, on)
+        for step in range(MOVES):
+            seed = (seed * 6364136223846793005 + 1442695040888963407) % 2 ** 64
+            a = b = 1 + (seed >> 33) % (len(part) - 1)
+            n = part[b]
+            kind, cand, other = (seed >> 20) % 4, part, on
+            if kind >= 2 and len(queue[n]) > 1:
+                other = list(on)
+                other[n] = sum(queue[n]) - on[n]
+                swap = [k for k in range(max(0, b - 20), min(b + 20, len(part)))
+                        if on[part[k]] == other[n] and on[n] in queue[part[k]]]
+                if kind == 3 and swap:
+                    k = swap[(seed >> 45) % len(swap)]
+                    other[part[k]] = on[n]
+                    a = min(a, k)
+            if other is on or (seed >> 26) & 1:
+                mine = [k for k in range(max(0, b - 40), b) if other[part[k]] == other[n]][-1 - (seed >> 28) % 4:]
+                if mine:
+                    cand = moved(part, mine[0], b, (seed >> 27) & 1)
+                    a = min(a, mine[0])
+                if cand is None or (cand is part and other is on):
+                    continue
+            if (seed >> 12) % 16 < REFIT:
+                cand = refit(cand, other, a, cur[0])
+            w, new = worth(cand, other, a, cur)
+            if w <= now + heat * (1.0 - step / MOVES) * ((seed >> 50) & 15) / 15.0:
+                now, part, on, cur = w, cand, other, new
+                if w < best:
+                    best, keep = w, (part, on)
+        return seq[:p0] + keep[0] + seq[p1:], keep[1]
 
-    def whole(s):
-        first, end = pack(s, pred, c0, False)
-        return max(end) + 0.1 * sum(end) / n_ops, first
-    best, key = whole(seq)
-    for turn in range(PASSES * PARTS):
-        total = max(key)
-        t0 = total * (turn % PARTS) / PARTS - 1e4
-        t1, t2 = t0 + 1e4 + 1.5 * total / PARTS, t0 + 1e4 + 2.7 * total / PARTS
-        t0 = t0 + 1e4 - 0.5 * total / PARTS
-        order = rank_by(key, pred)
-        held = [n for n in order if key[n] < t0]
-        live = sorted(n for n in order if t0 <= key[n] < t2)
-        moving = [n for n in live if key[n] < t1]
-        mark = [n for n in live if key[n] >= t1]
-        inside = set(live)
-        near = {n: [m for m in pred[n] if m in inside] for n in live}
-        line0, first0, end0 = [[] for q in range(6)], [0.0] * n_ops, [0.0] * n_ops
-        extend(held, line0, first0, end0)
-        line0 = [ln[-12:] for ln in line0]
-        cur, now, keep, top = {n: key[n] for n in live}, 1e18, None, 1e18
-        for step in range(STEPS):
-            new = dict(cur)
-            for rep in range(0 if step == 0 else 1 + (seed >> 60) % 2):
-                seed = (seed * 6364136223846793005 + 1442695040888963407) % 2 ** 64
-                n = moving[(seed >> 33) % len(moving)]
-                far = ((seed >> 12) & 1023) / 1024.0 * (2500.0 if (seed >> 24) & 1 else 500.0)
-                new[n] += far if (seed >> 27) & 1 else -far
-                stack = [n]
-                while stack:
-                    x = stack.pop()
-                    for m in near[x]:
-                        if new[m] >= new[x]:
-                            new[m] = new[x] - 0.001
-                            stack.append(m)
-            for n in live:
-                for m in near[n]:
-                    if new[m] >= new[n]:
-                        new[n] = new[m] + 0.001
-            first, end = list(first0), list(end0)
-            extend(sorted(live, key=lambda n: new[n]), [list(ln) for ln in line0], first, end)
-            w = 0.1 * sum(end[n] for n in live) / len(live)
-            w += max(end) if t2 > total else sum(end[n] for n in mark) / len(mark)
-            if w <= now + WARM * (1.0 - step / STEPS) * ((seed >> 50) & 7) / 7.0:
-                now, cur = w, {n: first[n] for n in live}
-                if w < top:
-                    top, keep = w, cur
-        shift = max(keep.values()) - min([key[n] for n in order if key[n] >= t2], default=1e18)
-        cand = rank_by([keep[n] if n in inside else key[n] + (max(shift, 0.0) if key[n] >= t2 else 0.0) for n in range(n_ops)], pred)
-        w, first = whole(cand)
-        if w < best:
-            best, key = w, first
-    return rank_by(key, pred)
+    found = []
+    for seed in SEEDS:
+        seq, on = seq0, on0
+        for turn in range(PASSES):
+            for p0 in range(-((turn * 17) % (WINDOW // 2)), n_ops - WINDOW // 2, WINDOW // 2):
+                seq, on = stretch(seq, on, p0, HEAT * (1.0 - COOL * turn / PASSES), 1000003 * seed + 1009 * turn + p0 + WINDOW)
+        found.append((sum(max(x[0]) / u for x, u in zip(whole(seq, on), unit)), seq, on))
+    return min(found)[1:]
 
 
 SEMAPHORES = ["pe", "dve", "act", "pool", "sent", "out"] + ["arr%d" % t for t in range(RO)] + ["d%d" % k for k in range(NDMA)]
@@ -318,36 +294,40 @@ def rank_program(g, core, T, topo):
         rows = 128 if p is None else len(range(*p))
         return (ap, [(name, a, b)], [], n, 4 if SB[name][1] in (f32, i32) else 2, "s", rows)
 
+    def AB(c0, c1, a=0, b=S):
+        return (T.AB[:, c0:c1, a:b], [("AB", S * c0, S * c1)], [], (c1 - c0) * (b - a), 2, "s", 128)
+
     def X(win, off):
         return (win[0].indirect(off[0]), win[1], off[1], 16 * off[3], win[4], "x")
 
     def H(ap):
         return (ap, [], [], 0, 4, "h")
 
-    def op(eng, fn, out, ins, dma=False, pre=(), cost=None, per=1.0):
+    def size(eng, out, ins, dma, per):
+        n = out[3]
+        wide = [x for x in ins + [out] if x[3] == n]
+        if dma:
+            side = out if out[5] == "s" else ins[0]
+            return ("dma", side[3] * side[4] * side[6])
+        if eng == "pool":
+            return ("cyc", 170 + 2 * n)
+        if out[5] == "x":
+            return ("scat", n)
+        if any(x[5] == "x" for x in ins):
+            return ("gath", n)
+        if eng == "act":
+            return ("cyc", n)
+        if not all(x[5] == "s" for x in ins if x[3] == n):
+            per = 1.0
+        return ("cyc", max(64, n * per * (0.5 if all(x[4] == 2 for x in wide) else 1.0)))
+
+    def op(fns, out, ins, dma=False, pre=(), cost=None, per=1.0):
         rd = list(out[2])
         ins = [x for x in ins if isinstance(x, tuple)]
         for x in ins:
             rd += x[1] + x[2]
-        if cost is None:
-            n = out[3]
-            wide = [x for x in ins + [out] if x[3] == n]
-            if dma:
-                side = out if out[5] == "s" else ins[0]
-                cost = ("dma", side[3] * side[4] * side[6])
-            elif eng == "pool":
-                cost = ("cyc", 100 + 2 * n)
-            elif out[5] == "x":
-                cost = ("scat", n)
-            elif any(x[5] == "x" for x in ins):
-                cost = ("gath", n)
-            elif eng == "act":
-                cost = ("cyc", n)
-            else:
-                if not all(x[5] == "s" for x in ins if x[3] == n):
-                    per = 1.0
-                cost = ("cyc", max(64, n * per * (0.5 if all(x[4] == 2 for x in wide) else 1.0)))
-        ops.append({"e": eng, "fn": fn, "w": out[1], "r": rd, "dma": dma, "pre": pre, "c": cost})
+        ways = [(e,) + (cost or size(e, out, ins, dma, per)) for e in fns]
+        ops.append({"fns": fns, "ways": ways, "w": out[1], "r": rd, "dma": dma, "pre": pre})
 
     def a_(x):
         return x[0] if isinstance(x, tuple) else x
@@ -357,569 +337,473 @@ def rank_program(g, core, T, topo):
             for o, l, r, st, sp in items:
                 ins = g.tensor.matmul(o[0], l[0], r[0], st, sp)
             return ins
-        op("pe", fn, items[0][0], [x for it in items for x in it[1:3]],
-           cost=("pe", sum(max(min(64, l[3]), r[3]) * (4 if r[4] == 4 else 1) for o, l, r, st, sp in items)))
+        op({"pe": fn}, items[0][0], [x for it in items for x in it[1:3]],
+           cost=("pe", sum(max(min(64, l[3]), r[3]) for o, l, r, st, sp in items)))
 
-    def mm(o, l, r, st=True, sp=True):
-        mms([(o, l, r, st, sp)])
+    def group(items, first=True, stop=True):
+        mms([(o, l, r, first and n == 0, stop and n == len(items) - 1) for n, (o, l, r) in enumerate(items)])
 
-    def grp(o, pairs):
-        return [(o, l, r, n == 0, n == len(pairs) - 1) for n, (l, r) in enumerate(pairs)]
+    def act(o, i, f=Act.Identity, bias=0.0, scale=1.0, total=None):
+        op({"act": lambda: g.scalar.activation(o[0], i[0], f, bias=a_(bias), scale=a_(scale), accum_out=a_(total))},
+           o, [i, bias, scale])
+        if total:
+            ops[-1]["w"] = o[1] + total[1]
 
-    def group(o, pairs):
-        mms(grp(o, pairs))
+    def lin(o, i, scale=None, bias=None, pre=()):
+        def vec():
+            if scale is None and bias is None:
+                return g.vector.tensor_copy(o[0], i[0])
+            if bias is None:
+                return g.vector.tensor_scalar(o[0], i[0], a_(scale), None, Alu.mult)
+            if scale is None:
+                return g.vector.tensor_scalar(o[0], i[0], a_(bias), None, Alu.add)
+            return g.vector.tensor_scalar(o[0], i[0], a_(scale), a_(bias), Alu.mult, Alu.add)
 
-    def act(o, i, f=Act.Identity, bias=0.0, scale=1.0, pre=()):
-        op("act", lambda: g.scalar.activation(o[0], i[0], f, bias=a_(bias), scale=a_(scale)), o, [i, bias, scale], pre=pre)
+        def sca():
+            return g.scalar.activation(o[0], i[0], Act.Identity, bias=0.0 if bias is None else a_(bias),
+                                       scale=1.0 if scale is None else a_(scale))
+        op({"act": sca, "dve": vec}, o, [i, bias, scale], pre=pre)
 
     def cp(o, i):
-        op("dve", lambda: g.vector.tensor_copy(o[0], i[0]), o, [i])
+        op({"dve": lambda: g.vector.tensor_copy(o[0], i[0])}, o, [i])
 
     def tt(o, x, y, f):
-        op("dve", lambda: g.vector.tensor_tensor(o[0], x[0], y[0], f), o, [x, y], per=2.0)
+        op({"dve": lambda: g.vector.tensor_tensor(o[0], x[0], y[0], f)}, o, [x, y], per=2.0)
 
     def ts(o, x, s1, f0, s2=None, f1=None):
         if f1 is None:
-            op("dve", lambda: g.vector.tensor_scalar(o[0], x[0], a_(s1), None, f0), o, [x, s1])
+            op({"dve": lambda: g.vector.tensor_scalar(o[0], x[0], a_(s1), None, f0)}, o, [x, s1])
         else:
-            op("dve", lambda: g.vector.tensor_scalar(o[0], x[0], a_(s1), a_(s2), f0, f1), o, [x, s1, s2])
+            op({"dve": lambda: g.vector.tensor_scalar(o[0], x[0], a_(s1), a_(s2), f0, f1)}, o, [x, s1, s2])
+
+    def scan(o, d0, d1, f):
+        op({"dve": lambda: g.vector.tensor_tensor_scan(o[0], d0[0], d1[0], 0.0, Alu.add, f)}, o, [d0, d1])
 
     def ms(o, c):
-        op("dve", lambda: g.vector.memset(o[0], c), o, [])
+        op({"dve": lambda: g.vector.memset(o[0], c)}, o, [])
 
     def iota(o, pat, base=0, cm=0):
-        if SB[o[1][0][0]][1] == i32:
-            op("pool", lambda: g.iota(o[0], pat, base, cm), o, [])
-        else:
-            op("pool", lambda: g.iota(o[0], pat, base, cm, allow_small_or_imprecise_dtypes=True), o, [])
+        op({"pool": lambda: g.iota(o[0], pat, base, cm, allow_small_or_imprecise_dtypes=True)}, o, [])
 
     def fill(o, c):
-        iota(o, [[0, o[3]]], c)
+        if SB[o[1][0][0]][1] == i32:
+            fns = {"pool": lambda: g.iota(o[0], [[0, o[3]]], c, 0)}
+        else:
+            fns = {"pool": lambda: g.iota(o[0], [[0, o[3]]], c, 0, allow_small_or_imprecise_dtypes=True)}
+        fns["dve"] = lambda: g.vector.memset(o[0], c if SB[o[1][0][0]][1] == i32 else float(c))
+        op(fns, o, [])
 
-    def sel(o, i, pat, cmp, base, cm, other=0.0, pre=()):
-        op("pool", lambda: g.affine_select(o[0], i[0], pat, cmp, other, base, cm), o, [i], pre=pre)
+    def sel(o, i, pat, cmp, base, cm, other=0.0):
+        op({"pool": lambda: g.affine_select(o[0], i[0], pat, cmp, other, base, cm)}, o, [i])
 
-    def move(o, i, pre=()):
-        sel(o, i, [[0, o[3]]], Alu.is_ge, 0, 0, pre=pre)
+    def move(o, i):
+        op({"pool": lambda: g.affine_select(o[0], i[0], [[0, o[3]]], Alu.is_ge, 0.0, 0, 0),
+            "dve": lambda: g.vector.tensor_copy(o[0], i[0])}, o, [i])
 
     def dma(q, o, i, pre=()):
-        op(q, lambda: Q[q].dma_start(o[0], i[0]), o, [i], dma=True, pre=pre)
+        op({e: (lambda e=e: Q[e].dma_start(o[0], i[0])) for e in (q if q == BOTH else (q,))}, o, [i], dma=True, pre=pre)
 
     def win(z, blk, r):
         return V(z, 128 * blk + 15 - r, 128 * blk + 143 - r)
 
-    def to_list(o, z, src, a, b, first=True, last=True, per_r=False):
-        mms([(o, win(z, r if per_r else 0, r), V(src, a + r, b, 16), first and r == 0, last and r == 15) for r in range(16)])
+    def listed(o, z, src, a, b, per_r=False, p=None):
+        return [(o, V(z, 128 * r * per_r + 15 - r, 128 * r * per_r + 143 - r, p=p), V(src, a + r, b, 16, p=p)) for r in range(16)]
 
     others = [(rank + N - 1 - s) % N for s in range(N - 1)]
     mask = topo.mask(core, T.cores[others[0]])
     for r in others:
         mask &= topo.mask(core, T.cores[r])
     nloc = bin(mask).count("1")
-    nsig = (N - 1) * nloc
 
-    def send(t):
-        src = V("NEW", t * S, (t + 1) * S)
+    def send(t, a, b):
+        src = V("NEW", t * S + a, t * S + b)
         ids = [DstId(rid=topo.addr(T.cores[r])[0], pnc=topo.addr(T.cores[r])[1]) for r in others]
-        dsts = [T.Y[:, W + t * GH + s * S:W + t * GH + (s + 1) * S] for s in range(N - 1)]
+        dsts = [T.Y[:, W + t * GH + s * S + a:W + t * GH + s * S + b] for s in range(N - 1)]
         trs = [RemoteDMATransfer(dst_ids=ids, dma_engine_mask=mask, remote_sem=T.sem["arr%d" % t], srcs=[src[0]], dsts=dsts)]
-        op("pool", lambda: g.remote_dma_fused(trs, local_sem=T.sem.sent), H(None), [src], cost=("rem", 1))
+        op({"pool": lambda: g.remote_dma_fused(trs, local_sem=T.sem.sent)}, H(None), [src], cost=("rem", 0.4 + 0.6 * (b - a) / S))
         ops[-1]["send"] = "arr%d" % t
 
-    dma("sp", V("C", 0, S), H(T.cl[:, 0:S]))
-    dma("act", V("FW"), H(T.fw0[:, :]))
-    for q in range(4):
-        dma("sp", V("LK", 512 * q, 512 * (q + 1)), H(T.lk[:, 512 * q:512 * (q + 1)]))
-    dma("sp", V("Y", 0, W0), H(T.y0[:, :]))
-    dma("sp", V("TH", p=(0, 8, 1)), H(T.th[:, :]))
+    for name in LOADS:
+        if name == "FW":
+            dma("sp", V("FW"), H(T.fw0[:, :]))
+        elif name == "C":
+            dma("sp", V("C", 0, S), H(T.cl[:, 0:S]))
+        elif name == "LK":
+            dma("sp", V("LK"), H(T.lk[:, :]))
+        elif name == "TH":
+            dma("sp", V("TH", p=(0, 8, 1)), H(T.th[:, :]))
+        else:
+            dma("sp", V("Y", 0, W0), H(T.y0[:, :]))
     dma("sp", V("C", S, M), H(T.cl[:, S:M]))
-    dma("sp", V("C", W0, W0 + S), H(T.cl[:, 0:S]))
 
-    ms(V("ONE"), 1.0)
-    ms(V("HF"), 0.0)
-    ms(V("ZD"), 0.0)
-    iota(V("PI", 0, 1), [[0, 1]], 0, 1)
-    iota(V("LO"), [[1, S]])
-    iota(V("HF", 1, 160, 16), [[S, 10]])
-    iota(V("HF", 3, 64, 16), [[S, 4]])
-    iota(V("HF", 115, 160, 16), [[S, 3]], W0)
-    iota(V("HF", 4, 48, 16), [[S, 3]], S)
-    iota(V("HF", 132, 160, 16), [[S, 2]], S)
+    fill(V("ONE"), 1)
+    fill(V("HF"), 0)
+    fill(V("ZD"), 0)
+    iota(V("HF", 14, 24), [[S, 10]])
+    iota(V("HF", 42, 46), [[S, 4]])
+    iota(V("HF", 49, 52), [[S, 3]], W0)
+    iota(V("HF", 40, 42), [[S, 2]], W0)
+    for a, b, c in ((10, 11, 1), (32, 35, 1), (39, 40, S - W0), (54, 56, 1)):
+        fill(V("HF", a, b), c)
+    iota(V("HG", 0, 16), [[0, 8], [-1, 2]], 1)
+    iota(V("HG", 16, 32), [[0, 8], [1, 2]])
+    iota(V("HG", 32, 64), [[1, 32]])
     sel(V("ZD", 15, 2063, 16), V("ONE"), [[-1, 16], [-16, 8]], Alu.is_equal, 0, 1)
-    sel(V("ID"), V("ONE"), [[-1, 128]], Alu.is_equal, 0, 1)
-    for a, b, s, c in ((66, 112, 16, 1.0), (69, 112, 16, 1.0), (162, 163, 1, S - W0), (165, 166, 1, 2 * S), (178, 179, 1, W0),
-                       (179, 181, 1, 1.0), (194, 195, 1, -(W0 + S)), (210, 211, 1, W0 + S), (211, 212, 1, 1.0), (224, 225, 1, 1.0),
-                       (242, 244, 1, 1.0 / 16)):
-        ms(V("HF", a, b, s), float(c))
+    if PACKED:
+        fill(V("ZP"), 0)
+        lin(V("Z5"), V("ZD", 15, 2063, 16), KEY)
+        tt(V("ZP", 15, 15 + 16 * 88, 16), V("ZD", 15, 15 + 16 * 88, 16), V("Z5", 40, 128), Alu.add)
+        tt(V("ZP", 15 + 16 * 88, 2063, 16), V("ZD", 15 + 16 * 88, 2063, 16), V("Z5", 0, 40), Alu.add)
+    group([(V("P7", 0, 14), win("ZD", r, r), V("HF", 14 * r, 14 * (r + 1))) for r in range(4)]
+          + listed(V("P7", 14, 18), "ZD", "HG", 0, 64, per_r=True))
+    lin(V("CT"), V("P7", 0, 18))
+    row, row16, even, odd = V("CT", 16, 17), V("CT", 17, 18), V("CT", 14, 15), V("CT", 15, 16)
+    iota(V("LO"), [[1, S]])
+    for B in range(10):
+        lin(V("FP", S * B, S * (B + 1)), V("LO"), V("CT", 10, 11), V("CT", B, B + 1))
     cp(V("AU"), V("C", 0, S))
     cp(V("FL", 0, 112), V("FW"))
-    to_list(V("P7", 0, 16), "ZD", "HF", 0, S, per_r=True)
-    act(V("CT"), V("P7", 0, 16))
-    ts(V("PI", 1, 2), V("PI", 0, 1), 15, Alu.bitwise_and)
-    ts(V("PI", 2, 3), V("PI", 0, 1), 63, Alu.bitwise_and)
-    ts(V("PI", 3, 4), V("PI", 0, 1), 1, Alu.bitwise_and)
+    for a, b in ((0, 56), (56, 112)):
+        lin(V("YF", 16 * a, 16 * b), X(V("Y", 0, W0), V("FL", a, b)))
+        lin(V("FS", 16 * a, 16 * b), X(V("FP", 0, W0), V("FL", a, b)))
+        ops[-1]["lead"] = LEAD
+    move(V("FS", W0, W), V("FP", W0, W))
+    move(V("C", W0, W0 + S), V("C", 0, S))
+    iota(V("PF"), [[-32, 4]], 0, 1)
+    ts(V("ID"), V("LO", 0, 128), V("PF", 0, 1), Alu.is_equal)
+    lin(V("NI"), V("ID"), -1.0)
+    lin(V("N4"), V("ID"), -KEY)
+    ts(V("IE"), V("ID"), 0.5 - 2.0 ** -11, Alu.mult)
+    iota(V("KR"), [[1, 32], [0, 16]])
+    for u in range(3):
+        ts(V("R", 512 * u, 512 * (u + 1)), V("KR"), V("PF", u, u + 1), Alu.is_equal, V("ID", 96, 97), Alu.max)
+    ms(V("OT", p=(96, 128, 1)), MAGIC)
+    ms(V("MG"), MAGIC)
+    ts(V("PG"), V("PF", 0, 1), row, Alu.subtract)
+    ts(V("BO"), V("KR", 0, 128), 16.0, Alu.mult, V("PG"), Alu.is_equal)
+    ts(V("E2"), V("KR", 0, 128), 2.0, Alu.mult, V("PF", 0, 1), Alu.is_equal)
     fill(V("ZE"), 0)
-    fill(V("BIG"), -4096)
-    fill(V("S16"), 16)
-    cp(V("PF", 0, 4), V("PI"))
-    act(V("PF", 4, 5), V("PF", 1, 2), bias=16.0)
-    sel(V("TMP"), V("ONE"), [[-16, 8], [0, 16]], Alu.is_ge, 0, 1)
-    sel(V("BO"), V("TMP"), [[16, 8], [0, 16]], Alu.is_ge, 15, -1)
-    iota(V("R"), [[1, 64], [0, 16]])
-    sel(V("GX"), V("S16"), [[-1, 8], [0, 16]], Alu.is_equal, 0, 1)
-    iota(V("KC"), [[-15, 2], [0, 8], [-1, 16]], 15)
-    iota(V("BLI", 0, 16), [[1, 16]])
-    iota(V("BLI", 16, 32), [[0, 2], [1, 8]])
-    iota(V("BLI", 32, 40), [[2, 4], [0, 2]])
-    fill(V("K0"), 120)
+    move(V("ZE", 15, 143, 16), V("BO", 0, 128, 16))
+    lin(V("ZK"), V("ZE"), KEY)
+    lin(V("ZB"), V("ZE"), -KEY)
+    iota(V("KI"), [[0, 16], [1, 16]])
+    ts(V("EYE", 0, S), V("KI"), row, Alu.is_equal)
+    wide = 256 * max(c1 - c0 for parts in PARTS for c0, c1 in parts)
+    for a, b in ((S, 2 * S), (2 * S, M)):
+        move(V("EYE", a, b), V("EYE", 0, b - a))
+    for a in range(M, wide, M):
+        dma("sp", V("EYE", a, a + M), V("EYE", 0, M))
+    ts(V("TRI"), V("KI"), row, Alu.is_le, 2 * KEY, Alu.mult)
+    fill(V("RP"), 1)
+    fill(V("RP", 0, S, 16), 1 - 2 ** 24)
+    lin(V("RQ"), V("RP"), -1.0)
+    fill(V("GX"), 0)
+    lin(V("GX", 15, 143, 16, p=(0, 8, 1)), V("ID", 0, 8, p=(0, 8, 1)), -KEY)
+    ts(V("TF", p=(0, 8, 1)), V("TH", p=(0, 8, 1)), 2048.0, Alu.subtract)
+    group(listed(V("P6", 0, 16), "GX", "TF", 0, S, p=(0, 8, 1)))
+    lin(V("LIM"), V("P6", 0, 16), bias=-2048.0 * KEY)
+    lin(V("LI0"), V("LIM"), bias=-7.5 * KEY)
     iota(V("IDL"), [[16, 160]])
-    iota(V("NR"), [[1, RO * S]], W0)
-    act(V("YF", 0, W0), X(V("Y", 0, W0), V("FL", 0, 112)), scale=0.5)
-    act(V("NI"), V("ID"), scale=-1.0)
-    sel(V("IF"), V("ONE"), [[-1, 128]], Alu.is_equal, 0, 1)
-    for B in range(10):
-        act(V("FB", S * B, S * (B + 1)), V("LO"), scale=V("CT", 14, 15), bias=V("CT", B, B + 1))
-    for q in range(3):
-        cp(V("L", 32 + 512 * q, 32 + 512 * (q + 1)), V("LK", 512 * q, 512 * (q + 1)))
+    lin(V("IDL"), V("IDL"), bias=row)
+    lin(V("XJ"), V("IDL", 0, 16), 16.0, 15.0)
+    lin(V("LI"), V("IDL", 0, 16))
+    ts(V("LJ", 0, 16), V("IDL", 0, 16), OFS, Alu.subtract)
+    ts(V("LJ", 16, 48), V("IDL", 128, 160), OFS, Alu.subtract)
+    move(V("FO", 144, 160), V("IDL", 144, 160))
+    ms(V("KA"), 32.0 - OFS)
+    tt(V("ZF", 0, 143), V("ZD", 0, 143), V("ZD", 128, 271), Alu.add)
+    tt(V("ZV", 0, 143), V("ZD", 256, 399), V("ZD", 384, 527), Alu.add)
+    for u in range(2):
+        lin(V("ZG", 144 * u, 144 * u + 143), V("ZD", 256, 399), float(W - M + u * GH))
+        tt(V("ZY%d" % u, 0, 143), V("ZG", 144 * u, 144 * u + 143), V("ZF", 0, 143), Alu.add)
+    iota(V("OB"), [[S, 4]], W0)
+    lin(V("OB"), V("OB"), odd)
+    for t in range(RO):
+        lin(V("NW", t * S, (t + 1) * S), V("LO"), odd, V("OB", t, t + 1))
+    for q in range(4):
+        move(V("L", 32 + 512 * q, 32 + 512 * (q + 1)), V("LK", 512 * q, 512 * (q + 1)))
+    fill(V("L", 0, 32), 0)
+    dma("sp", H(T.lo[0:128:2, :]), V("L", 32, 32 + NA, p=(0, 128, 2)))
+    fill(V("C", M, W0), 0)
+    fill(V("Y", W0 + S, W), 0)
+    fill(V("FS", W, W + GH), 0)
 
-    def late_a():
-        ts(V("R"), V("R"), V("PF", 2, 3), Alu.is_equal)
-        ts(V("GO", 0, 8), V("BO", 0, 128, 16), 16.0, Alu.mult)
-        ts(V("GO", 8, 16), V("BO", 0, 128, 16), -16.0, Alu.mult)
-        sel(V("C128"), V("ONE"), [[0, 128]], Alu.is_equal, 0, 1)
-        cp(V("TF", p=(0, 8, 1)), V("TH", p=(0, 8, 1)))
-
-    def late_b():
-        for h in range(2):
-            mm(V("P7", 128 * h, 128 * (h + 1)), V("TF", 128 * h, 128 * (h + 1), p=(0, 8, 1)), V("GX", p=(0, 8, 1)))
-        for h in range(2):
-            act(V("S%d" % h, 256, 384), V("P7", 128 * h, 128 * (h + 1)), bias=15.0)
-        act(V("FA", 0, W0), X(V("FB", 0, W0), V("FL", 0, 112)))
-        dma("sp", V("FA", W0, W), V("FB", W0, W))
-        fill(V("RM"), 0)
-        fill(V("RM", 0, S, 16), -16000000)
-        sel(V("E0"), V("ONE"), [[0, 8], [1, 16]], Alu.is_equal, 0, 0)
-        move(V("FV"), V("FA", 0, S))
-        cp(V("BL"), V("BLI"))
-        fill(V("ST0", 15, 16), 1)
-        fill(V("ST1", 15, 16), 1)
-        move(V("ZE", 15, 143, 16), V("BO", 0, 128, 16))
-        act(V("ZB"), V("ZE"), scale=-4096.0)
-        act(V("N2"), V("ID"), scale=-2.0)
-        cp(V("L", 32 + 1536, 32 + NA), V("LK", 1536, NA))
-        fill(V("L", 0, 32), 0)
-        dma("sp", H(T.lo[0:128:2, :]), V("L", 32, 32 + NA, p=(0, 128, 2)))
-
-    def late_c():
-        for q in range(4):
-            fill(V("ZT", 516 * q, 516 * (q + 1)), 0)
-        sel(V("TM2"), V("BIG"), [[0, 16], [-16, 8]], Alu.is_ge, 0, 1)
-        sel(V("ZT", 15, 2063, 16), V("TM2"), [[1, 16], [16, 8]], Alu.is_gt, 0, -1)
-        tt(V("ZF", 0, 143), V("ZD", 0, 143), V("ZD", 128, 271), Alu.add)
-        tt(V("ZV", 0, 143), V("ZD", 256, 399), V("ZD", 384, 527), Alu.add)
-        tt(V("ZX", 0, 143), V("ZD", 512, 655), V("ZD", 640, 783), Alu.add)
-        ts(V("IDL"), V("IDL"), V("PF", 1, 2), Alu.add)
-        fill(V("C16"), 16)
-        fill(V("C", M, W0), 0)
-        cp(V("FL", 112, 160), V("IDL", 112, 160))
-        cp(V("FY", 112, 144), V("IDL", 112, 144))
-        fill(V("Y", W0 + S, W), 0)
-        fill(V("FA", W, W + S), 0)
-        fill(V("FB", W, W + S), 0)
-        ts(V("LJ"), V("IDL", 0, 16), W - OFS, Alu.add)
-        act(V("BV"), V("BO"), scale=V("CT", 15, 16))
-        for u in range(2):
-            act(V("ZK", 144 * u, 144 * u + 143), V("ZD", 256, 399), scale=float(W - M + u * GH))
-            tt(V("ZY%d" % u, 0, 143), V("ZK", 144 * u, 144 * u + 143), V("ZF", 0, 143), Alu.add)
-        act(V("LI"), V("IDL", 0, 16))
-        act(V("HI"), V("ID"), scale=0.5)
-        act(V("NR"), V("NR"), scale=V("PF", 3, 4))
-        move(V("FO", 144, 160), V("IDL", 144, 160))
-
-    def nrs():
-        return [(V("C16"), V("ST%d" % h, 272, 400)) for h in range(2)]
-
-    def keys0(h, more):
-        bank = "P%d" % (5 + h)
-        mms([(V(bank, 0, S), V("C128"), V("KC"), True, False)] + [(V(bank, 0, 128), l, r, False, False) for l, r in more])
-
-    pend = []
     for t in range(RO):
         wt = W0 + t * S
-        F, F2 = ("FA", "FB") if t % 2 == 0 else ("FB", "FA")
         last = t == RO - 1
-        a32 = V("C", 0, S) if t == 0 else V("A32")
-        fv = V("FV")
+        atoms = "C" if t == 0 else "A32"
         own = "Y" if t == 0 else "OWN"
         lwin = V("LK") if t == 0 else V("L", 32, 32 + NA)
+        parts = PARTS[t]
+        nsig = (N - 1) * nloc * (len(parts) if APART else 1)
+        F1, F2 = ("FP", "FS") if t == 1 else ("FS", "FP")
 
-        def links(q):
-            for j in ((2 * q, 2 * q + 1) if q == 1 else (None,)):
-                c0, c1 = (64 * q, 64 * (q + 1)) if j is None else (32 * j, 32 * (j + 1))
-                ts(V("G", 16 * c0, 16 * c1), X(lwin, V("AU", c0, c1)), OFS, Alu.subtract)
+        if t > 0:
+            lin(V("OWN"), X(V("Y", 0, wt), V("VU")))
+        for u, a in enumerate((0, 96, 160)):
+            group([(V("P7", 128 * u, 128 * (u + 1), p=(0, 96, 1)), V(own, a, a + 96), V("NI"))])
+        lin(V("OT", p=(0, 96, 1)), V("P7", 0, 384, p=(0, 96, 1)))
+        if not last:
+            group([(V("P6", 0, S), V("BO"), V(own, 0, S))])
+            lin(V("U"), V("P6", 0, S), bias=float(t + 1))
 
-        def lists(q):
-            bank, c0 = "P%d" % (q // 2), 64 * (q % 2)
+        for a, b in LINKS:
+            ts(V("G", 16 * a, 16 * b), X(lwin, V("AU", a, b)), OFS, Alu.subtract)
+        for a, b in (() if PACKED else PICKS):
             for j in range(2):
-                group(V(bank, 128 * j + c0, 128 * j + c0 + 64),
-                      [(win("ZD", (k + 5 * j) % 16, k), V("G", 1024 * q + k, 1024 * (q + 1), 16)) for k in range(16)])
-                if j == 0 or q == 0:
-                    ts(V("BC", S * j + 64 * q, S * j + 64 * (q + 1)), V(bank, 128 * j + c0, 128 * j + c0 + 64), OFS, Alu.add)
-            if q == 1:
-                ts(V("BC", S + 64, S + 128), V(bank, 192, S), OFS, Alu.add)
-            if q == 3:
-                ts(V("BC", S + 128, 2 * S), V(bank, 128, S), OFS, Alu.add)
-            if q % 2:
-                act(V("B32", S * (q // 2), S * (q // 2 + 1)), V(bank, 0, S))
+                group([(V("P%d" % j, a, b), win("ZD", (k + 5 * j) % 16, k), V("G", 16 * a + k, 16 * b, 16)) for k in range(16)])
+                ts(V("BC", S * j + a, S * j + b), V("P%d" % j, a, b), OFS, Alu.add)
+            if a % 128 == 0:
+                lin(V("B32", a, a + 128), V("P0", a, a + 128))
+        for n, (a, b) in enumerate(PICKS if PACKED else ()):
+            x = V("P%d" % (n % 2), a, b)
+            group([(x, win("ZP", k, k), V("G", 16 * a + k, 16 * b, 16)) for k in range(16)])
+            ts(V("CK", a, b), x, KEY * MAGIC, Alu.add, KEY * MAGIC, Alu.subtract)
+            ts(V("BC", S + a, S + b), V("CK", a, b), 1.0 / KEY, Alu.mult, OFS, Alu.add)
+            tt(V("B32", a, b), x, V("CK", a, b), Alu.subtract)
+            ts(V("BC", a, b), V("B32", a, b), OFS, Alu.add)
 
-        def bl(j, o):
-            return V("BC", S * o + 32 * j, S * o + 32 * (j + 1))
+        for a, b in STATES:
+            for j, name in enumerate(("GA", "GB")):
+                lin(V(name, 16 * a, 16 * b), X(V("YF", 0, wt), V("BC", S * j + a, S * j + b)))
 
-        def ga(j):
-            if (t, j) in GA_DVE:
-                ts(V("G1", 512 * j, 512 * (j + 1)), X(V("YF", 0, wt), bl(j, 0)), 1023.75, Alu.add)
-            else:
-                act(V("G1", 512 * j, 512 * (j + 1)), X(V("YF", 0, wt), bl(j, 0)), bias=1023.75)
+        def distances(n, c0, c1):
+            u = min(c0 // 6, 2)
+            a, b, r0 = S * c0, S * c1, S * (c0 - (0, 6, 10)[u])
+            bank = V("P%d" % (2 + n % 3), 0, b - a)
+            group([(bank, V("IE"), V("GA", a, b)), (bank, V("IE"), V("GB", a, b)),
+                   (bank, V("OT", 128 * u, 128 * (u + 1), p=(0, 97, 1)), V("R", r0, r0 + b - a, p=(0, 97, 1)))])
+            act(AB(c0, c1), bank, Act.Abs, bias=-MAGIC)
 
-        def gb(j):
-            tt(V("YH", 512 * j, 512 * (j + 1)), X(V("YF", 0, wt), bl(j, 1)), V("G1", 512 * j, 512 * (j + 1)), Alu.add)
-            h, u = j // 4, (j % 4) // 2
-            group(V("P%d" % (2 + j % 3)), [(V("ID"), V("YH", 512 * j, 512 * (j + 1))),
-                                           (V("OT", 128 * h, 128 * (h + 1), p=(64 * u, 64 * u + 64, 1)),
-                                            V("R", 512 * (j % 2), 512 * (j % 2 + 1), p=(64 * u, 64 * u + 64, 1)))])
+        def scans(bank, c0, c1):
+            scan(V("SC", 16 * c0, 16 * c1), V("RQ", 0, 16 * (c1 - c0)), V(bank, 16 * c0, 16 * c1), Alu.min)
+            scan(V("SC", S + 16 * c0, S + 16 * c1), V("RP", 0, 16 * (c1 - c0)), V(bank, 16 * c0, 16 * c1), Alu.max)
 
-        def ab(j):
-            act(V("AB", 512 * j, 512 * (j + 1)), V("P%d" % (2 + j % 3)), Act.Abs, bias=-1024.0)
+        def part(n, c0, c1):
+            nc, a, b = c1 - c0, 16 * c0, 16 * c1
+            nl = b - a
+            final = n == len(parts) - 1
+            bl, ba, bz = ("P5", "P6", "P0") if final else ("P5", "P5", "P0")
+            bq, bp, bd = ("P2", "P3", "P4") if final else ("P7", "P7", "P1")
+            top = c1
+            for k, (d0, d1) in enumerate(SUMS):
+                if c0 <= d0 < c1:
+                    distances(k, d0, d1)
+                    for e0, e1 in KEYS:
+                        if e0 == d0:
+                            bank = "P6" if e1 <= SCANS else "P5"
+                            group([(V(bank, 16 * e0, 16 * e1), win("ZK", 0, r), AB(e0, e1, 16 * r, 16 * r + 16)) for r in range(16)])
+                            if e0 in (c0, SCANS):
+                                scans(bank, e0, top)
+                                top = e0
+            m0 = 2 * c0
+            tt(V("MI", m0 + nc, m0 + 2 * nc), V("SC", a + 15, b, 16), V("XJ", 0, nc), Alu.add)
+            tt(V("MI", m0, m0 + nc), V("XJ", 0, nc), V("SC", S + a + 15, S + b, 16), Alu.subtract)
+            for j0, j1 in (((m0 + nc, m0 + 2 * nc), (m0, m0 + nc)) if QFIRST[t] else ((m0, m0 + 2 * nc),)):
+                ts(V("JI", j0, j1), V("MI", j0, j1), int(KEY) - 1, Alu.bitwise_and)
+                cp(V("JU", j0, j1), V("JI", j0, j1))
+            jp, jq = V("JU", m0, m0 + nc), V("JU", m0 + nc, m0 + 2 * nc)
+            nr = V("NR", c0, c1)
+            tt(nr, V("MI", m0, m0 + nc), V("LIM", c0, c1), Alu.is_ge)
+            eye = V("EYE", 0, 16 * nl)
 
-        def keys(h):
-            bank = "P%d" % (5 + h)
+            for j, name in enumerate(("GA", "GB")):
+                lin(V("PQ", S * j + a, S * j + b), X(V(name, 16 * a, 16 * b), jq))
+            o = V(bq, 0, nl)
+            group([(o, V("NI"), V(own, a, b))], stop=False)
+            group([(o, V("IE"), V("PQ", a, b)), (o, V("IE"), V("PQ", S + a, S + b)), (o, V("ID"), V("MG", 0, nl))], first=False)
+            act(V("SG", a, b), o, Act.Sign, bias=-MAGIC)
+            new = V("NEW", t * S + a, t * S + b)
+            tt(new, V("SG", a, b), V(own, a, b), Alu.add)
+            if APART:
+                send(t, a, b)
+            elif final:
+                send(t, 0, S)
+
+            pa, pb, pq, l0 = 3 * a, 3 * a + nl, 3 * a + 2 * nl, 4 * c0
+            tt(V("PR", pa, pa + nl), X(eye, jp), V(atoms, a, b), Alu.mult)
+            cols = (0, nc, 1)
+            group([(V(ba, r, 128, 16, p=cols), V("PR", pa + r, pa + nl, 16), V("BO", 0, 128, 16)) for r in range(16)]
+                  + [(V(ba, 0, 128, p=cols), nr, V("N4"))])
+            at = V("AT", 128 * n, 128 * (n + 1), p=cols)
+            ts(at, V(ba, 0, 128, p=cols), -1.0, Alu.mult)
+
+            def lst(k0, k1, name="LL"):
+                return V(name, (l0 if name == "LL" else 0) + nc * k0, (l0 if name == "LL" else 0) + nc * k1)
+            tt(V("PR", pq, pq + nl), X(eye, jq), V("B32", a, b), Alu.mult)
+            if not last:
+                tt(V("PR", pb, pb + nl), X(eye, jp), V("B32", a, b), Alu.mult)
+            lj = V("LJ", 16 * t + c0, 16 * t + c1)
+            al = [(lst(2, 3, bl), at, V("NI", 0, nc, p=cols)), (lst(2, 3, bl), V("ID"), V("KA", 0, nc))]
             if t == 0:
-                keys0(h, [])
-            for a, b in (((0, 128),) if h == 0 else ((0, 64), (64, 96), (96, 128))):
-                mms([(V(bank, k, S, 16, p=(a, b, 1)), V("AB", 2048 * h + 16 * a + k, 2048 * h + 16 * b, 16), V("GO"), False,
-                      k == 15) for k in range(16)])
+                group(listed(V("P1", 0, nc), "ZE", "PR", pq, pq + nl) + [(V("P1", 0, nc), V("NI"), lj)])
+                tt(V("NH", c0, c1), V("P1", 0, nc), nr, Alu.mult)
+                group(listed(lst(0, 1, bl), "ZE", "PR", pb, pb + nl) + al
+                      + [(lst(1, 2, bl), V("ID"), lj), (lst(1, 2, bl), V("ID"), V("NH", c0, c1))])
+                ts(lst(0, 3), lst(0, 3, bl), OFS, Alu.add)
+            else:
+                tt(V("NV", c0, c1), nr, V("VS", c0, c1), Alu.mult)
+                k0 = 1 if last or not MERGE else 0
+                group(listed(lst(k0, 2, bl), "ZE", "PR", pb + nl * k0, pq + nl) + al
+                      + [(lst(3, 4, bl), V("ID"), V("NV", c0, c1)), (lst(3, 4, bl), V("ID"), lj)])
+                ts(lst(k0, 4), lst(k0, 4, bl), OFS, Alu.add)
+                if not last and not MERGE:
+                    group(listed(V("P1", 0, nc), "ZE", "PR", pb, pb + nl))
+                    ts(lst(0, 1), V("P1", 0, nc), OFS, Alu.add)
+            lin(V("EF", a, b), X(V(F1, 0, wt), lst(1, 2)))
+            lin(V("VAL", a, b), X(V("L"), lst(2, 3)), even)
 
-        def choose(h):
-            sb, st = "S%d" % h, "ST%d" % h
-            o, d0, d1 = V(sb, 0, S), V("RM"), V("P%d" % (5 + h), 0, S)
-            op("dve", lambda: g.vector.tensor_tensor_scan(o[0], d0[0], d1[0], 0.0, Alu.add, Alu.max), o, [d0, d1])
-            ops[-1]["hint"] = list(early)
-            cp(V("SF", 16 * h, 16 * (h + 1)), V(sb, 15, S, 16))
-            tt(V(st, 16, 400), X(V("SF", 16 * h, 16 * (h + 1)), V("BL", 0, 24)), V(sb), Alu.is_le)
+            d1, d2 = V(bd, 0, nl), V(bd, nl, nl + nl // 2)
+            ne = 3 * nl // 2 if PAIRS else nl
+            group([(d1, V("BO"), V("PR", pa, pa + nl)), (d1, V("ID"), V("TRI", 0, nl))]
+                  + [(V(bd, nl + 16 * c, nl + 16 * (c + 1)), V("BO"), V("PR", pa + 32 * c + 16, pa + 32 * c + 32))
+                     for c in range(nc // 2 * PAIRS)], stop=False)
+            group([(d1, at, V("R", 0, nl, p=cols))] + [(d2, at, V("E2", 0, nl // 2, p=cols))] * PAIRS, first=False)
+            e0 = 3 * a // 2
+            if EQ_ACT[t]:
+                act(V("EA", e0, e0 + ne), V(bd, 0, ne), Act.Abs)
+                act(V("EQ", e0, e0 + ne), V("EA", e0, e0 + ne), Act.Relu, bias=1.0, scale=-1.0)
+            else:
+                ts(V("EQ", e0, e0 + ne), V(bd, 0, ne), 0.0, Alu.is_equal)
+            z = V(bz, 0, nc)
+            group([(z, at, V("NI", 0, nc, p=cols)), (z, V("ID"), V("KA", 0, nc))] + listed(z, "ZB", "EQ", e0, e0 + nl)
+                  + listed(V(bz, 1, nc, 2), "ZB", "EQ", e0 + nl, e0 + 3 * nl // 2) * PAIRS)
+            if PAIRS:
+                for u, spare in enumerate((row, row16)):
+                    ts(V("OC", c0 + u, c1, 2), V(bz, u, nc, 2), OFS, Alu.add, spare, Alu.max)
+                for c in range(c1 - 2, c0 - 2, -2):
+                    tt(X(V("L"), V("OC", c, c + 2)), V("VAL", 16 * c, 16 * c + 32), V("NW", t * S + 16 * c, t * S + 16 * c + 32), Alu.add)
+            else:
+                ts(V("OC", 2 * c0, 2 * c1, 2), z, OFS, Alu.add, row, Alu.max)
+                for c in range(c1 - 1, c0 - 1, -1):
+                    tt(X(V("L"), V("OC", 2 * c, 2 * c + 1)), V("VAL", 16 * c, 16 * c + 16), V("NW", t * S + 16 * c, t * S + 16 * c + 16), Alu.add)
 
-            def hot(c):
-                return [(V(st, c, c + 128), V("ID")), (V(st, c - 1, c + 127), V("NI")), (V("E0"), V("ID"))]
-            mms(grp(oh(h, 0), hot(144)) + grp(oh(h, 1), [(V(st, 272, 400), V("ID"))]))
-            mms(grp(oh(h, 3), hot(16) + [(V(st, 272, 400), V("N2"))]) + grp(oh(h, 2), hot(16)))
+            for j, name in enumerate(("GA", "GB")):
+                lin(V("PQ", S * (2 + j) + a, S * (2 + j) + b), X(V(name, 16 * a, 16 * b), jp))
+            o = V(bp, S, S + nl)
+            group([(o, V("IE"), V("PQ", 2 * S + a, 2 * S + b)), (o, V("IE"), V("PQ", 3 * S + a, 3 * S + b)),
+                   (o, V("ID"), V("MG", 0, nl))])
+            lin(V("Y" if last else "YF", wt + a, wt + b), o, bias=-MAGIC)
+            if not last:
+                move(V("Y", wt + a, wt + b), V("YF", wt + a, wt + b))
+            if t == 0:
+                move(V("Y", a, b), new)
+            else:
+                cp(X(V("Y", 0, wt), V("VU", c0, c1)), new)
 
-        def oh(h, j):
-            return V("P4" if h == 1 and j > 1 else "P%d" % h, 128 * j, 128 * (j + 1))
+            if not last:
+                tt(V("PC", a, b), X(eye, jp), V("U", a, b), Alu.mult)
+                tt(V("C" if t == 0 else "CN", a, b), V("PC", a, b), V(atoms, a, b), Alu.add)
+                if DIRECT:
+                    ts(V("C" if t == 0 else "CN", a, b), V("C" if t == 0 else "CN", a, b), NA - 1, Alu.bitwise_and)
+                if t > 0:
+                    cp(X(V("C", 0, wt), V("VU", c0, c1)), V("CN", a, b))
 
-        def half(name, h, c0=0):
-            return V(name, c0 + 128 * h, c0 + 128 * (h + 1))
+        for n, (c0, c1) in enumerate(parts):
+            part(n, c0, c1)
+        for c0, c1 in parts:
+            if t == 0:
+                lin(V(F1, 16 * c0, 16 * c1), V("EF", 16 * c0, 16 * c1))
+            else:
+                cp(X(V(F1, 0, W), V("LL", c0 + 3 * c1, 4 * c1)), V("EF", 16 * c0, 16 * c1))
 
-        def picks_q(h):
-            for o in range(2):
-                tt(half("PR", 3 + o, 768 * h), oh(h, 0), half("B32", o, S * h), Alu.mult)
+        def squares():
+            nb = S if t == 0 else M
+            fp = V(F1, 0, W + t * GH if t else W0)
+            for a, b in (((64, 88), (88, 112)) if t else ((16, 64), (64, 112))):
+                lin(V(F2, 16 * a, 16 * b), X(fp, V("FY" if t else "FL", a, b)))
+            group(listed(V("P2", 0, nb // 16), "ZF", F1, 0, nb))
             if t > 0:
-                tt(half("PR", 5, 768 * h), oh(h, 1), half("VB", h), Alu.mult)
-
-        def lists_of(h, bank, a, b, skip):
-            b -= 1 if t == 0 and b == 6 else 0
-            to_list(V(bank, 0, 8 * (b - a)), "ZE", "PR", 768 * h + 128 * a, 768 * h + 128 * b, last=b < 6)
-            if b == 6:
-                mm(V(bank, 8 * (5 - a), 8 * (6 - a)), V("ID"), V("LJ", 8 * h, 8 * h + 8), False, True)
-            return lambda: ts(V("LU", 40 * h + 8 * (a + skip - 1), 40 * h + 8 * (b - 1)), V(bank, 8 * skip, 8 * (b - a)), OFS, Alu.add)
-
-        def picks_p(h):
-            tt(half("PR", 0, 768 * h), oh(h, 3), half("A1", h), Alu.mult)
-            for o in range(2):
-                tt(half("PR", 1 + o, 768 * h), oh(h, 2), half("B32", o, S * h), Alu.mult)
-
-        def state_q(h):
-            c0 = 512 * h + S
-            act(V("PQ", c0, c0 + S), X(V("YF", 0, wt), V("LU", 40 * h + 16, 40 * h + 32)))
-            group(V("P7", 0, 128), [(V("ID"), half("PQ", 0, c0)), (V("ID"), half("PQ", 1, c0)), (V("NI"), half(own, h))])
-            act(half("SG", 0, S * h), V("P7", 0, 128), Act.Sign, bias=-0.75)
-            act(half("SG", 1, S * h), V("P7", 0, 128), Act.Sign, bias=0.25)
-            group(V("P7", 128, S), [(V("ID"), half(own, h)), (V("HI"), half("SG", 0, S * h)), (V("HI"), half("SG", 1, S * h))])
-            act(half("NEW", h, t * S), V("P7", 128, S))
-
-        def state_p(h):
-            c0 = 512 * h
-            act(V("PQ", c0, c0 + S), X(V("YF", 0, wt), V("LU", 40 * h, 40 * h + 16)))
-            group(V("P7", S, S + 128), [(V("ID"), half("PQ", 0, c0)), (V("ID"), half("PQ", 1, c0))])
-            act(half("RP", h), V("P7", S, S + 128), bias=MAGIC, scale=1.0 - 2.0 ** -10)
-            act(half("Y", h, wt), half("RP", h), bias=-MAGIC)
-
-        def claims(h):
-            z = V("P5", 8 * h, 8 * (h + 1))
-            mm(z, V("IF"), V("AL", 8 * h, 8 * (h + 1)), True, False)
-            c0 = S * h
-            tt(V("EQ", c0, c0 + S), X(V("AL", 8 * h, 8 * (h + 1)), V("BL", 24, 40)), V("AR", c0, c0 + S), Alu.is_equal)
-            mms([(V("P5", 8 * h + 1, 8 * h + 8, 2), win("ZB", 0, r), V("EQ", c0 + 144 + r, c0 + S, 32), False, False)
-                 for r in range(16)]
-                + [(z, win("ZT", r, r), V("EQ", c0 + r, c0 + 128, 16), False, r == 15) for r in range(16)])
-            for u in range(2):
-                ts(V("OC", 8 * h + u, 8 * (h + 1), 2), V("P5", 8 * h + u, 8 * (h + 1), 2), 31.0, Alu.add,
-                   V("PF", 1 + 3 * u, 2 + 3 * u), Alu.max)
-            act(half("VAL", h), X(V("L"), V("OC", 8 * h, 8 * (h + 1))))
-
-        def forward(h):
+                group(listed(V("P2", 64, 64 + 16 * t), "ZF", F1, W0, wt))
+            cp(V("FL", 0, nb // 16 + 16 * t), V("P2", 0, nb // 16 + 16 * t))
+            for a in range(0, nb // 16, 32):
+                b = min(a + 32, nb // 16)
+                lin(V(F2, 16 * a, 16 * b), X(fp, V("FL", a, b)))
             if t > 0:
-                act(half("EF", h), X(V(F, 0, wt), V("LU", 40 * h + 16, 40 * h + 24)))
-                return
-            tt(half("DF", h), X(V(F, 0, wt), V("LU", 40 * h + 16, 40 * h + 24)), half("FV", h), Alu.subtract)
-            tt(half("EF", h), oh(h, 1), half("DF", h), Alu.mult)
+                lin(V(F2, W0, wt), X(fp, V("FL", 64, 64 + 16 * t)))
+        if not TWICE:
+            squares()
 
-        early = []
-        links(0)
-        if t > 0:
-            act(V("OWN"), X(V("Y", 0, wt), V("VU")))
-        for h in range(2):
-            mm(V("P7", 128 * h, 128 * (h + 1)), half(own, h), V("NI"))
         if not last:
-            mm(V("P7", S, 2 * S), V("BO"), V(own, 0, S))
-        act(V("OT"), V("P7", 0, S))
-        if not last:
-            act(V("U"), V("P7", S, 2 * S), bias=float(t + 1))
-        if t == 0:
-            late_a()
-        links(1)
-        lists(0)
-        first_list = len(ops) - 3
-        ga(0)
-        ga(1)
-        for fn in pend:
-            fn()
-        pend = []
-        gb(0)
-        links(2)
-        ops[-1]["hint"] = [first_list]
-        lists(1)
-        ab(0)
-        ga(2)
-        gb(1)
-        ga(3)
-        ab(1)
-        gb(2)
-        links(3)
-        lists(2)
-        lists(3)
-        ab(2)
-        ga(4)
-        gb(3)
-        if t == 0:
-            late_b()
-        ts(V("A1"), a32, 1.0, Alu.add)
-        ga(5)
-        ab(3)
-        keys(0)
-        gb(4)
-        ga(6)
-        ab(4)
-        if t == 0:
-            late_c()
-        gb(5)
-        choose(0)
-        ga(7)
-        ab(5)
-        gb(6)
-        ab(6)
-        gb(7)
-        ab(7)
-        keys(1)
-        picks_q(0)
-        picks_p(0)
-        early = range(len(ops) - (5 if t == 0 else 6), len(ops))
-        take = lists_of(0, "P5", 0, 6, 1)
-        mms([(half("P5", u), V("BO"), half("PR", 0), True, True) for u in (1, 2)])
-        take()
-        act(V("AL", 0, 8), V("P5", 0, 8))
-        act(V("AR", 0, S), V("P5", 128, 384))
-        state_q(0)
-        state_p(0)
-        forward(0)
-        claims(0)
+            if t == 0:
+                group([(V("P7", r, S, 16), win("ZD", r, 2), V("NR")) for r in range(16)])
+                lin(V("MR"), V("P7", 0, S), V("CT", 11, 12), V("CT", 12, 13))
+            else:
+                tt(V("AD"), V("NR"), V("NB"), Alu.mult)
+                group([(V("P7", r, S, 16), win("ZD", r, 2), V("AD")) for r in range(16)])
+                lin(V("MR"), V("P7", 0, S), bias=V("CT", 13, 14))
+            if TWICE:
+                for c0, c1 in parts:
+                    lin(V("W1", 16 * c0, 16 * c1), X(V(F1, 0, wt), V("LL", 4 * c0, 3 * c0 + c1)))
+                group(listed(V("P5", 0, 16), "ZF", "W1", 0, S))
+                cp(V("WU"), V("P5", 0, 16))
+                tt(V("PW"), X(V(F1, 0, wt), V("WU")), V("MR"), Alu.mult)
+            else:
+                for c0, c1 in parts:
+                    tt(V("PW", 16 * c0, 16 * c1), X(V(F2, 0, wt), V("LL", 4 * c0, 3 * c0 + c1)), V("MR", 16 * c0, 16 * c1), Alu.mult)
+            v = V("P5", 0, 16)
+            group([(v, V("ID"), V("LI"))] + listed(v, "ZV", "PW", 0, S))
+            cp(V("VU"), v)
+            if DIRECT:
+                cp(V("AU"), X(V("C", 0, wt + S), V("VU")))
+                move(V("A32"), V("AU"))
+            else:
+                ts(V("A32"), X(V("C", 0, wt + S), V("VU")), NA - 1, Alu.bitwise_and)
+                cp(V("AU"), V("A32"))
+            lin(V("VA", 0, 16), v, bias=1.5 * 2 ** 15 - 127.5)
+            lin(V("VS"), V("VA", 0, 16), bias=-(1.5 * 2 ** 15 + wt + S))
+            if t == 0:
+                move(V("C", wt + S, wt + 2 * S), V("A32"))
+                lin(V("VA", 16, 32), v, bias=1.5 * 2 ** 17 + S - 511.5)
+                lin(V("VA", 32, 48), V("VA", 16, 32), bias=-(1.5 * 2 ** 17 + S))
+                tt(V("NB"), V("VS"), V("VA", 32, 48), Alu.subtract)
+            group([(V("P4", 0, 16), V("BO"), V("NR"))])
+            act(V("JK"), V("P4", 0, 16), bias=7.5 / 16, total=V("AI", 0, 1))
+            act(V("AI", 1, 2), V("AI", 0, 1), bias=MAGIC, scale=1.0 / 16)
+            act(V("AI", 2, 3), V("AI", 1, 2), bias=16 * KEY * MAGIC, scale=-16 * KEY)
+            act(V("AI", 3, 4), V("AI", 0, 1), bias=V("AI", 2, 3), scale=KEY)
+            lin(V("LIM"), V("LI0"), bias=V("AI", 3, 4))
+        if TWICE:
+            squares()
 
-        choose(1)
-        picks_q(1)
-        take = lists_of(1, "P2", 3, 6, 0)
-        picks_p(1)
-        take_p = lists_of(1, "P3", 0, 3, 1)
-        mms([(half("P3", u), V("BO"), half("PR", 0, 768), True, True) for u in (1, 2)])
-        take()
-        state_q(1)
-        n_new = len(ops) - 1
-        send(t)
-        forward(1)
-        take_p()
-        act(V("AL", 8, 16), V("P3", 0, 8))
-        act(V("AR", S, 2 * S), V("P3", 128, 384))
-        n_ar = len(ops) - 1
-        claims(1)
-        n_val = len(ops) - 1
-        if t == 0:
-            tt(V(F, 0, S), V("EF"), fv, Alu.add)
+        if not last:
+            move(V(F2, W + t * GH, W + (t + 1) * GH), V(F2, M, W0))
+            group(listed(V("P4", 0, wt // 16), "ZY%d" % t, F2, 0, wt))
+            cp(V("FY", 0, wt // 16), V("P4", 0, wt // 16))
+            top = wt // 16
+            for a in range(0, top, top // 4):
+                lin(V("YF", 16 * a, 16 * a + 4 * top), X(V("Y", 0, W + (t + 1) * GH), V("FY", a, a + top // 4)),
+                    pre=[("arr%d" % t, nsig)])
         else:
-            for h in range(2):
-                cp(X(V(F), V("LU", 40 * h + 32, 40 * h + 40)), half("EF", h))
-        if last and HINT:
-            ops[-1]["hint"] = [n_val - 4]
-        new = V("NEW", t * S, (t + 1) * S)
-        nb = S if t == 0 else M
-        to_list(V("P2", 0, nb // 16), "ZF", F, 0, nb)
-        if t > 0:
-            to_list(V("P2", 64, 64 + 16 * t), "ZF", F, W0, wt)
-        act(V(F2, M, W0), X(V(F, 0, wt), V("FL", 64, 112)))
-        cp(V("FL", 0, nb // 16), V("P2", 0, nb // 16))
-        if t > 0:
-            cp(V("FL", 112, 112 + 16 * t), V("P2", 64, 64 + 16 * t))
-        act(V(F2, 0, M), X(V(F, 0, wt), V("FL", 0, 64)))
-        if last:
-            ops[-1]["hint"] = [n_val]
-        elif t > 0:
-            act(V(F2, W0, wt), X(V(F, 0, wt), V("FL", 112, 112 + 16 * t)))
-
-        def f2room():
-            (cp if F2_DVE else act)(V(F2, W0, wt), X(V(F, 0, wt), V("FL", 112, 112 + 16 * t)))
-            if F2_DVE:
-                ops[-1]["hint"] = [n_link]
-
-        def ys():
-            if t == 0:
-                move(V("Y", 0, S), new)
-            else:
-                cp(X(V("Y", 0, wt), V("VU")), new)
-                if last and HINT:
-                    ops[-1]["hint"] = [n_link]
-
-        def room():
             n0 = len(ops)
-            state_p(1)
-            if last:
-                ops[n0]["hint"] = [n_ar]
-
-        def f2list(bank, a, b):
-            to_list(V(bank, a // 16, b // 16), "ZF", F2, a, b)
-
-        def c1():
-            for h in range(2):
-                tt(half("PC", h), oh(h, 2), half("U", h), Alu.mult)
-
-        def c2():
-            tt(V("C", 0, S) if t == 0 else V("CN"), V("PC"), a32, Alu.add)
-
-        def c3():
-            if t > 0:
-                cp(X(V("C", 0, wt), V("VU")), V("CN"))
-
-        def m1():
-            if t == 0:
-                for h in range(2):
-                    act(half("MR", h), oh(h, 1), bias=V("CT", 11, 12), scale=V("CT", 10, 11))
-            else:
-                for h in range(2):
-                    tt(half("MT", h), oh(h, 1), half("X1", h), Alu.mult)
-                act(V("MR"), V("MT"), bias=V("CT", 13, 14))
-
-        def l1():
-            to_list(V("P2", M // 16, wt // 16), "ZY%d" % t, F2, M, wt)
-            cp(V("FY", M // 16, wt // 16), V("P2", M // 16, wt // 16))
-
-        def l2():
-            to_list(V("P3", 0, 64), "ZY%d" % t, F2, 0, M)
-            cp(V("FY", 0, 64), V("P3", 0, 64))
-
-        def l3():
-            f2list("P2", M, W0)
-            cp(V("FL", 64, 112), V("P2", 64, 112))
-
-        def yf():
-            act(V("YF", 0, wt + S), X(V("Y", 0, W + (t + 1) * GH), V("FY", 0, 112 + 16 * (t + 1))), scale=0.5,
-                pre=[("arr%d" % t, nsig)])
-
-        def w1():
-            for h in range(2):
-                tt(half("PW", h), X(V(F2, 0, wt), V("LU", 40 * h, 40 * h + 8)), half("MR", h), Alu.mult)
-            mm(V("P6", 0, 16), V("ID"), V("LI"), True, False)
-            to_list(V("P6", 0, 16), "ZV", "PW", 0, S, first=False)
-            if t == 0:
-                mm(V("P7", 0, S), win("ZX", 0, 2), V("PW"))
-            mm(V("P7", S, 2 * S), V("BV"), V("PW"))
-            act(V("VB"), V("P7", S, 2 * S), bias=-W / 16.0)
-
-        def w2():
-            cp(V("VU"), V("P6", 0, 16))
-
-        def w3():
-            ts(V("A32"), X(V("C", 0, wt + S), V("VU")), NA - 1, Alu.bitwise_and)
-
-        def w4():
-            cp(V("AU"), V("A32"))
-            if t == 0:
-                dma("sp", V("C", wt + S, wt + 2 * S), V("A32"))
-
-        def count():
-            group(V("P7", 0, 128), nrs() + [(V("C128"), V("K0"))])
-            act(V("AI"), V("P7", 0, 128), bias=MAGIC + 16.0, scale=-1.0 / 256)
-            act(V("AJ"), V("AI"), bias=-256.0 * MAGIC - 4096.0, scale=256.0)
-            for h in range(2):
-                keys0(h, nrs() + [(V("C128"), V("AJ"))])
-
-        def x1():
-            act(V("X1"), V("P7", 0, S), bias=V("CT", 12, 13))
-
-        def out_y():
-            dma("act", H(T.yo[:, W0:W]), V("Y", W0, W))
-            dma("act", H(T.yo[:, 0:M]), V("Y", 0, M))
-
-        def out_f():
-            f2list("P7", 0, M)
-            f2list("P7", M, wt)
-            act(V("FO", 0, wt // 16), V("P7", 0, wt // 16))
-            dma("act", H(T.fo[:, :]), V("FO"))
-
-        if last:
-            between = {}
-            after = [lambda: dma("sp", H(T.lo[1:128:2, :]), V("L", 32, 32 + NA, p=(1, 128, 2))), f2room, room, ys, out_y, out_f,
-                     lambda: dma("sp", H(T.yo[:, M:W0]), V("Y", W + t * GH, W + (t + 1) * GH),
-                                 pre=[("arr%d" % t, nsig)])]
-        else:
-            between = {15: [ys, room], 14: [m1], 13: [l1], 12: [c1], 11: [l2], 10: [c2], 9: [w1, yf, l3], 8: [c3], 7: [w2],
-                       6: [w3], 5: [w4]}
-            after = []
-            pend = [count]
-        for c in range(7, -1, -1):
-            tt(X(V("L"), V("OC", 2 * c, 2 * c + 2)), V("VAL", 32 * c, 32 * (c + 1)),
-               V("NR", t * S + 32 * c, t * S + 32 * (c + 1)), Alu.max)
-        n_link = len(ops) - 1
-        for c in range(15, -1, -1):
-            for fn in between.get(c, ()):
-                fn()
-        if t == 0:
-            x1()
-        n0 = len(ops)
-        for fn in after:
-            fn()
-        for o in ops[n0:]:
-            o["end"] = True
+            dma(BOTH, H(T.lo[1:128:2, :]), V("L", 32, 32 + NA, p=(1, 128, 2)))
+            dma(BOTH, H(T.yo[:, W0:W]), V("Y", W0, W))
+            dma(BOTH, H(T.yo[:, 0:M]), V("Y", 0, M))
+            group(listed(V("P7", M // 16, wt // 16), "ZF", F2, M, wt))
+            group(listed(V("P7", 0, M // 16), "ZF", F2, 0, M))
+            lin(V("FO", 0, wt // 16), V("P7", 0, wt // 16))
+            dma(BOTH, H(T.fo[:, :]), V("FO"))
+            dma(BOTH, H(T.yo[:, M:W0]), V("Y", W + t * GH, W + (t + 1) * GH), pre=[("arr%d" % t, nsig)])
+            for o in ops[n0:]:
+                o["end"] = True
 
     seen, sends, lastdma = {}, {}, {}
     for n, o in enumerate(ops):
-        e = o["e"]
-        deps, order = set(), set()
+        deps, near, order = set(), set(), set()
         for kind, regs in (("r", o["r"]), ("w", o["w"])):
             for name, a, b in regs:
                 psum = name[0] == "P" and name[1:].isdigit()
                 for m, k2, a2, b2 in seen.get(name, ()):
                     if a2 < b and a < b2 and m != n:
-                        same = ops[m]["e"] == e and not ops[m]["dma"]
-                        if same and e == "pe":
+                        if "pe" in o["fns"] and "pe" in ops[m]["fns"]:
                             if psum:
                                 order.add(m)
-                        elif kind == "w" or k2 == "w" or (psum and not same):
+                        elif kind == "w" and INORDER and not (o["dma"] or ops[m]["dma"] or "send" in ops[m]):
+                            near.add(m)
+                        elif kind == "w" or k2 == "w":
                             deps.add(m)
+                        elif psum:
+                            near.add(m)
         for kind, regs in (("r", o["r"]), ("w", o["w"])):
             for name, a, b in regs:
                 lst = seen.setdefault(name, [])
@@ -930,15 +814,19 @@ def rank_program(g, core, T, topo):
             sends[o["send"]] = n
         late = {sends[name] for name, v in o["pre"]}
         if o["dma"] and not o["r"]:
-            order |= {lastdma[e]} if e in lastdma else set()
-            lastdma[e] = n
-        o["deps"], o["order"], o["late"] = deps, order | set(o.get("hint", ())), late
+            order |= set(lastdma.values())
+            lastdma["load"] = n
+        o["deps"], o["near"], o["order"], o["late"] = deps, near - deps, order, late
 
     if "seq" not in PLAN:
-        names = sorted(Q)
-        PLAN["seq"] = arrange([o["c"][0] for o in ops], [o["c"][1] for o in ops], [names.index(o["e"]) for o in ops],
-                              [sorted(o["deps"] | o["late"]) for o in ops], [sorted(o["order"]) for o in ops])
-    seq = PLAN["seq"]
+        PLAN["seq"] = arrange([o["ways"] for o in ops], [sorted(o["deps"] | o["late"]) for o in ops],
+                              [sorted(o["near"]) for o in ops], [sorted(o["order"]) for o in ops],
+                              [o.get("lead", 0.0) for o in ops])
+    seq, on = PLAN["seq"]
+    for o, q in zip(ops, on):
+        o["e"] = QUEUES[q]
+    for o in ops:
+        o["deps"] = o["deps"] | {m for m in o["near"] if ops[m]["e"] != o["e"]}
     place = {n: k for k, n in enumerate(seq)}
     ops = [ops[n] for n in seq]
 
@@ -968,14 +856,16 @@ def rank_program(g, core, T, topo):
         ck = dict(known[e])
         ck[o["key"]] = n
         clock.append(ck)
-    value, count_of, left = {}, {}, []
+    value, count_of, left, arrived = {}, {}, [], set()
     for n, o in enumerate(ops):
         q = Q[o["e"]]
         for m in waits[n]:
             q.wait_ge(T.sem[ops[m]["key"]], value[m])
         for name, v in o["pre"]:
-            q.wait_ge(T.sem[name], v)
-        ins = o["fn"]()
+            if (o["e"], name) not in arrived:
+                arrived.add((o["e"], name))
+                q.wait_ge(T.sem[name], v)
+        ins = o["fns"][o["e"]]()
         if o["dma"]:
             ins.then_inc(T.sem[o["key"]], 16)
             value[n] = 16
@@ -985,6 +875,6 @@ def rank_program(g, core, T, topo):
             count_of[o["key"]] = count_of.get(o["key"], 0) + 1
             value[n] = count_of[o["key"]]
             ins.then_inc(T.sem[o["key"]], 1)
-    g.wait_ge(T.sem.sent, RO * nloc)
+    g.wait_ge(T.sem.sent, nloc * sum("send" in o for o in ops))
     for key in sorted(set(left)):
         g.wait_ge(T.sem[key], 16 * left.count(key))

from concourse.bass import DstId, RemoteDMATransfer
from concourse.mybir import AluOpType as Alu, ActivationFunctionType as Act

N, S, M, NA, RO = 4, 256, 1024, 2048, 3
W0 = M + (N - 1) * S
W = W0 + RO * S
GH = (N - 1) * S
MAGIC = 12582912.0
OFS = 1280.0
KEY = 4096.0

f32, b16, h16, i32, u16 = "float32", "bfloat16", "float16", "int32", "uint16"
SB = {
    "LK": (NA, i32), "L": (32 + NA, f32), "C": (W0 + 2 * S, i32), "Y": (W + RO * GH, b16), "YF": (W0 + 2 * S, b16),
    "FS": (W + 2 * GH, b16), "FP": (W + GH, b16), "FW": (112, i32), "FL": (144, u16), "FY": (144, u16), "FO": (160, f32),
    "TH": (S, i32), "TF": (S, h16), "G": (4096, h16), "GA": (4096, b16), "GB": (4096, b16), "AB": (4096, b16),
    "A32": (S, i32), "AU": (S, u16), "BC": (2 * S, u16), "B32": (S, f32), "OWN": (S, b16), "OT": (384, b16), "U": (S, f32),
    "SC": (2 * S, f32), "MI": (32, i32), "JI": (32, i32), "JU": (32, u16), "NR": (16, b16), "NV": (16, b16), "VS": (16, b16),
    "NB": (16, b16), "NH": (16, h16), "AD": (16, b16), "PR": (3 * S, h16), "LQ": (32, u16), "LP": (32, u16), "PQ": (4 * S, b16), "SG": (S, b16),
    "NEW": (RO * S, b16), "EF": (S, b16), "AT": (S, h16), "EQ": (384, b16), "EA": (384, b16), "OC": (32, u16), "VAL": (S, f32),
    "NW": (RO * S, f32), "PC": (S, f32), "CN": (S, i32), "MR": (S, b16), "W1": (S, b16), "WU": (16, u16), "PW": (S, b16),
    "VU": (16, u16), "LIM": (16, f32), "LI0": (16, f32), "AI": (4, f32),
    "ONE": (128, b16), "ID": (128, b16), "NI": (128, b16), "IE": (128, h16), "N4": (128, b16), "BO": (128, b16),
    "MG": (S, b16), "KA": (16, h16), "E2": (128, b16), "GX": (144, b16), "KR": (512, b16), "PG": (1, b16), "OB": (4, f32),
    "ZP": (2064, b16), "Z5": (128, b16), "CK": (S, f32), "ZD": (2064, b16), "ZE": (144, b16), "ZK": (144, b16), "ZB": (144, b16), "ZF": (144, b16), "ZV": (144, b16),
    "ZG": (288, b16), "ZY0": (144, b16), "ZY1": (144, b16), "R": (1536, b16), "EYE": (4096, b16), "KI": (S, b16), "TRI": (S, b16),
    "RP": (S, b16), "RQ": (S, b16), "XJ": (16, f32), "IDL": (160, f32), "LI": (16, b16), "LJ": (48, h16), "PF": (4, b16),
    "HF": (56, b16), "HG": (64, b16), "CT": (18, f32), "LO": (S, b16), "VA": (48, b16), "JK": (16, f32), "LL": (64, u16),
}
SCRATCH = {k: ("sbuf", [128, v[0]], v[1]) for k, v in SB.items()}
SCRATCH["AB"] = ("sbuf", [128, 16, S], b16)
for _k in range(8):
    SCRATCH["P%d" % _k] = ("psum", [128, 512], f32)

PARTS = [[(0, 16)]] * RO
LINKS = [(192, 256), (128, 192), (64, 128), (0, 64)]
PICKS = [(192, 256), (128, 192), (64, 128), (0, 64)]
STATES = [(192, 256), (128, 192), (64, 128), (32, 64), (0, 32)]
SUMS = [(14, 16), (12, 14), (10, 12), (8, 10), (6, 8), (4, 6), (2, 4), (0, 2)]
KEYS, SCANS = [(12, 16), (8, 12), (4, 8), (0, 4)], 4
TWICE = True
MERGE, QFIRST, DIRECT = True, (0, 0, 0), True
PAIRS = 1
PACKED = True
INORDER = False
APART = False
EQ_ACT = (False, True, False)
LOADS, LEAD = ("FW", "C", "TH", "LK", "Y"), 20000.0
BOTH = ("sp", "act")
GUESS = [dict(cyc=0.95, gath=1.45, scat=3.5, pe=0.48, dma=0.004, rem=4500.0, hop=80.0),
         dict(cyc=1.0, gath=1.1, scat=4.5, pe=0.58, dma=0.004, rem=3000.0, hop=100.0),
         dict(cyc=1.15, gath=2.2, scat=4.5, pe=0.56, dma=0.004, rem=3500.0, hop=70.0)]
FIX = {"dve": 50.0, "act": 65.0, "pe": 30.0, "pool": 0.0, "sp": 0.0}
DMA_FIX, ISSUE, COOL, REFIT = 2000.0, 1000.0, 1.0, 8
LEAN, HEAT, SEEDS, PASSES, WINDOW, MOVES = 0.6, 0.012, (1, 2, 3, 4, 5, 6), 4, 80, 2500
PLAN = {}
NDMA = 30
QUEUES = ("act", "dve", "pe", "pool", "sp")


def arrange(ways, before, near, after, lead):
    n_ops, models = len(ways), range(len(GUESS))
    cost = [[{QUEUES.index(q): size * G[kind] + FIX[q] * (kind not in ("dma", "rem")) for q, kind, size in ways[n]}
             for n in range(n_ops)] for G in GUESS]
    queue = [[QUEUES.index(q) for q, kind, size in ways[n]] for n in range(n_ops)]
    code = [{"dma": 1, "rem": 2}.get(ways[n][0][1], 0) for n in range(n_ops)]
    loose = [sorted(set(near[n]) | set(after[n])) for n in range(n_ops)]
    pred = [sorted(set(before[n]) | set(loose[n])) for n in range(n_ops)]
    succ = [[] for n in range(n_ops)]
    for n in range(n_ops):
        for m in pred[n]:
            succ[m].append(n)

    def run(j, part, on, done, fin, free):
        c, hop = cost[j], GUESS[j]["hop"]
        for n in part:
            q = on[n]
            s = free[q]
            for m in before[n]:
                if done[m] > s:
                    s = done[m]
            for m in near[n]:
                if done[m] > s and on[m] != q:
                    s = done[m]
            if code[n] == 0:
                s += c[n][q]
                done[n] = s + hop
            elif code[n] == 1:
                free[5] = max(free[5], s + 0.7 * DMA_FIX) + c[n][q]
                done[n] = free[5] + 0.3 * DMA_FIX + hop
                s += 60.0
            else:
                free[5] = max(free[5], s + 0.7 * DMA_FIX) + c[n][q]
                done[n] = free[5] + 0.3 * DMA_FIX + hop
                s += ISSUE
            free[q] = fin[n] = s

    def tails(j, part, on):
        c, hop = cost[j], GUESS[j]["hop"]
        tail, free = {}, [0.0] * 6
        for n in reversed(part):
            q = on[n]
            behind = hop + max([tail[m] for m in succ[n] if n in before[m] or (n in near[m] and on[m] != q)], default=0.0)
            if code[n] == 0:
                free[q] = c[n][q] + max(behind, free[q])
            else:
                free[5] = c[n][q] + max(0.3 * DMA_FIX + behind, free[5])
                free[q] = max((60.0 if code[n] == 1 else ISSUE) + free[q], 0.7 * DMA_FIX + free[5])
            tail[n] = free[q]
        return tail, free

    def whole(seq, on):
        times = [([0.0] * n_ops, [0.0] * n_ops) for j in models]
        for j in models:
            run(j, seq, on, times[j][0], times[j][1], [0.0] * 6)
        return times

    def pack(order, on):
        c, hop = cost[0], GUESS[0]["hop"]
        line, first, done, dfree = [[] for q in range(5)], [0.0] * n_ops, [0.0] * n_ops, 0.0
        for n in order:
            s0 = max([done[m] for m in before[n]], default=0.0)
            best = None
            for q in queue[n]:
                s = max([s0] + [first[m] + 60.0 if code[m] else done[m] - hop * (on[m] == q) for m in loose[n]])
                b = c[n][q] if code[n] == 0 else 60.0 if code[n] == 1 else ISSUE
                ln = line[q]
                k = top = len(ln)
                while k and ln[k - 1][1] > s:
                    k -= 1
                while k < top and s + b > ln[k][0]:
                    s = max(s, ln[k][1])
                    k += 1
                if best is None or s + b < best[0]:
                    best = (s + b, s, q, k)
            e, s, q, k = best
            on[n] = q
            line[q].insert(k, (s, e))
            first[n] = s
            if code[n] == 0:
                done[n] = e + hop
            elif code[n] == 1:
                dfree = max(dfree, s + 0.7 * DMA_FIX) + c[n][q]
                done[n] = dfree + 0.3 * DMA_FIX + hop
            else:
                done[n] = s + c[n][q] + hop
        return first

    def rank_by(key):
        key = list(key)
        for n in range(n_ops):
            for m in pred[n]:
                if key[m] >= key[n]:
                    key[n] = key[m] + 0.001
        return sorted(range(n_ops), key=lambda n: key[n])

    def moved(seq, a, b, ahead):
        part, take = seq[a:b + 1], {seq[b] if ahead else seq[a]}
        for n in (part[::-1] if ahead else part):
            if n in take:
                take.update(pred[n] if ahead else succ[n])
        if (seq[a] if ahead else seq[b]) in take:
            return None
        one, two = [n for n in part if n in take], [n for n in part if n not in take]
        return seq[:a] + (one + two if ahead else two + one) + seq[b + 1:]

    rest = [0.0] * n_ops
    for n in range(n_ops - 1, -1, -1):
        rest[n] = (min(cost[0][n].values()) + DMA_FIX * (code[n] == 1) + lead[n]
                   + max([rest[m] + GUESS[0]["hop"] for m in succ[n]], default=0.0))
    on0 = [0] * n_ops
    seq0 = rank_by(pack(rank_by([-x for x in rest]), on0))
    unit = [max(x[0]) for x in whole(seq0, on0)]

    def stretch(seq, on, p0, heat, seed):
        times = whole(seq, on)
        seq = rank_by([times[0][1][n] - (cost[0][n][on[n]] if code[n] == 0 else 60.0 if code[n] == 1 else ISSUE)
                       for n in range(n_ops)])
        p0, p1 = max(p0, 0), min(p0 + WINDOW, n_ops)
        part, free0, ext, base, queue_tail = seq[p0:p1], [], [], [], []
        for j in models:
            free0.append([0.0] * 6)
            run(j, seq[:p0], on, times[j][0], times[j][1], free0[j])
            tail, free = tails(j, seq[p1:], on)
            ext.append({n: max([tail[m] for m in succ[n] if m in tail], default=0.0) for n in seq[:p1]})
            base.append(max([times[j][0][n] + ext[j][n] for n in seq[:p0]], default=0.0))
            queue_tail.append(free)

        def worth(part, on, a, old):
            last = {on[n]: n for n in part[:a]}
            dmas = [n for n in part[:a] if code[n]]
            w, new, behind = 0.0, [], part[a:]
            for j in models:
                done, fin, free, e = list(old[j][0]), list(old[j][1]), list(free0[j]), ext[j]
                for q, n in last.items():
                    free[q] = fin[n]
                if dmas:
                    free[5] = done[dmas[-1]] - 0.3 * DMA_FIX - GUESS[j]["hop"]
                run(j, behind, on, done, fin, free)
                ends = [done[n] + e[n] for n in part]
                end = max(max(ends), base[j], max(x + y for x, y in zip(free, queue_tail[j])))
                w += (end + LEAN * (sum(ends) / len(ends) + sum(free[:3]) / 3)) / unit[j]
                new.append((done, fin))
            return w, new

        def refit(part, on, a, old):
            c, hop, done, first = cost[0], GUESS[0]["hop"], list(old[0]), {}
            free = list(free0[0])
            for n in part[:a]:
                free[on[n]] = old[1][n]
            line = [[(0.0, f)] for f in free]
            for n in part[a:]:
                q = on[n]
                s = 0.0
                for m in before[n]:
                    if done[m] > s:
                        s = done[m]
                for m in loose[n]:
                    d = done[m] if on[m] != q else first.get(m, 0.0) + 1.0
                    if d > s:
                        s = d
                b = c[n][q] if code[n] == 0 else 60.0 if code[n] == 1 else ISSUE
                ln = line[q]
                k = top = len(ln)
                while ln[k - 1][1] > s and k > 1:
                    k -= 1
                s = max(s, ln[k - 1][1])
                while k < top and s + b > ln[k][0]:
                    s = ln[k][1]
                    k += 1
                ln.insert(k, (s, s + b))
                first[n] = s
                done[n] = s + b + hop if code[n] == 0 else s + DMA_FIX + c[n][q] + hop
            return part[:a] + sorted(part[a:], key=lambda n: first[n])
        now, cur = worth(part, on, 0, times)
        best, keep = now, (part, on)
        for step in range(MOVES):
            seed = (seed * 6364136223846793005 + 1442695040888963407) % 2 ** 64
            a = b = 1 + (seed >> 33) % (len(part) - 1)
            n = part[b]
            kind, cand, other = (seed >> 20) % 4, part, on
            if kind >= 2 and len(queue[n]) > 1:
                other = list(on)
                other[n] = sum(queue[n]) - on[n]
                swap = [k for k in range(max(0, b - 20), min(b + 20, len(part)))
                        if on[part[k]] == other[n] and on[n] in queue[part[k]]]
                if kind == 3 and swap:
                    k = swap[(seed >> 45) % len(swap)]
                    other[part[k]] = on[n]
                    a = min(a, k)
            if other is on or (seed >> 26) & 1:
                mine = [k for k in range(max(0, b - 40), b) if other[part[k]] == other[n]][-1 - (seed >> 28) % 4:]
                if mine:
                    cand = moved(part, mine[0], b, (seed >> 27) & 1)
                    a = min(a, mine[0])
                if cand is None or (cand is part and other is on):
                    continue
            if (seed >> 12) % 16 < REFIT:
                cand = refit(cand, other, a, cur[0])
            w, new = worth(cand, other, a, cur)
            if w <= now + heat * (1.0 - step / MOVES) * ((seed >> 50) & 15) / 15.0:
                now, part, on, cur = w, cand, other, new
                if w < best:
                    best, keep = w, (part, on)
        return seq[:p0] + keep[0] + seq[p1:], keep[1]

    found = []
    for seed in SEEDS:
        seq, on = seq0, on0
        for turn in range(PASSES):
            for p0 in range(-((turn * 17) % (WINDOW // 2)), n_ops - WINDOW // 2, WINDOW // 2):
                seq, on = stretch(seq, on, p0, HEAT * (1.0 - COOL * turn / PASSES), 1000003 * seed + 1009 * turn + p0 + WINDOW)
        found.append((sum(max(x[0]) / u for x, u in zip(whole(seq, on), unit)), seq, on))
    return min(found)[1:]


SEMAPHORES = ["pe", "dve", "act", "pool", "sent", "out"] + ["arr%d" % t for t in range(RO)] + ["d%d" % k for k in range(NDMA)]


def rank_program(g, core, T, topo):
    rank = T.rank_of(core)
    if rank is None:
        return
    Q = {"pe": g.tensor, "dve": g.vector, "act": g.scalar, "pool": g, "sp": g.sync}
    ops = []

    def V(name, a=0, b=None, s=1, p=None):
        if b is None:
            b = T[name].shape[1]
        ap = T[name][:, a:b:s] if p is None else T[name][p[0]:p[1]:p[2], a:b:s]
        n = len(range(a, b, s))
        if name[0] == "P" and name[1:].isdigit():
            return (ap, [(name, 0, 512)], [], n, 4, "p")
        rows = 128 if p is None else len(range(*p))
        return (ap, [(name, a, b)], [], n, 4 if SB[name][1] in (f32, i32) else 2, "s", rows)

    def AB(c0, c1, a=0, b=S):
        return (T.AB[:, c0:c1, a:b], [("AB", S * c0, S * c1)], [], (c1 - c0) * (b - a), 2, "s", 128)

    def X(win, off):
        return (win[0].indirect(off[0]), win[1], off[1], 16 * off[3], win[4], "x")

    def H(ap):
        return (ap, [], [], 0, 4, "h")

    def size(eng, out, ins, dma, per):
        n = out[3]
        wide = [x for x in ins + [out] if x[3] == n]
        if dma:
            side = out if out[5] == "s" else ins[0]
            return ("dma", side[3] * side[4] * side[6])
        if eng == "pool":
            return ("cyc", 170 + 2 * n)
        if out[5] == "x":
            return ("scat", n)
        if any(x[5] == "x" for x in ins):
            return ("gath", n)
        if eng == "act":
            return ("cyc", n)
        if not all(x[5] == "s" for x in ins if x[3] == n):
            per = 1.0
        return ("cyc", max(64, n * per * (0.5 if all(x[4] == 2 for x in wide) else 1.0)))

    def op(fns, out, ins, dma=False, pre=(), cost=None, per=1.0):
        rd = list(out[2])
        ins = [x for x in ins if isinstance(x, tuple)]
        for x in ins:
            rd += x[1] + x[2]
        ways = [(e,) + (cost or size(e, out, ins, dma, per)) for e in fns]
        ops.append({"fns": fns, "ways": ways, "w": out[1], "r": rd, "dma": dma, "pre": pre})

    def a_(x):
        return x[0] if isinstance(x, tuple) else x

    def mms(items):
        def fn():
            for o, l, r, st, sp in items:
                ins = g.tensor.matmul(o[0], l[0], r[0], st, sp)
            return ins
        op({"pe": fn}, items[0][0], [x for it in items for x in it[1:3]],
           cost=("pe", sum(max(min(64, l[3]), r[3]) for o, l, r, st, sp in items)))

    def group(items, first=True, stop=True):
        mms([(o, l, r, first and n == 0, stop and n == len(items) - 1) for n, (o, l, r) in enumerate(items)])

    def act(o, i, f=Act.Identity, bias=0.0, scale=1.0, total=None):
        op({"act": lambda: g.scalar.activation(o[0], i[0], f, bias=a_(bias), scale=a_(scale), accum_out=a_(total))},
           o, [i, bias, scale])
        if total:
            ops[-1]["w"] = o[1] + total[1]

    def lin(o, i, scale=None, bias=None, pre=()):
        def vec():
            if scale is None and bias is None:
                return g.vector.tensor_copy(o[0], i[0])
            if bias is None:
                return g.vector.tensor_scalar(o[0], i[0], a_(scale), None, Alu.mult)
            if scale is None:
                return g.vector.tensor_scalar(o[0], i[0], a_(bias), None, Alu.add)
            return g.vector.tensor_scalar(o[0], i[0], a_(scale), a_(bias), Alu.mult, Alu.add)

        def sca():
            return g.scalar.activation(o[0], i[0], Act.Identity, bias=0.0 if bias is None else a_(bias),
                                       scale=1.0 if scale is None else a_(scale))
        op({"act": sca, "dve": vec}, o, [i, bias, scale], pre=pre)

    def cp(o, i):
        op({"dve": lambda: g.vector.tensor_copy(o[0], i[0])}, o, [i])

    def tt(o, x, y, f):
        op({"dve": lambda: g.vector.tensor_tensor(o[0], x[0], y[0], f)}, o, [x, y], per=2.0)

    def ts(o, x, s1, f0, s2=None, f1=None):
        if f1 is None:
            op({"dve": lambda: g.vector.tensor_scalar(o[0], x[0], a_(s1), None, f0)}, o, [x, s1])
        else:
            op({"dve": lambda: g.vector.tensor_scalar(o[0], x[0], a_(s1), a_(s2), f0, f1)}, o, [x, s1, s2])

    def scan(o, d0, d1, f):
        op({"dve": lambda: g.vector.tensor_tensor_scan(o[0], d0[0], d1[0], 0.0, Alu.add, f)}, o, [d0, d1])

    def ms(o, c):
        op({"dve": lambda: g.vector.memset(o[0], c)}, o, [])

    def iota(o, pat, base=0, cm=0):
        op({"pool": lambda: g.iota(o[0], pat, base, cm, allow_small_or_imprecise_dtypes=True)}, o, [])

    def fill(o, c):
        if SB[o[1][0][0]][1] == i32:
            fns = {"pool": lambda: g.iota(o[0], [[0, o[3]]], c, 0)}
        else:
            fns = {"pool": lambda: g.iota(o[0], [[0, o[3]]], c, 0, allow_small_or_imprecise_dtypes=True)}
        fns["dve"] = lambda: g.vector.memset(o[0], c if SB[o[1][0][0]][1] == i32 else float(c))
        op(fns, o, [])

    def sel(o, i, pat, cmp, base, cm, other=0.0):
        op({"pool": lambda: g.affine_select(o[0], i[0], pat, cmp, other, base, cm)}, o, [i])

    def move(o, i):
        op({"pool": lambda: g.affine_select(o[0], i[0], [[0, o[3]]], Alu.is_ge, 0.0, 0, 0),
            "dve": lambda: g.vector.tensor_copy(o[0], i[0])}, o, [i])

    def dma(q, o, i, pre=()):
        op({e: (lambda e=e: Q[e].dma_start(o[0], i[0])) for e in (q if q == BOTH else (q,))}, o, [i], dma=True, pre=pre)

    def win(z, blk, r):
        return V(z, 128 * blk + 15 - r, 128 * blk + 143 - r)

    def listed(o, z, src, a, b, per_r=False, p=None):
        return [(o, V(z, 128 * r * per_r + 15 - r, 128 * r * per_r + 143 - r, p=p), V(src, a + r, b, 16, p=p)) for r in range(16)]

    others = [(rank + N - 1 - s) % N for s in range(N - 1)]
    mask = topo.mask(core, T.cores[others[0]])
    for r in others:
        mask &= topo.mask(core, T.cores[r])
    nloc = bin(mask).count("1")

    def send(t, a, b):
        src = V("NEW", t * S + a, t * S + b)
        ids = [DstId(rid=topo.addr(T.cores[r])[0], pnc=topo.addr(T.cores[r])[1]) for r in others]
        dsts = [T.Y[:, W + t * GH + s * S + a:W + t * GH + s * S + b] for s in range(N - 1)]
        trs = [RemoteDMATransfer(dst_ids=ids, dma_engine_mask=mask, remote_sem=T.sem["arr%d" % t], srcs=[src[0]], dsts=dsts)]
        op({"pool": lambda: g.remote_dma_fused(trs, local_sem=T.sem.sent)}, H(None), [src], cost=("rem", 0.4 + 0.6 * (b - a) / S))
        ops[-1]["send"] = "arr%d" % t

    for name in LOADS:
        if name == "FW":
            dma("sp", V("FW"), H(T.fw0[:, :]))
        elif name == "C":
            dma("sp", V("C", 0, S), H(T.cl[:, 0:S]))
        elif name == "LK":
            dma("sp", V("LK"), H(T.lk[:, :]))
        elif name == "TH":
            dma("sp", V("TH", p=(0, 8, 1)), H(T.th[:, :]))
        else:
            dma("sp", V("Y", 0, W0), H(T.y0[:, :]))
    dma("sp", V("C", S, M), H(T.cl[:, S:M]))

    fill(V("ONE"), 1)
    fill(V("HF"), 0)
    fill(V("ZD"), 0)
    iota(V("HF", 14, 24), [[S, 10]])
    iota(V("HF", 42, 46), [[S, 4]])
    iota(V("HF", 49, 52), [[S, 3]], W0)
    iota(V("HF", 40, 42), [[S, 2]], W0)
    for a, b, c in ((10, 11, 1), (32, 35, 1), (39, 40, S - W0), (54, 56, 1)):
        fill(V("HF", a, b), c)
    iota(V("HG", 0, 16), [[0, 8], [-1, 2]], 1)
    iota(V("HG", 16, 32), [[0, 8], [1, 2]])
    iota(V("HG", 32, 64), [[1, 32]])
    sel(V("ZD", 15, 2063, 16), V("ONE"), [[-1, 16], [-16, 8]], Alu.is_equal, 0, 1)
    if PACKED:
        fill(V("ZP"), 0)
        lin(V("Z5"), V("ZD", 15, 2063, 16), KEY)
        tt(V("ZP", 15, 15 + 16 * 88, 16), V("ZD", 15, 15 + 16 * 88, 16), V("Z5", 40, 128), Alu.add)
        tt(V("ZP", 15 + 16 * 88, 2063, 16), V("ZD", 15 + 16 * 88, 2063, 16), V("Z5", 0, 40), Alu.add)
    group([(V("P7", 0, 14), win("ZD", r, r), V("HF", 14 * r, 14 * (r + 1))) for r in range(4)]
          + listed(V("P7", 14, 18), "ZD", "HG", 0, 64, per_r=True))
    lin(V("CT"), V("P7", 0, 18))
    row, row16, even, odd = V("CT", 16, 17), V("CT", 17, 18), V("CT", 14, 15), V("CT", 15, 16)
    iota(V("LO"), [[1, S]])
    for B in range(10):
        lin(V("FP", S * B, S * (B + 1)), V("LO"), V("CT", 10, 11), V("CT", B, B + 1))
    cp(V("AU"), V("C", 0, S))
    cp(V("FL", 0, 112), V("FW"))
    for a, b in ((0, 56), (56, 112)):
        lin(V("YF", 16 * a, 16 * b), X(V("Y", 0, W0), V("FL", a, b)))
        lin(V("FS", 16 * a, 16 * b), X(V("FP", 0, W0), V("FL", a, b)))
        ops[-1]["lead"] = LEAD
    move(V("FS", W0, W), V("FP", W0, W))
    move(V("C", W0, W0 + S), V("C", 0, S))
    iota(V("PF"), [[-32, 4]], 0, 1)
    ts(V("ID"), V("LO", 0, 128), V("PF", 0, 1), Alu.is_equal)
    lin(V("NI"), V("ID"), -1.0)
    lin(V("N4"), V("ID"), -KEY)
    ts(V("IE"), V("ID"), 0.5 - 2.0 ** -11, Alu.mult)
    iota(V("KR"), [[1, 32], [0, 16]])
    for u in range(3):
        ts(V("R", 512 * u, 512 * (u + 1)), V("KR"), V("PF", u, u + 1), Alu.is_equal, V("ID", 96, 97), Alu.max)
    ms(V("OT", p=(96, 128, 1)), MAGIC)
    ms(V("MG"), MAGIC)
    ts(V("PG"), V("PF", 0, 1), row, Alu.subtract)
    ts(V("BO"), V("KR", 0, 128), 16.0, Alu.mult, V("PG"), Alu.is_equal)
    ts(V("E2"), V("KR", 0, 128), 2.0, Alu.mult, V("PF", 0, 1), Alu.is_equal)
    fill(V("ZE"), 0)
    move(V("ZE", 15, 143, 16), V("BO", 0, 128, 16))
    lin(V("ZK"), V("ZE"), KEY)
    lin(V("ZB"), V("ZE"), -KEY)
    iota(V("KI"), [[0, 16], [1, 16]])
    ts(V("EYE", 0, S), V("KI"), row, Alu.is_equal)
    wide = 256 * max(c1 - c0 for parts in PARTS for c0, c1 in parts)
    for a, b in ((S, 2 * S), (2 * S, M)):
        move(V("EYE", a, b), V("EYE", 0, b - a))
    for a in range(M, wide, M):
        dma("sp", V("EYE", a, a + M), V("EYE", 0, M))
    ts(V("TRI"), V("KI"), row, Alu.is_le, 2 * KEY, Alu.mult)
    fill(V("RP"), 1)
    fill(V("RP", 0, S, 16), 1 - 2 ** 24)
    lin(V("RQ"), V("RP"), -1.0)
    fill(V("GX"), 0)
    lin(V("GX", 15, 143, 16, p=(0, 8, 1)), V("ID", 0, 8, p=(0, 8, 1)), -KEY)
    ts(V("TF", p=(0, 8, 1)), V("TH", p=(0, 8, 1)), 2048.0, Alu.subtract)
    group(listed(V("P6", 0, 16), "GX", "TF", 0, S, p=(0, 8, 1)))
    lin(V("LIM"), V("P6", 0, 16), bias=-2048.0 * KEY)
    lin(V("LI0"), V("LIM"), bias=-7.5 * KEY)
    iota(V("IDL"), [[16, 160]])
    lin(V("IDL"), V("IDL"), bias=row)
    lin(V("XJ"), V("IDL", 0, 16), 16.0, 15.0)
    lin(V("LI"), V("IDL", 0, 16))
    ts(V("LJ", 0, 16), V("IDL", 0, 16), OFS, Alu.subtract)
    ts(V("LJ", 16, 48), V("IDL", 128, 160), OFS, Alu.subtract)
    move(V("FO", 144, 160), V("IDL", 144, 160))
    ms(V("KA"), 32.0 - OFS)
    tt(V("ZF", 0, 143), V("ZD", 0, 143), V("ZD", 128, 271), Alu.add)
    tt(V("ZV", 0, 143), V("ZD", 256, 399), V("ZD", 384, 527), Alu.add)
    for u in range(2):
        lin(V("ZG", 144 * u, 144 * u + 143), V("ZD", 256, 399), float(W - M + u * GH))
        tt(V("ZY%d" % u, 0, 143), V("ZG", 144 * u, 144 * u + 143), V("ZF", 0, 143), Alu.add)
    iota(V("OB"), [[S, 4]], W0)
    lin(V("OB"), V("OB"), odd)
    for t in range(RO):
        lin(V("NW", t * S, (t + 1) * S), V("LO"), odd, V("OB", t, t + 1))
    for q in range(4):
        move(V("L", 32 + 512 * q, 32 + 512 * (q + 1)), V("LK", 512 * q, 512 * (q + 1)))
    fill(V("L", 0, 32), 0)
    dma("sp", H(T.lo[0:128:2, :]), V("L", 32, 32 + NA, p=(0, 128, 2)))
    fill(V("C", M, W0), 0)
    fill(V("Y", W0 + S, W), 0)
    fill(V("FS", W, W + GH), 0)

    for t in range(RO):
        wt = W0 + t * S
        last = t == RO - 1
        atoms = "C" if t == 0 else "A32"
        own = "Y" if t == 0 else "OWN"
        lwin = V("LK") if t == 0 else V("L", 32, 32 + NA)
        parts = PARTS[t]
        nsig = (N - 1) * nloc * (len(parts) if APART else 1)
        F1, F2 = ("FP", "FS") if t == 1 else ("FS", "FP")

        if t > 0:
            lin(V("OWN"), X(V("Y", 0, wt), V("VU")))
        for u, a in enumerate((0, 96, 160)):
            group([(V("P7", 128 * u, 128 * (u + 1), p=(0, 96, 1)), V(own, a, a + 96), V("NI"))])
        lin(V("OT", p=(0, 96, 1)), V("P7", 0, 384, p=(0, 96, 1)))
        if not last:
            group([(V("P6", 0, S), V("BO"), V(own, 0, S))])
            lin(V("U"), V("P6", 0, S), bias=float(t + 1))

        for a, b in LINKS:
            ts(V("G", 16 * a, 16 * b), X(lwin, V("AU", a, b)), OFS, Alu.subtract)
        for a, b in (() if PACKED else PICKS):
            for j in range(2):
                group([(V("P%d" % j, a, b), win("ZD", (k + 5 * j) % 16, k), V("G", 16 * a + k, 16 * b, 16)) for k in range(16)])
                ts(V("BC", S * j + a, S * j + b), V("P%d" % j, a, b), OFS, Alu.add)
            if a % 128 == 0:
                lin(V("B32", a, a + 128), V("P0", a, a + 128))
        for n, (a, b) in enumerate(PICKS if PACKED else ()):
            x = V("P%d" % (n % 2), a, b)
            group([(x, win("ZP", k, k), V("G", 16 * a + k, 16 * b, 16)) for k in range(16)])
            ts(V("CK", a, b), x, KEY * MAGIC, Alu.add, KEY * MAGIC, Alu.subtract)
            ts(V("BC", S + a, S + b), V("CK", a, b), 1.0 / KEY, Alu.mult, OFS, Alu.add)
            tt(V("B32", a, b), x, V("CK", a, b), Alu.subtract)
            ts(V("BC", a, b), V("B32", a, b), OFS, Alu.add)

        for a, b in STATES:
            for j, name in enumerate(("GA", "GB")):
                lin(V(name, 16 * a, 16 * b), X(V("YF", 0, wt), V("BC", S * j + a, S * j + b)))

        def distances(n, c0, c1):
            u = min(c0 // 6, 2)
            a, b, r0 = S * c0, S * c1, S * (c0 - (0, 6, 10)[u])
            bank = V("P%d" % (2 + n % 3), 0, b - a)
            group([(bank, V("IE"), V("GA", a, b)), (bank, V("IE"), V("GB", a, b)),
                   (bank, V("OT", 128 * u, 128 * (u + 1), p=(0, 97, 1)), V("R", r0, r0 + b - a, p=(0, 97, 1)))])
            act(AB(c0, c1), bank, Act.Abs, bias=-MAGIC)

        def scans(bank, c0, c1):
            scan(V("SC", 16 * c0, 16 * c1), V("RQ", 0, 16 * (c1 - c0)), V(bank, 16 * c0, 16 * c1), Alu.min)
            scan(V("SC", S + 16 * c0, S + 16 * c1), V("RP", 0, 16 * (c1 - c0)), V(bank, 16 * c0, 16 * c1), Alu.max)

        def part(n, c0, c1):
            nc, a, b = c1 - c0, 16 * c0, 16 * c1
            nl = b - a
            final = n == len(parts) - 1
            bl, ba, bz = ("P5", "P6", "P0") if final else ("P5", "P5", "P0")
            bq, bp, bd = ("P2", "P3", "P4") if final else ("P7", "P7", "P1")
            top = c1
            for k, (d0, d1) in enumerate(SUMS):
                if c0 <= d0 < c1:
                    distances(k, d0, d1)
                    for e0, e1 in KEYS:
                        if e0 == d0:
                            bank = "P6" if e1 <= SCANS else "P5"
                            group([(V(bank, 16 * e0, 16 * e1), win("ZK", 0, r), AB(e0, e1, 16 * r, 16 * r + 16)) for r in range(16)])
                            if e0 in (c0, SCANS):
                                scans(bank, e0, top)
                                top = e0
            m0 = 2 * c0
            tt(V("MI", m0 + nc, m0 + 2 * nc), V("SC", a + 15, b, 16), V("XJ", 0, nc), Alu.add)
            tt(V("MI", m0, m0 + nc), V("XJ", 0, nc), V("SC", S + a + 15, S + b, 16), Alu.subtract)
            for j0, j1 in (((m0 + nc, m0 + 2 * nc), (m0, m0 + nc)) if QFIRST[t] else ((m0, m0 + 2 * nc),)):
                ts(V("JI", j0, j1), V("MI", j0, j1), int(KEY) - 1, Alu.bitwise_and)
                cp(V("JU", j0, j1), V("JI", j0, j1))
            jp, jq = V("JU", m0, m0 + nc), V("JU", m0 + nc, m0 + 2 * nc)
            nr = V("NR", c0, c1)
            tt(nr, V("MI", m0, m0 + nc), V("LIM", c0, c1), Alu.is_ge)
            eye = V("EYE", 0, 16 * nl)

            for j, name in enumerate(("GA", "GB")):
                lin(V("PQ", S * j + a, S * j + b), X(V(name, 16 * a, 16 * b), jq))
            o = V(bq, 0, nl)
            group([(o, V("NI"), V(own, a, b))], stop=False)
            group([(o, V("IE"), V("PQ", a, b)), (o, V("IE"), V("PQ", S + a, S + b)), (o, V("ID"), V("MG", 0, nl))], first=False)
            act(V("SG", a, b), o, Act.Sign, bias=-MAGIC)
            new = V("NEW", t * S + a, t * S + b)
            tt(new, V("SG", a, b), V(own, a, b), Alu.add)
            if APART:
                send(t, a, b)
            elif final:
                send(t, 0, S)

            pa, pb, pq, l0 = 3 * a, 3 * a + nl, 3 * a + 2 * nl, 4 * c0
            tt(V("PR", pa, pa + nl), X(eye, jp), V(atoms, a, b), Alu.mult)
            cols = (0, nc, 1)
            group([(V(ba, r, 128, 16, p=cols), V("PR", pa + r, pa + nl, 16), V("BO", 0, 128, 16)) for r in range(16)]
                  + [(V(ba, 0, 128, p=cols), nr, V("N4"))])
            at = V("AT", 128 * n, 128 * (n + 1), p=cols)
            ts(at, V(ba, 0, 128, p=cols), -1.0, Alu.mult)

            def lst(k0, k1, name="LL"):
                return V(name, (l0 if name == "LL" else 0) + nc * k0, (l0 if name == "LL" else 0) + nc * k1)
            tt(V("PR", pq, pq + nl), X(eye, jq), V("B32", a, b), Alu.mult)
            if not last:
                tt(V("PR", pb, pb + nl), X(eye, jp), V("B32", a, b), Alu.mult)
            lj = V("LJ", 16 * t + c0, 16 * t + c1)
            al = [(lst(2, 3, bl), at, V("NI", 0, nc, p=cols)), (lst(2, 3, bl), V("ID"), V("KA", 0, nc))]
            if t == 0:
                group(listed(V("P1", 0, nc), "ZE", "PR", pq, pq + nl) + [(V("P1", 0, nc), V("NI"), lj)])
                tt(V("NH", c0, c1), V("P1", 0, nc), nr, Alu.mult)
                group(listed(lst(0, 1, bl), "ZE", "PR", pb, pb + nl) + al
                      + [(lst(1, 2, bl), V("ID"), lj), (lst(1, 2, bl), V("ID"), V("NH", c0, c1))])
                ts(lst(0, 3), lst(0, 3, bl), OFS, Alu.add)
            else:
                tt(V("NV", c0, c1), nr, V("VS", c0, c1), Alu.mult)
                k0 = 1 if last or not MERGE else 0
                group(listed(lst(k0, 2, bl), "ZE", "PR", pb + nl * k0, pq + nl) + al
                      + [(lst(3, 4, bl), V("ID"), V("NV", c0, c1)), (lst(3, 4, bl), V("ID"), lj)])
                ts(lst(k0, 4), lst(k0, 4, bl), OFS, Alu.add)
                if not last and not MERGE:
                    group(listed(V("P1", 0, nc), "ZE", "PR", pb, pb + nl))
                    ts(lst(0, 1), V("P1", 0, nc), OFS, Alu.add)
            lin(V("EF", a, b), X(V(F1, 0, wt), lst(1, 2)))
            lin(V("VAL", a, b), X(V("L"), lst(2, 3)), even)

            d1, d2 = V(bd, 0, nl), V(bd, nl, nl + nl // 2)
            ne = 3 * nl // 2 if PAIRS else nl
            group([(d1, V("BO"), V("PR", pa, pa + nl)), (d1, V("ID"), V("TRI", 0, nl))]
                  + [(V(bd, nl + 16 * c, nl + 16 * (c + 1)), V("BO"), V("PR", pa + 32 * c + 16, pa + 32 * c + 32))
                     for c in range(nc // 2 * PAIRS)], stop=False)
            group([(d1, at, V("R", 0, nl, p=cols))] + [(d2, at, V("E2", 0, nl // 2, p=cols))] * PAIRS, first=False)
            e0 = 3 * a // 2
            if EQ_ACT[t]:
                act(V("EA", e0, e0 + ne), V(bd, 0, ne), Act.Abs)
                act(V("EQ", e0, e0 + ne), V("EA", e0, e0 + ne), Act.Relu, bias=1.0, scale=-1.0)
            else:
                ts(V("EQ", e0, e0 + ne), V(bd, 0, ne), 0.0, Alu.is_equal)
            z = V(bz, 0, nc)
            group([(z, at, V("NI", 0, nc, p=cols)), (z, V("ID"), V("KA", 0, nc))] + listed(z, "ZB", "EQ", e0, e0 + nl)
                  + listed(V(bz, 1, nc, 2), "ZB", "EQ", e0 + nl, e0 + 3 * nl // 2) * PAIRS)
            if PAIRS:
                for u, spare in enumerate((row, row16)):
                    ts(V("OC", c0 + u, c1, 2), V(bz, u, nc, 2), OFS, Alu.add, spare, Alu.max)
                for c in range(c1 - 2, c0 - 2, -2):
                    tt(X(V("L"), V("OC", c, c + 2)), V("VAL", 16 * c, 16 * c + 32), V("NW", t * S + 16 * c, t * S + 16 * c + 32), Alu.add)
            else:
                ts(V("OC", 2 * c0, 2 * c1, 2), z, OFS, Alu.add, row, Alu.max)
                for c in range(c1 - 1, c0 - 1, -1):
                    tt(X(V("L"), V("OC", 2 * c, 2 * c + 1)), V("VAL", 16 * c, 16 * c + 16), V("NW", t * S + 16 * c, t * S + 16 * c + 16), Alu.add)

            for j, name in enumerate(("GA", "GB")):
                lin(V("PQ", S * (2 + j) + a, S * (2 + j) + b), X(V(name, 16 * a, 16 * b), jp))
            o = V(bp, S, S + nl)
            group([(o, V("IE"), V("PQ", 2 * S + a, 2 * S + b)), (o, V("IE"), V("PQ", 3 * S + a, 3 * S + b)),
                   (o, V("ID"), V("MG", 0, nl))])
            lin(V("Y" if last else "YF", wt + a, wt + b), o, bias=-MAGIC)
            if not last:
                move(V("Y", wt + a, wt + b), V("YF", wt + a, wt + b))
            if t == 0:
                move(V("Y", a, b), new)
            else:
                cp(X(V("Y", 0, wt), V("VU", c0, c1)), new)

            if not last:
                tt(V("PC", a, b), X(eye, jp), V("U", a, b), Alu.mult)
                tt(V("C" if t == 0 else "CN", a, b), V("PC", a, b), V(atoms, a, b), Alu.add)
                if DIRECT:
                    ts(V("C" if t == 0 else "CN", a, b), V("C" if t == 0 else "CN", a, b), NA - 1, Alu.bitwise_and)
                if t > 0:
                    cp(X(V("C", 0, wt), V("VU", c0, c1)), V("CN", a, b))

        for n, (c0, c1) in enumerate(parts):
            part(n, c0, c1)
        for c0, c1 in parts:
            if t == 0:
                lin(V(F1, 16 * c0, 16 * c1), V("EF", 16 * c0, 16 * c1))
            else:
                cp(X(V(F1, 0, W), V("LL", c0 + 3 * c1, 4 * c1)), V("EF", 16 * c0, 16 * c1))

        def squares():
            nb = S if t == 0 else M
            fp = V(F1, 0, W + t * GH if t else W0)
            for a, b in (((64, 88), (88, 112)) if t else ((16, 64), (64, 112))):
                lin(V(F2, 16 * a, 16 * b), X(fp, V("FY" if t else "FL", a, b)))
            group(listed(V("P2", 0, nb // 16), "ZF", F1, 0, nb))
            if t > 0:
                group(listed(V("P2", 64, 64 + 16 * t), "ZF", F1, W0, wt))
            cp(V("FL", 0, nb // 16 + 16 * t), V("P2", 0, nb // 16 + 16 * t))
            for a in range(0, nb // 16, 32):
                b = min(a + 32, nb // 16)
                lin(V(F2, 16 * a, 16 * b), X(fp, V("FL", a, b)))
            if t > 0:
                lin(V(F2, W0, wt), X(fp, V("FL", 64, 64 + 16 * t)))
        if not TWICE:
            squares()

        if not last:
            if t == 0:
                group([(V("P7", r, S, 16), win("ZD", r, 2), V("NR")) for r in range(16)])
                lin(V("MR"), V("P7", 0, S), V("CT", 11, 12), V("CT", 12, 13))
            else:
                tt(V("AD"), V("NR"), V("NB"), Alu.mult)
                group([(V("P7", r, S, 16), win("ZD", r, 2), V("AD")) for r in range(16)])
                lin(V("MR"), V("P7", 0, S), bias=V("CT", 13, 14))
            if TWICE:
                for c0, c1 in parts:
                    lin(V("W1", 16 * c0, 16 * c1), X(V(F1, 0, wt), V("LL", 4 * c0, 3 * c0 + c1)))
                group(listed(V("P5", 0, 16), "ZF", "W1", 0, S))
                cp(V("WU"), V("P5", 0, 16))
                tt(V("PW"), X(V(F1, 0, wt), V("WU")), V("MR"), Alu.mult)
            else:
                for c0, c1 in parts:
                    tt(V("PW", 16 * c0, 16 * c1), X(V(F2, 0, wt), V("LL", 4 * c0, 3 * c0 + c1)), V("MR", 16 * c0, 16 * c1), Alu.mult)
            v = V("P5", 0, 16)
            group([(v, V("ID"), V("LI"))] + listed(v, "ZV", "PW", 0, S))
            cp(V("VU"), v)
            if DIRECT:
                cp(V("AU"), X(V("C", 0, wt + S), V("VU")))
                move(V("A32"), V("AU"))
            else:
                ts(V("A32"), X(V("C", 0, wt + S), V("VU")), NA - 1, Alu.bitwise_and)
                cp(V("AU"), V("A32"))
            lin(V("VA", 0, 16), v, bias=1.5 * 2 ** 15 - 127.5)
            lin(V("VS"), V("VA", 0, 16), bias=-(1.5 * 2 ** 15 + wt + S))
            if t == 0:
                move(V("C", wt + S, wt + 2 * S), V("A32"))
                lin(V("VA", 16, 32), v, bias=1.5 * 2 ** 17 + S - 511.5)
                lin(V("VA", 32, 48), V("VA", 16, 32), bias=-(1.5 * 2 ** 17 + S))
                tt(V("NB"), V("VS"), V("VA", 32, 48), Alu.subtract)
            group([(V("P4", 0, 16), V("BO"), V("NR"))])
            act(V("JK"), V("P4", 0, 16), bias=7.5 / 16, total=V("AI", 0, 1))
            act(V("AI", 1, 2), V("AI", 0, 1), bias=MAGIC, scale=1.0 / 16)
            act(V("AI", 2, 3), V("AI", 1, 2), bias=16 * KEY * MAGIC, scale=-16 * KEY)
            act(V("AI", 3, 4), V("AI", 0, 1), bias=V("AI", 2, 3), scale=KEY)
            lin(V("LIM"), V("LI0"), bias=V("AI", 3, 4))
        if TWICE:
            squares()

        if not last:
            move(V(F2, W + t * GH, W + (t + 1) * GH), V(F2, M, W0))
            group(listed(V("P4", 0, wt // 16), "ZY%d" % t, F2, 0, wt))
            cp(V("FY", 0, wt // 16), V("P4", 0, wt // 16))
            top = wt // 16
            for a in range(0, top, top // 4):
                lin(V("YF", 16 * a, 16 * a + 4 * top), X(V("Y", 0, W + (t + 1) * GH), V("FY", a, a + top // 4)),
                    pre=[("arr%d" % t, nsig)])
        else:
            n0 = len(ops)
            dma(BOTH, H(T.lo[1:128:2, :]), V("L", 32, 32 + NA, p=(1, 128, 2)))
            dma(BOTH, H(T.yo[:, W0:W]), V("Y", W0, W))
            dma(BOTH, H(T.yo[:, 0:M]), V("Y", 0, M))
            group(listed(V("P7", M // 16, wt // 16), "ZF", F2, M, wt))
            group(listed(V("P7", 0, M // 16), "ZF", F2, 0, M))
            lin(V("FO", 0, wt // 16), V("P7", 0, wt // 16))
            dma(BOTH, H(T.fo[:, :]), V("FO"))
            dma(BOTH, H(T.yo[:, M:W0]), V("Y", W + t * GH, W + (t + 1) * GH), pre=[("arr%d" % t, nsig)])
            for o in ops[n0:]:
                o["end"] = True

    seen, sends, lastdma = {}, {}, {}
    for n, o in enumerate(ops):
        deps, near, order = set(), set(), set()
        for kind, regs in (("r", o["r"]), ("w", o["w"])):
            for name, a, b in regs:
                psum = name[0] == "P" and name[1:].isdigit()
                for m, k2, a2, b2 in seen.get(name, ()):
                    if a2 < b and a < b2 and m != n:
                        if "pe" in o["fns"] and "pe" in ops[m]["fns"]:
                            if psum:
                                order.add(m)
                        elif kind == "w" and INORDER and not (o["dma"] or ops[m]["dma"] or "send" in ops[m]):
                            near.add(m)
                        elif kind == "w" or k2 == "w":
                            deps.add(m)
                        elif psum:
                            near.add(m)
        for kind, regs in (("r", o["r"]), ("w", o["w"])):
            for name, a, b in regs:
                lst = seen.setdefault(name, [])
                if kind == "w":
                    lst[:] = [x for x in lst if not (a <= x[2] and x[3] <= b)]
                lst.append((n, kind, a, b))
        if "send" in o:
            sends[o["send"]] = n
        late = {sends[name] for name, v in o["pre"]}
        if o["dma"] and not o["r"]:
            order |= set(lastdma.values())
            lastdma["load"] = n
        o["deps"], o["near"], o["order"], o["late"] = deps, near - deps, order, late

    if "seq" not in PLAN:
        PLAN["seq"] = arrange([o["ways"] for o in ops], [sorted(o["deps"] | o["late"]) for o in ops],
                              [sorted(o["near"]) for o in ops], [sorted(o["order"]) for o in ops],
                              [o.get("lead", 0.0) for o in ops])
    seq, on = PLAN["seq"]
    for o, q in zip(ops, on):
        o["e"] = QUEUES[q]
    for o in ops:
        o["deps"] = o["deps"] | {m for m in o["near"] if ops[m]["e"] != o["e"]}
    place = {n: k for k, n in enumerate(seq)}
    ops = [ops[n] for n in seq]

    known = {e: {} for e in Q}
    clock, waits, needed = [], [], set()
    ndma = 0
    for n, o in enumerate(ops):
        e = o["e"]
        mine = []
        for m in sorted((place[k] for k in o["deps"]), reverse=True):
            key = ops[m]["key"]
            if known[e].get(key, -1) >= m:
                continue
            mine.append(m)
            needed.add(m)
            for k2, v2 in clock[m].items():
                if known[e].get(k2, -1) < v2:
                    known[e][k2] = v2
        waits.append(mine)
        if o["dma"] and not o["w"] and o.get("end"):
            o["key"] = "out"
        elif o["dma"]:
            o["key"] = "d%d" % ndma
            ndma += 1
        else:
            o["key"] = e
        ck = dict(known[e])
        ck[o["key"]] = n
        clock.append(ck)
    value, count_of, left, arrived = {}, {}, [], set()
    for n, o in enumerate(ops):
        q = Q[o["e"]]
        for m in waits[n]:
            q.wait_ge(T.sem[ops[m]["key"]], value[m])
        for name, v in o["pre"]:
            if (o["e"], name) not in arrived:
                arrived.add((o["e"], name))
                q.wait_ge(T.sem[name], v)
        ins = o["fns"][o["e"]]()
        if o["dma"]:
            ins.then_inc(T.sem[o["key"]], 16)
            value[n] = 16
            if n not in needed:
                left.append(o["key"])
        elif n in needed:
            count_of[o["key"]] = count_of.get(o["key"], 0) + 1
            value[n] = count_of[o["key"]]
            ins.then_inc(T.sem[o["key"]], 1)
    g.wait_ge(T.sem.sent, nloc * sum("send" in o for o in ops))
    for key in sorted(set(left)):
        g.wait_ge(T.sem[key], 16 * left.count(key))
